import numpy as np
import ml_dtypes


def mxq(x, axis, fmt="e4m3"):
    dtype, down = {"e4m3": (ml_dtypes.float8_e4m3fn, 7), "e5m2": (ml_dtypes.float8_e5m2, 14)}[fmt]
    v = np.moveaxis(np.asarray(x, np.float32).astype(ml_dtypes.bfloat16).astype(np.float64), axis, -1)
    blocks = v.reshape(v.shape[:-1] + (-1, 32))
    amax = np.abs(blocks).max(-1, keepdims=True)
    byte = np.maximum(np.where(amax > 0, np.frexp(amax)[1] - 1 + 127, 0) - down, 1)
    scale = np.exp2(byte - 127.0)
    codes = (blocks / scale).astype(np.float32).astype(dtype).astype(np.float64)
    return np.moveaxis((codes * scale).reshape(v.shape), -1, axis)


WIDE = False


def mx_kscale(k):
    if not WIDE:
        return np.ones(k)
    levels = np.array([10, -10, 5, -5, 0])
    if k % 512:
        return np.exp2(np.random.permutation(np.resize(levels, k // 32))).repeat(32)
    a = np.empty((k // 512, 16))
    for p in range(k // 512):
        a[p, :8] = np.random.permutation(np.resize(levels, 8))
        for g in range(8):
            far = levels[np.abs(levels - a[p, g]) >= 10]
            a[p, g + 8] = far[np.random.randint(len(far))]
    return np.exp2(a.ravel()).repeat(32)


def f64(x):
    return np.asarray(x).astype(np.float64)


def striped(idx):
    return np.tile(idx.reshape(-1, 16).T, (8, 1)).astype(np.uint16)


def unstriped(offs):
    return offs[:16].T.reshape(-1).astype(np.int64)


E2M1 = np.array([0.0, 0.5, 1.0, 1.5, 2.0, 3.0, 4.0, 6.0, -0.0, -0.5, -1.0, -1.5, -2.0, -3.0, -4.0, -6.0])


def pack_weight(w, fmt):
    k, n = w.shape
    w = f64(np.asarray(w, np.float32).astype(ml_dtypes.bfloat16)).reshape(k // 32, 32, n)
    amax = np.abs(w).max(1)
    if fmt == "e4m3":
        byte = np.frexp(amax)[1] - 1 + 127 - 7
    else:
        mant, ex = np.frexp(amax / 6.0)
        byte = np.where(mant > 0.5, ex, ex - 1) + 127
    byte = np.clip(np.where(amax > 0, byte, 1), 1, 254)
    scaled = (w * np.exp2(127.0 - byte)[:, None, :]).reshape(k, n).astype(np.float32)
    by_word = np.ascontiguousarray(scaled.reshape(k // 512, 128, 4, n).transpose(0, 1, 3, 2))
    if fmt == "e4m3":
        words = by_word.astype(ml_dtypes.float8_e4m3fn).view(np.uint8)
    else:
        c = by_word.astype(ml_dtypes.float4_e2m1fn).view(np.uint8) & 0xF
        words = (c[..., 0::2] | (c[..., 1::2] << 4)).reshape(k // 512, 128, 2 * n)
    return np.ascontiguousarray(words), np.ascontiguousarray(byte.astype(np.uint8).reshape(k // 512, 16, n))


def unpack_weight(words, scales, fmt):
    g, _, n = scales.shape
    words = np.ascontiguousarray(words).reshape(g, 128, n, -1)
    if fmt == "e4m3":
        vals = words.view(ml_dtypes.float8_e4m3fn).astype(np.float64)
    else:
        nib = np.empty((g, 128, n, 4), np.uint8)
        nib[..., 0::2] = words & 0xF
        nib[..., 1::2] = words >> 4
        vals = E2M1[nib]
    vals = vals * np.repeat(np.exp2(scales.astype(np.float64) - 127.0), 8, axis=1)[..., None]
    return vals.transpose(0, 1, 3, 2).reshape(g * 512, n)


def gelu(v):
    return 0.5 * v * (1.0 + np.tanh(np.sqrt(2.0 / np.pi) * (v + 0.044715 * v**3)))


K, K2, H, N, T, S = 512, 1024, 1024, 512, 2048, 1024

def setup_inputs():
    n = np.random.standard_normal
    s, s2, u = mx_kscale(K)[:, None], mx_kscale(K2)[:, None], mx_kscale(H)[:, None]
    tab_words, tab_scales = pack_weight(n((K, T)) * s, "e4m3")
    tab2_words, tab2_scales = pack_weight(n((K2, T)) * s2, "e4m3")
    wd_words, wd_scales = pack_weight(n((K2, H)) / np.sqrt(K2) / s2, "e2m1")
    return {
        "tab_words": tab_words, "tab_scales": tab_scales,
        "tab2_words": tab2_words, "tab2_scales": tab2_scales,
        "offs": striped(np.random.permutation(T)[:S]),
        "offs2": striped(np.random.permutation(T)[:S]),
        "wq": (n((K, H)) / np.sqrt(K) / s).astype(np.float32),
        "wd_words": wd_words, "wd_scales": wd_scales,
        "gain": (0.3 * np.exp(0.3 * n(H)) * u[:, 0]).astype(np.float32),
        "wf": (n((H, N)) / np.sqrt(H) / u).astype(np.float32),
        "bf": (0.3 * n(N)).astype(np.float32),
    }

def reference(tab_words, tab_scales, tab2_words, tab2_scales, offs, offs2, wq, wd_words, wd_scales, gain, wf, bf):
    v = unpack_weight(tab_words, tab_scales, "e4m3")[:, unstriped(offs)]
    v2 = unpack_weight(tab2_words, tab2_scales, "e4m3")[:, unstriped(offs2)]
    p = mxq(f64(wq), 0, "e4m3").T @ v
    d = unpack_weight(wd_words, wd_scales, "e2m1").T @ v2
    h = f64(gain)[:, None] * np.square(p - d)
    y = mxq(f64(wf), 0, "e4m3").T @ mxq(h, 0, "e4m3")
    out = np.tanh(y + f64(bf)[:, None])
    return out

@@ -1,0 +1,279 @@
+from contextlib import ExitStack
+
+import concourse.mybir as mybir
+from concourse.masks import make_identity
+
+K, K2, H, N, T, S = 512, 1024, 1024, 512, 2048, 1024
+FLOPS = 2 * S * (K * H + K2 * H + H * N)
+
+F32 = mybir.dt.float32
+BF16 = mybir.dt.bfloat16
+I32 = mybir.dt.int32
+U32 = mybir.dt.uint32
+U16 = mybir.dt.uint16
+U8 = mybir.dt.uint8
+FP8X4 = mybir.dt.float8_e4m3fn_x4
+FP4X4 = mybir.dt.float4_e2m1fn_x4
+ACT = mybir.ActivationFunctionType
+ALU = mybir.AluOpType
+
+P = 128
+PACK = 4
+HALF = 512
+GROUPS = 2
+QUERY_PLANE = 8
+
+
+def tile_list_duplicate_match_features_kernel(
+    tc, tab_words, tab_scales, tab2_words, tab2_scales, offs, offs2, wq, wd_words, wd_scales, gain, wf, bf, out
+):
+    nc = tc.nc
+    with ExitStack() as ctx:
+        sb = ctx.enter_context(tc.tile_pool(name="sb", bufs=1))
+        psum = ctx.enter_context(tc.psum_pool(name="psum", bufs=8))
+
+        def tile(name, shape, dtype):
+            return sb.tile(shape, dtype, name=name, align_bytes=64)
+
+        doc_list = tile("doc_list", [P, S // 16], U16)
+        query_list = tile("query_list", [P, S // 16], U16)
+        doc_scale_win = tile("doc_scale_win", [P, T // 4], I32)
+        doc_scales_moved = tile("doc_scales_moved", [P, S // 4], I32)
+        query_scale_win = tile("query_scale_win", [P, T // 4], I32)
+        wd_scale_raw = tile("wd_scale_raw", [P, 2, H // 4], I32)
+        vec_rows = tile("vec_rows", [P, P], F32)
+        doc_win = [tile("doc_win%d" % a, [P, T], I32) for a in range(2)]
+        query_win = tile("query_win", [P, T], I32)
+        wd_raw = [tile("wd_raw%d" % g, [P, 2, 256], I32) for g in range(GROUPS)]
+        wq_raw = [tile("wq_raw%d" % g, [P, PACK, 512], F32) for g in range(GROUPS)]
+        wf_raw = [tile("wf_raw%d" % g, [P, PACK, N], F32) for g in range(GROUPS)]
+
+        nc.vector.memset(doc_scale_win[:], 0)
+        nc.vector.memset(wd_scale_raw[:], 0)
+        nc.vector.memset(query_scale_win[:], 0)
+        nc.vector.memset(doc_scales_moved[:], 0)
+        nc.gpsimd.memset(vec_rows[:], 0.0)
+        halves = tile("halves", [P, 8], F32)
+        nc.gpsimd.memset(halves[:], 0.5)
+        warm = tile("warm", [P, 1], F32)
+        nc.scalar.activation(out=warm[:], in_=halves[:, 0:1], func=ACT.Tanh)
+
+        def table_words(words, a):
+            return words[a].rearrange("p t i -> p (t i)").bitcast(I32)
+
+        def load_wd(g):
+            nc.sync.dma_start(out=wd_raw[g][:], in_=wd_words[:, :, 1024 * g : 1024 * (g + 1)].rearrange("a p c -> p a c").bitcast(I32))
+
+        def load_wq(g):
+            nc.sync.dma_start(out=wq_raw[g][:], in_=wq[:, 512 * g : 512 * (g + 1)].rearrange("(p j) c -> p j c", j=PACK))
+
+        def load_wf(g):
+            rows = wf[512 * g : 512 * (g + 1), :].rearrange("(b t i) n -> t b i n", t=PACK, i=8)
+            for t in range(PACK):
+                nc.sync.dma_start(out=wf_raw[g][:, t, :], in_=rows[t])
+
+        for g in range(GROUPS):
+            nc.gpsimd.dma_start(
+                out=vec_rows[4 * g : 4 * g + 4, :].rearrange("t (b i) -> t b i", i=8),
+                in_=gain[512 * g : 512 * (g + 1)].rearrange("(b t i) -> t b i", t=PACK, i=8),
+            )
+        bias = tile("bias", [P, 4], F32)
+        with nc.allow_non_contiguous_dma(reason="one bias value for each partition and output tile"):
+            nc.gpsimd.dma_start(out=bias[:], in_=bf.rearrange("(c p) -> p c", p=P))
+
+        ident = tile("ident", [P, P], F32)
+        make_identity(nc, ident[:])
+        vec_bank = psum.tile([P, HALF], F32, name="vec_bank", tag="bank")
+        nc.tensor.transpose(vec_bank[:, 0:P], vec_rows[:], ident[:])
+        vec_cols = tile("vec_cols", [P, 8], F32)
+        nc.scalar.copy(out=vec_cols[:], in_=vec_bank[:, 0:8])
+        root_gain = tile("root_gain", [P, 8], F32)
+        nc.gpsimd.tensor_tensor(root_gain[:], vec_cols[:], halves[:], ALU.pow)
+
+        nc.sync.dma_start(doc_list[:], offs2)
+        for q in range(4):
+            nc.sync.dma_start(
+                out=doc_scale_win[32 * q : 32 * q + 8, :],
+                in_=tab2_scales[:, 4 * q : 4 * q + 4, :].bitcast(I32),
+            )
+        nc.sync.dma_start(out=doc_win[0][:], in_=table_words(tab2_words, 0))
+        nc.sync.dma_start(query_list[:], offs)
+        for r in range(4):
+            nc.sync.dma_start(
+                out=query_scale_win[QUERY_PLANE + r : P : 32, :],
+                in_=tab_scales[0, r:16:4, :].bitcast(I32),
+            )
+        nc.sync.dma_start(out=query_win[:], in_=table_words(tab_words, 0))
+        load_wq(0)
+        doc_scales_picked = tile("doc_scales_picked", [P, S], U8)
+        nc.vector.tensor_copy(doc_scales_picked[:], doc_scale_win[:].bitcast(U8).indirect(doc_list[:]))
+        nc.sync.dma_start(out=doc_scales_moved[0:112, :], in_=doc_scales_picked[4:116, :].bitcast(I32))
+        for r in range(4):
+            nc.sync.dma_start(
+                out=wd_scale_raw[r:P:32, :, :],
+                in_=wd_scales[:, r:16:4, :].rearrange("a q c -> q a c").bitcast(I32),
+            )
+        load_wd(0)
+        nc.sync.dma_start(out=doc_win[1][:], in_=table_words(tab2_words, 1))
+        load_wq(1)
+        load_wd(1)
+        load_wf(0)
+        load_wf(1)
+
+        def gather(picked, window, offsets):
+            nc.vector.tensor_copy(picked, window.bitcast(picked.dtype).indirect(offsets))
+
+        doc_codes_first = tile("doc_codes_first", [P, S], U32)
+        query_scales_all = tile("query_scales_all", [P, S], U8)
+        query_codes_all = tile("query_codes_all", [P, S], U32)
+        gather(doc_codes_first[:], doc_win[0][:], doc_list[:])
+        gather(query_scales_all[:], query_scale_win[:], query_list[:])
+        gather(query_codes_all[:], query_win[:], query_list[:])
+        doc_scales, doc_codes, query_scales, query_codes = {}, {}, {}, {}
+        for h in range(2):
+            cols = slice(HALF * h, HALF * (h + 1))
+            doc_scales[h, 0] = doc_scales_picked[:, cols]
+            doc_scales[h, 1] = doc_scales_moved[:].bitcast(U8)[:, cols]
+            doc_codes[h, 0] = doc_codes_first[:, cols]
+            query_scales[h] = query_scales_all[QUERY_PLANE:P, cols]
+            query_codes[h] = query_codes_all[:, cols]
+
+        def gather_half(h):
+            picked = tile("doc_codes_second%d" % h, [P, HALF], U32)
+            gather(picked[:], doc_win[1][:], doc_list[:, 32 * h : 32 * (h + 1)])
+            doc_codes[h, 1] = picked[:]
+
+        wd_codes, wd_plane, wq_codes, wq_plane, wf_codes, wf_plane = {}, {}, {}, {}, {}, {}
+
+        def permute_wd(g):
+            wd_codes[g] = tile("wd_codes%d" % g, [P, 2, PACK, 256], U8)
+            nc.vector.tensor_copy(
+                out=wd_codes[g][:].bitcast(I32).rearrange("p a t (b w) -> p a t b w", w=4),
+                in_=wd_raw[g][:].rearrange("p a (b t w) -> p a t b w", t=PACK, w=4),
+            )
+            wd_plane[g] = tile("wd_plane%d" % g, [P, 2, PACK, P], U8)
+            nc.vector.tensor_copy(
+                out=wd_plane[g][:].bitcast(I32).rearrange("p a t (b w) -> p a t b w", w=2),
+                in_=wd_scale_raw[:, :, 128 * g : 128 * (g + 1)].rearrange("p a (b t w) -> p a t b w", t=PACK, w=2),
+            )
+
+        def quantize(name, grouped, width):
+            codes = tile(name + "_codes", [P, width], U32)
+            plane = tile(name + "_plane", [P, width], U8)
+            nc.vector.quantize_mx(out=codes[:].bitcast(FP8X4), scales=plane[:], in_=grouped)
+            return codes, plane
+
+        def prepare_wq(g, on_scalar):
+            grouped = tile("wq_bf%d" % g, [P, PACK, 512], BF16)
+            for t in range(PACK):
+                dst = grouped[:, t, :].rearrange("p (b i j) -> p b i j", i=8, j=PACK)
+                src = wq_raw[g][:].rearrange("p j (b t i) -> p t b i j", t=PACK, i=8)[:, t]
+                if t in on_scalar:
+                    nc.scalar.activation(out=dst, in_=src, func=ACT.Copy, scale=-1.0)
+                else:
+                    nc.vector.tensor_scalar(dst, src, -1.0, None, ALU.mult)
+            wq_codes[g], wq_plane[g] = quantize("wq%d" % g, grouped[:].rearrange("p t c -> p (t c)"), 512)
+
+        def interleave(dst, src):
+            nc.vector.tensor_copy(
+                out=dst.rearrange("p (c i t) -> p c t i", i=4, t=PACK),
+                in_=src.rearrange("p t (c i) -> p c t i", i=4),
+            )
+
+        def prepare_wf(g):
+            grouped = tile("wf_bf%d" % g, [P, PACK * N], BF16)
+            interleave(grouped[:], wf_raw[g][:])
+            wf_codes[g], wf_plane[g] = quantize("wf%d" % g, grouped[:], N)
+
+        h_codes, h_plane = {}, {}
+
+        def doc_pass(bank, h, g, t, a):
+            nc.tensor.matmul_mx(
+                out=bank[:],
+                lhsT=wd_codes[g][:, a, t, :].bitcast(FP4X4),
+                lhsT_scale=wd_plane[g][:, a, t, :],
+                rhs=doc_codes[h, a].bitcast(FP8X4),
+                rhs_scale=doc_scales[h, a],
+                start=(a == 0),
+                stop=(a == 1),
+            )
+
+        def difference(h, g):
+            banks = []
+            for t in range(PACK):
+                bank = psum.tile([P, HALF], F32, name="diff%d%d%d" % (h, g, t), tag="bank")
+                doc_pass(bank, h, g, t, 0)
+                cols = slice(P * t, P * (t + 1))
+                nc.tensor.matmul_mx(
+                    out=bank[:],
+                    lhsT=wq_codes[g][:, cols].bitcast(FP8X4),
+                    lhsT_scale=wq_plane[g][:, cols],
+                    rhs=query_codes[h].bitcast(FP8X4),
+                    rhs_scale=query_scales[h],
+                    start=False,
+                    stop=False,
+                )
+                doc_pass(bank, h, g, t, 1)
+                banks.append(bank)
+            return banks
+
+        def square_and_quantize(h, g, banks, pieces):
+            width = HALF // pieces
+            for u in range(pieces):
+                cols = slice(width * u, width * (u + 1))
+                planar = tile("h_planar%d%d%d" % (h, g, u), [P, PACK, width], BF16)
+                for t in range(PACK):
+                    nc.scalar.activation(
+                        out=planar[:, t, :], in_=banks[t][:, cols], func=ACT.Square,
+                        scale=root_gain[:, PACK * g + t : PACK * g + t + 1],
+                    )
+                grouped = tile("h_bf%d%d%d" % (h, g, u), [P, PACK * width], BF16)
+                interleave(grouped[:], planar[:])
+                codes, plane = quantize("h%d%d%d" % (h, g, u), grouped[:], width)
+                for v in range(width // 256):
+                    h_codes[h, g, (width * u) // 256 + v] = codes[:, 256 * v : 256 * (v + 1)]
+                    h_plane[h, g, (width * u) // 256 + v] = plane[:, 256 * v : 256 * (v + 1)]
+
+        def features(h, u):
+            tokens = slice(HALF * h + 256 * u, HALF * h + 256 * (u + 1))
+            for pair in range(2):
+                bank = psum.tile([P, 2, 256], F32, name="y%d%d%d" % (h, u, pair), tag="bank")
+                for e in range(2):
+                    cols = slice(P * (2 * pair + e), P * (2 * pair + e + 1))
+                    for g in range(GROUPS):
+                        nc.tensor.matmul_mx(
+                            out=bank[:, e, :],
+                            lhsT=wf_codes[g][:, cols].bitcast(FP8X4),
+                            lhsT_scale=wf_plane[g][:, cols],
+                            rhs=h_codes[h, g, u].bitcast(FP8X4),
+                            rhs_scale=h_plane[h, g, u],
+                            start=(g == 0),
+                            stop=(g == GROUPS - 1),
+                        )
+                result = tile("result%d%d%d" % (h, u, pair), [P, 2, 256], F32)
+                for e in range(2):
+                    c = 2 * pair + e
+                    nc.scalar.activation(out=result[:, e, :], in_=bank[:, e, :], func=ACT.Tanh, bias=bias[:, c : c + 1])
+                nc.sync.dma_start(
+                    out=out[256 * pair : 256 * (pair + 1), tokens].rearrange("(e p) j -> p e j", p=P), in_=result[:]
+                )
+
+        permute_wd(0)
+        prepare_wq(0, (0, 1, 2, 3))
+        gather_half(0)
+        banks00 = difference(0, 0)
+        gather_half(1)
+        banks10 = difference(1, 0)
+        permute_wd(1)
+        prepare_wq(1, (0, 1))
+        square_and_quantize(0, 0, banks00, 1)
+        banks01 = difference(0, 1)
+        square_and_quantize(1, 0, banks10, 1)
+        banks11 = difference(1, 1)
+        prepare_wf(0)
+        prepare_wf(1)
+        square_and_quantize(0, 1, banks01, 1)
+        square_and_quantize(1, 1, banks11, 2)
+        for h in range(2):
+            for u in range(2):
+                features(h, u)

@@ -32,8 +32,8 @@ def tile_list_duplicate_match_features_kernel(
         sb = ctx.enter_context(tc.tile_pool(name="sb", bufs=1))
         psum = ctx.enter_context(tc.psum_pool(name="psum", bufs=8))
 
-        def tile(name, shape, dtype):
-            return sb.tile(shape, dtype, name=name, align_bytes=64)
+        def tile(name, shape, dtype, tag=None):
+            return sb.tile(shape, dtype, name=name, tag=tag or name, align_bytes=64)
 
         doc_list = tile("doc_list", [P, S // 16], U16)
         query_list = tile("query_list", [P, S // 16], U16)
@@ -53,10 +53,6 @@ def tile_list_duplicate_match_features_kernel(
         nc.vector.memset(query_scale_win[:], 0)
         nc.vector.memset(doc_scales_moved[:], 0)
         nc.gpsimd.memset(vec_rows[:], 0.0)
-        halves = tile("halves", [P, 8], F32)
-        nc.gpsimd.memset(halves[:], 0.5)
-        warm = tile("warm", [P, 1], F32)
-        nc.scalar.activation(out=warm[:], in_=halves[:, 0:1], func=ACT.Tanh)
 
         def table_words(words, a):
             return words[a].rearrange("p t i -> p (t i)").bitcast(I32)
@@ -77,18 +73,13 @@ def tile_list_duplicate_match_features_kernel(
                 out=vec_rows[4 * g : 4 * g + 4, :].rearrange("t (b i) -> t b i", i=8),
                 in_=gain[512 * g : 512 * (g + 1)].rearrange("(b t i) -> t b i", t=PACK, i=8),
             )
-        bias = tile("bias", [P, 4], F32)
-        with nc.allow_non_contiguous_dma(reason="one bias value for each partition and output tile"):
-            nc.gpsimd.dma_start(out=bias[:], in_=bf.rearrange("(c p) -> p c", p=P))
 
         ident = tile("ident", [P, P], F32)
         make_identity(nc, ident[:])
         vec_bank = psum.tile([P, HALF], F32, name="vec_bank", tag="bank")
         nc.tensor.transpose(vec_bank[:, 0:P], vec_rows[:], ident[:])
-        vec_cols = tile("vec_cols", [P, 8], F32)
-        nc.scalar.copy(out=vec_cols[:], in_=vec_bank[:, 0:8])
         root_gain = tile("root_gain", [P, 8], F32)
-        nc.gpsimd.tensor_tensor(root_gain[:], vec_cols[:], halves[:], ALU.pow)
+        nc.scalar.activation(out=root_gain[:], in_=vec_bank[:, 0:8], func=ACT.Sqrt)
 
         nc.sync.dma_start(doc_list[:], offs2)
         for q in range(4):
@@ -97,28 +88,31 @@ def tile_list_duplicate_match_features_kernel(
                 in_=tab2_scales[:, 4 * q : 4 * q + 4, :].bitcast(I32),
             )
         nc.sync.dma_start(out=doc_win[0][:], in_=table_words(tab2_words, 0))
-        nc.sync.dma_start(query_list[:], offs)
-        for r in range(4):
-            nc.sync.dma_start(
-                out=query_scale_win[QUERY_PLANE + r : P : 32, :],
-                in_=tab_scales[0, r:16:4, :].bitcast(I32),
-            )
-        nc.sync.dma_start(out=query_win[:], in_=table_words(tab_words, 0))
-        load_wq(0)
-        doc_scales_picked = tile("doc_scales_picked", [P, S], U8)
-        nc.vector.tensor_copy(doc_scales_picked[:], doc_scale_win[:].bitcast(U8).indirect(doc_list[:]))
-        nc.sync.dma_start(out=doc_scales_moved[0:112, :], in_=doc_scales_picked[4:116, :].bitcast(I32))
         for r in range(4):
             nc.sync.dma_start(
                 out=wd_scale_raw[r:P:32, :, :],
                 in_=wd_scales[:, r:16:4, :].rearrange("a q c -> q a c").bitcast(I32),
             )
         load_wd(0)
+        nc.sync.dma_start(query_list[:], offs)
+        load_wq(0)
+        for r in range(4):
+            nc.sync.dma_start(
+                out=query_scale_win[QUERY_PLANE + r : P : 32, :],
+                in_=tab_scales[0, r:16:4, :].bitcast(I32),
+            )
+        nc.sync.dma_start(out=query_win[:], in_=table_words(tab_words, 0))
+        doc_scales_picked = tile("doc_scales_picked", [P, S], U8)
+        nc.vector.tensor_copy(doc_scales_picked[:], doc_scale_win[:].bitcast(U8).indirect(doc_list[:]))
+        nc.sync.dma_start(out=doc_scales_moved[0:112, :], in_=doc_scales_picked[4:116, :].bitcast(I32))
         nc.sync.dma_start(out=doc_win[1][:], in_=table_words(tab2_words, 1))
         load_wq(1)
         load_wd(1)
         load_wf(0)
         load_wf(1)
+        bias = tile("bias", [P, 4], F32)
+        with nc.allow_non_contiguous_dma(reason="one bias value for each partition and output tile"):
+            nc.sync.dma_start(out=bias[:], in_=bf.rearrange("(c p) -> p c", p=P))
 
         def gather(picked, window, offsets):
             nc.vector.tensor_copy(picked, window.bitcast(picked.dtype).indirect(offsets))
@@ -128,7 +122,8 @@ def tile_list_duplicate_match_features_kernel(
         query_codes_all = tile("query_codes_all", [P, S], U32)
         gather(doc_codes_first[:], doc_win[0][:], doc_list[:])
         gather(query_scales_all[:], query_scale_win[:], query_list[:])
-        gather(query_codes_all[:], query_win[:], query_list[:])
+        for h in range(2):
+            gather(query_codes_all[:, HALF * h : HALF * (h + 1)], query_win[:], query_list[:, 32 * h : 32 * (h + 1)])
         doc_scales, doc_codes, query_scales, query_codes = {}, {}, {}, {}
         for h in range(2):
             cols = slice(HALF * h, HALF * (h + 1))
@@ -157,9 +152,9 @@ def tile_list_duplicate_match_features_kernel(
                 in_=wd_scale_raw[:, :, 128 * g : 128 * (g + 1)].rearrange("p a (b t w) -> p a t b w", t=PACK, w=2),
             )
 
-        def quantize(name, grouped, width):
+        def quantize(name, grouped, width, plane_tag=None):
             codes = tile(name + "_codes", [P, width], U32)
-            plane = tile(name + "_plane", [P, width], U8)
+            plane = tile(name + "_plane", [P, width], U8, tag=plane_tag)
             nc.vector.quantize_mx(out=codes[:].bitcast(FP8X4), scales=plane[:], in_=grouped)
             return codes, plane
 
@@ -172,7 +167,10 @@ def tile_list_duplicate_match_features_kernel(
                     nc.scalar.activation(out=dst, in_=src, func=ACT.Copy, scale=-1.0)
                 else:
                     nc.vector.tensor_scalar(dst, src, -1.0, None, ALU.mult)
-            wq_codes[g], wq_plane[g] = quantize("wq%d" % g, grouped[:].rearrange("p t c -> p (t c)"), 512)
+            wq_codes[g], wq_plane[g] = quantize(
+                "wq%d" % g, grouped[:].rearrange("p t c -> p (t c)"), 512, "query_scale_win" if g == 0 else None
+            )
+            return grouped
 
         def interleave(dst, src):
             nc.vector.tensor_copy(
@@ -180,10 +178,28 @@ def tile_list_duplicate_match_features_kernel(
                 in_=src.rearrange("p t (c i) -> p c t i", i=4),
             )
 
+        def quantize_cols(codes, plane, grouped, first, width):
+            cols = slice(first, first + width)
+            nc.vector.quantize_mx(
+                out=codes[:, cols].bitcast(FP8X4),
+                scales=plane[:, cols],
+                in_=grouped[:, PACK * first : PACK * (first + width)],
+            )
+
+        def interleave_cols(grouped, planar, first, width):
+            interleave(grouped[:, PACK * first : PACK * (first + width)], planar[:, :, first : first + width])
+
+        def interleave_and_quantize(codes, plane, grouped, planar):
+            for first in (0, 256):
+                interleave_cols(grouped, planar, first, 256)
+            for first in (0, 256):
+                quantize_cols(codes, plane, grouped, first, 256)
+
         def prepare_wf(g):
             grouped = tile("wf_bf%d" % g, [P, PACK * N], BF16)
-            interleave(grouped[:], wf_raw[g][:])
-            wf_codes[g], wf_plane[g] = quantize("wf%d" % g, grouped[:], N)
+            wf_codes[g] = tile("wf_codes%d" % g, [P, N], U32)
+            wf_plane[g] = tile("wf_plane%d" % g, [P, N], U8)
+            interleave_and_quantize(wf_codes[g], wf_plane[g], grouped, wf_raw[g])
 
         h_codes, h_plane = {}, {}
 
@@ -217,63 +233,77 @@ def tile_list_duplicate_match_features_kernel(
                 banks.append(bank)
             return banks
 
-        def square_and_quantize(h, g, banks, pieces):
-            width = HALF // pieces
-            for u in range(pieces):
-                cols = slice(width * u, width * (u + 1))
-                planar = tile("h_planar%d%d%d" % (h, g, u), [P, PACK, width], BF16)
-                for t in range(PACK):
-                    nc.scalar.activation(
-                        out=planar[:, t, :], in_=banks[t][:, cols], func=ACT.Square,
-                        scale=root_gain[:, PACK * g + t : PACK * g + t + 1],
-                    )
-                grouped = tile("h_bf%d%d%d" % (h, g, u), [P, PACK * width], BF16)
-                interleave(grouped[:], planar[:])
-                codes, plane = quantize("h%d%d%d" % (h, g, u), grouped[:], width)
-                for v in range(width // 256):
-                    h_codes[h, g, (width * u) // 256 + v] = codes[:, 256 * v : 256 * (v + 1)]
-                    h_plane[h, g, (width * u) // 256 + v] = plane[:, 256 * v : 256 * (v + 1)]
+        h_planar, h_grouped = {}, {}
+        for h in range(2):
+            for g in range(GROUPS):
+                h_planar[h, g] = tile("h_planar%d%d" % (h, g), [P, PACK, HALF], BF16)
+                h_grouped[h, g] = tile("h_bf%d%d" % (h, g), [P, PACK * HALF], BF16, tag="wf_raw1" if (h, g) == (1, 0) else None)
+                h_codes[h, g] = tile("h_codes%d%d" % (h, g), [P, HALF], U32)
+                h_plane[h, g] = tile("h_plane%d%d" % (h, g), [P, HALF], U8)
 
-        def features(h, u):
-            tokens = slice(HALF * h + 256 * u, HALF * h + 256 * (u + 1))
-            for pair in range(2):
-                bank = psum.tile([P, 2, 256], F32, name="y%d%d%d" % (h, u, pair), tag="bank")
-                for e in range(2):
-                    cols = slice(P * (2 * pair + e), P * (2 * pair + e + 1))
+        def square(h, g, banks, first, width):
+            for t in range(PACK):
+                nc.scalar.activation(
+                    out=h_planar[h, g][:, t, first : first + width],
+                    in_=banks[t][:, first : first + width],
+                    func=ACT.Square,
+                    scale=root_gain[:, PACK * g + t : PACK * g + t + 1],
+                )
+
+        def quantize_h(h, g):
+            interleave_and_quantize(h_codes[h, g], h_plane[h, g], h_grouped[h, g], h_planar[h, g])
+
+        def features(h, first, width):
+            cols = slice(first, first + width)
+            tokens = slice(HALF * h + first, HALF * h + first + width)
+            per_bank = HALF // width
+            for c0 in range(0, 4, per_bank):
+                bank = psum.tile([P, per_bank, width], F32, name="y%d%d%d" % (h, first, c0), tag="bank")
+                for e in range(per_bank):
+                    rows = slice(P * (c0 + e), P * (c0 + e + 1))
                     for g in range(GROUPS):
                         nc.tensor.matmul_mx(
                             out=bank[:, e, :],
-                            lhsT=wf_codes[g][:, cols].bitcast(FP8X4),
-                            lhsT_scale=wf_plane[g][:, cols],
-                            rhs=h_codes[h, g, u].bitcast(FP8X4),
-                            rhs_scale=h_plane[h, g, u],
+                            lhsT=wf_codes[g][:, rows].bitcast(FP8X4),
+                            lhsT_scale=wf_plane[g][:, rows],
+                            rhs=h_codes[h, g][:, cols].bitcast(FP8X4),
+                            rhs_scale=h_plane[h, g][:, cols],
                             start=(g == 0),
                             stop=(g == GROUPS - 1),
                         )
-                result = tile("result%d%d%d" % (h, u, pair), [P, 2, 256], F32)
-                for e in range(2):
-                    c = 2 * pair + e
+                result = tile("result%d%d%d" % (h, first, c0), [P, per_bank, width], F32)
+                for e in range(per_bank):
+                    c = c0 + e
                     nc.scalar.activation(out=result[:, e, :], in_=bank[:, e, :], func=ACT.Tanh, bias=bias[:, c : c + 1])
                 nc.sync.dma_start(
-                    out=out[256 * pair : 256 * (pair + 1), tokens].rearrange("(e p) j -> p e j", p=P), in_=result[:]
+                    out=out[P * c0 : P * (c0 + per_bank), tokens].rearrange("(e p) j -> p e j", p=P), in_=result[:]
                 )
 
         permute_wd(0)
-        prepare_wq(0, (0, 1, 2, 3))
+        first_wq = prepare_wq(0, (0, 1, 2, 3))
+        warm = tile("warm", [P, 1], F32)
+        nc.scalar.activation(out=warm[:], in_=first_wq[:, 3, 0:1], func=ACT.Tanh, scale=root_gain[:, 0:1])
         gather_half(0)
         banks00 = difference(0, 0)
         gather_half(1)
         banks10 = difference(1, 0)
         permute_wd(1)
         prepare_wq(1, (0, 1))
-        square_and_quantize(0, 0, banks00, 1)
+        square(0, 0, banks00, 0, HALF)
+        quantize_h(0, 0)
         banks01 = difference(0, 1)
-        square_and_quantize(1, 0, banks10, 1)
+        square(0, 1, banks01, 0, HALF)
+        square(1, 0, banks10, 0, HALF)
         banks11 = difference(1, 1)
         prepare_wf(0)
         prepare_wf(1)
-        square_and_quantize(0, 1, banks01, 1)
-        square_and_quantize(1, 1, banks11, 2)
-        for h in range(2):
-            for u in range(2):
-                features(h, u)
+        quantize_h(0, 1)
+        for first in (0, 256):
+            square(1, 1, banks11, first, 256)
+        features(0, 0, HALF)
+        for first in (0, 256):
+            for g in range(GROUPS):
+                interleave_cols(h_grouped[1, g], h_planar[1, g], first, 256)
+            for g in range(GROUPS):
+                quantize_cols(h_codes[1, g], h_plane[1, g], h_grouped[1, g], first, 256)
+            features(1, first, 256)

@@ -48,11 +48,11 @@ def tile_list_duplicate_match_features_kernel(
         wq_raw = [tile("wq_raw%d" % g, [P, PACK, 512], F32) for g in range(GROUPS)]
         wf_raw = [tile("wf_raw%d" % g, [P, PACK, N], F32) for g in range(GROUPS)]
 
-        nc.vector.memset(doc_scale_win[:], 0)
+        nc.gpsimd.memset(doc_scale_win[:], 0)
+        nc.vector.memset(vec_rows[:], 0.0)
         nc.vector.memset(wd_scale_raw[:], 0)
         nc.vector.memset(query_scale_win[:], 0)
         nc.vector.memset(doc_scales_moved[:], 0)
-        nc.gpsimd.memset(vec_rows[:], 0.0)
 
         def table_words(words, a):
             return words[a].rearrange("p t i -> p (t i)").bitcast(I32)
@@ -68,11 +68,39 @@ def tile_list_duplicate_match_features_kernel(
             for t in range(PACK):
                 nc.sync.dma_start(out=wf_raw[g][:, t, :], in_=rows[t])
 
-        for g in range(GROUPS):
-            nc.gpsimd.dma_start(
+        def load_gain(g):
+            nc.sync.dma_start(
                 out=vec_rows[4 * g : 4 * g + 4, :].rearrange("t (b i) -> t b i", i=8),
                 in_=gain[512 * g : 512 * (g + 1)].rearrange("(b t i) -> t b i", t=PACK, i=8),
             )
+
+        nc.sync.dma_start(doc_list[:], offs2)
+        load_gain(0)
+        for r in range(4):
+            nc.sync.dma_start(
+                out=doc_scale_win[r:P:16, :],
+                in_=tab2_scales[:, r:16:4, :].rearrange("a q c -> q a c").bitcast(I32),
+            )
+        nc.sync.dma_start(out=doc_win[0][:], in_=table_words(tab2_words, 0))
+        load_wd(0)
+        load_gain(1)
+        for r in range(4):
+            nc.sync.dma_start(
+                out=wd_scale_raw[r:P:32, :, :],
+                in_=wd_scales[:, r:16:4, :].rearrange("a q c -> q a c").bitcast(I32),
+            )
+        load_wq(0)
+        nc.sync.dma_start(query_list[:], offs)
+        for r in range(4):
+            nc.sync.dma_start(
+                out=query_scale_win[QUERY_PLANE + r : P : 32, :],
+                in_=tab_scales[0, r:16:4, :].bitcast(I32),
+            )
+        nc.sync.dma_start(out=doc_win[1][:], in_=table_words(tab2_words, 1))
+        doc_scales_picked = tile("doc_scales_picked", [P, S], U8)
+        nc.vector.tensor_copy(doc_scales_picked[:], doc_scale_win[:].bitcast(U8).indirect(doc_list[:]))
+        nc.sync.dma_start(out=doc_scales_moved[0:112, :], in_=doc_scales_picked[16:128, :].bitcast(I32))
+        nc.sync.dma_start(out=query_win[:], in_=table_words(tab_words, 0))
 
         ident = tile("ident", [P, P], F32)
         make_identity(nc, ident[:])
@@ -80,34 +108,11 @@ def tile_list_duplicate_match_features_kernel(
         nc.tensor.transpose(vec_bank[:, 0:P], vec_rows[:], ident[:])
         root_gain = tile("root_gain", [P, 8], F32)
         nc.scalar.activation(out=root_gain[:], in_=vec_bank[:, 0:8], func=ACT.Sqrt)
+        warm = tile("warm", [P, 1], F32)
+        nc.scalar.activation(out=warm[:], in_=root_gain[:, 0:1], func=ACT.Tanh)
 
-        nc.sync.dma_start(doc_list[:], offs2)
-        for q in range(4):
-            nc.sync.dma_start(
-                out=doc_scale_win[32 * q : 32 * q + 8, :],
-                in_=tab2_scales[:, 4 * q : 4 * q + 4, :].bitcast(I32),
-            )
-        nc.sync.dma_start(out=doc_win[0][:], in_=table_words(tab2_words, 0))
-        for r in range(4):
-            nc.sync.dma_start(
-                out=wd_scale_raw[r:P:32, :, :],
-                in_=wd_scales[:, r:16:4, :].rearrange("a q c -> q a c").bitcast(I32),
-            )
-        load_wd(0)
-        nc.sync.dma_start(query_list[:], offs)
-        load_wq(0)
-        for r in range(4):
-            nc.sync.dma_start(
-                out=query_scale_win[QUERY_PLANE + r : P : 32, :],
-                in_=tab_scales[0, r:16:4, :].bitcast(I32),
-            )
-        nc.sync.dma_start(out=query_win[:], in_=table_words(tab_words, 0))
-        doc_scales_picked = tile("doc_scales_picked", [P, S], U8)
-        nc.vector.tensor_copy(doc_scales_picked[:], doc_scale_win[:].bitcast(U8).indirect(doc_list[:]))
-        nc.sync.dma_start(out=doc_scales_moved[0:112, :], in_=doc_scales_picked[4:116, :].bitcast(I32))
-        nc.sync.dma_start(out=doc_win[1][:], in_=table_words(tab2_words, 1))
-        load_wq(1)
         load_wd(1)
+        load_wq(1)
         load_wf(0)
         load_wf(1)
         bias = tile("bias", [P, 4], F32)
@@ -119,11 +124,8 @@ def tile_list_duplicate_match_features_kernel(
 
         doc_codes_first = tile("doc_codes_first", [P, S], U32)
         query_scales_all = tile("query_scales_all", [P, S], U8)
-        query_codes_all = tile("query_codes_all", [P, S], U32)
         gather(doc_codes_first[:], doc_win[0][:], doc_list[:])
         gather(query_scales_all[:], query_scale_win[:], query_list[:])
-        for h in range(2):
-            gather(query_codes_all[:, HALF * h : HALF * (h + 1)], query_win[:], query_list[:, 32 * h : 32 * (h + 1)])
         doc_scales, doc_codes, query_scales, query_codes = {}, {}, {}, {}
         for h in range(2):
             cols = slice(HALF * h, HALF * (h + 1))
@@ -131,49 +133,51 @@ def tile_list_duplicate_match_features_kernel(
             doc_scales[h, 1] = doc_scales_moved[:].bitcast(U8)[:, cols]
             doc_codes[h, 0] = doc_codes_first[:, cols]
             query_scales[h] = query_scales_all[QUERY_PLANE:P, cols]
-            query_codes[h] = query_codes_all[:, cols]
 
         def gather_half(h):
             picked = tile("doc_codes_second%d" % h, [P, HALF], U32)
             gather(picked[:], doc_win[1][:], doc_list[:, 32 * h : 32 * (h + 1)])
             doc_codes[h, 1] = picked[:]
 
+        def gather_query(h):
+            picked = tile("query_codes%d" % h, [P, HALF], U32)
+            gather(picked[:], query_win[:], query_list[:, 32 * h : 32 * (h + 1)])
+            query_codes[h] = picked[:]
+
         wd_codes, wd_plane, wq_codes, wq_plane, wf_codes, wf_plane = {}, {}, {}, {}, {}, {}
 
-        def permute_wd(g):
+        def permute_wd_codes(g):
             wd_codes[g] = tile("wd_codes%d" % g, [P, 2, PACK, 256], U8)
             nc.vector.tensor_copy(
                 out=wd_codes[g][:].bitcast(I32).rearrange("p a t (b w) -> p a t b w", w=4),
                 in_=wd_raw[g][:].rearrange("p a (b t w) -> p a t b w", t=PACK, w=4),
             )
-            wd_plane[g] = tile("wd_plane%d" % g, [P, 2, PACK, P], U8)
+
+        def permute_wd_scales(g, first, count, plane):
             nc.vector.tensor_copy(
-                out=wd_plane[g][:].bitcast(I32).rearrange("p a t (b w) -> p a t b w", w=2),
-                in_=wd_scale_raw[:, :, 128 * g : 128 * (g + 1)].rearrange("p a (b t w) -> p a t b w", t=PACK, w=2),
+                out=plane.bitcast(I32).rearrange("p (a t b w) -> p a t b w", a=2, t=count, w=2),
+                in_=wd_scale_raw[:, :, 128 * g : 128 * (g + 1)].rearrange("p a (b t w) -> p a t b w", t=PACK, w=2)[
+                    :, :, first : first + count
+                ],
             )
+            for a in range(2):
+                for e in range(count):
+                    wd_plane[g, a, first + e] = plane[:, P * (count * a + e) : P * (count * a + e + 1)]
 
-        def quantize(name, grouped, width, plane_tag=None):
-            codes = tile(name + "_codes", [P, width], U32)
-            plane = tile(name + "_plane", [P, width], U8, tag=plane_tag)
-            nc.vector.quantize_mx(out=codes[:].bitcast(FP8X4), scales=plane[:], in_=grouped)
-            return codes, plane
+        def prepare_wq(g, plane):
+            grouped = tile("wq_bf%d" % g, [P, PACK * 512], BF16)
+            dst = grouped[:].rearrange("p (t b i j) -> p b t i j", t=PACK, i=8, j=PACK)
+            src = wq_raw[g][:].rearrange("p j (b t i) -> p b t i j", t=PACK, i=8)
+            if g == 0:
+                nc.scalar.activation(out=dst, in_=src, func=ACT.Copy, scale=-1.0)
+            else:
+                nc.vector.tensor_scalar(dst, src, -1.0, None, ALU.mult)
+            wq_codes[g] = tile("wq_codes%d" % g, [P, 512], U32)
+            wq_plane[g] = plane
+            nc.vector.quantize_mx(out=wq_codes[g][:].bitcast(FP8X4), scales=plane, in_=grouped[:])
 
-        def prepare_wq(g, on_scalar):
-            grouped = tile("wq_bf%d" % g, [P, PACK, 512], BF16)
-            for t in range(PACK):
-                dst = grouped[:, t, :].rearrange("p (b i j) -> p b i j", i=8, j=PACK)
-                src = wq_raw[g][:].rearrange("p j (b t i) -> p t b i j", t=PACK, i=8)[:, t]
-                if t in on_scalar:
-                    nc.scalar.activation(out=dst, in_=src, func=ACT.Copy, scale=-1.0)
-                else:
-                    nc.vector.tensor_scalar(dst, src, -1.0, None, ALU.mult)
-            wq_codes[g], wq_plane[g] = quantize(
-                "wq%d" % g, grouped[:].rearrange("p t c -> p (t c)"), 512, "query_scale_win" if g == 0 else None
-            )
-            return grouped
-
-        def interleave(dst, src):
-            nc.vector.tensor_copy(
+        def interleave(dst, src, copy=nc.vector.tensor_copy):
+            copy(
                 out=dst.rearrange("p (c i t) -> p c t i", i=4, t=PACK),
                 in_=src.rearrange("p t (c i) -> p c t i", i=4),
             )
@@ -186,8 +190,8 @@ def tile_list_duplicate_match_features_kernel(
                 in_=grouped[:, PACK * first : PACK * (first + width)],
             )
 
-        def interleave_cols(grouped, planar, first, width):
-            interleave(grouped[:, PACK * first : PACK * (first + width)], planar[:, :, first : first + width])
+        def interleave_cols(grouped, planar, first, width, copy=nc.vector.tensor_copy):
+            interleave(grouped[:, PACK * first : PACK * (first + width)], planar[:, :, first : first + width], copy)
 
         def interleave_and_quantize(codes, plane, grouped, planar):
             for first in (0, 256):
@@ -207,11 +211,11 @@ def tile_list_duplicate_match_features_kernel(
             nc.tensor.matmul_mx(
                 out=bank[:],
                 lhsT=wd_codes[g][:, a, t, :].bitcast(FP4X4),
-                lhsT_scale=wd_plane[g][:, a, t, :],
+                lhsT_scale=wd_plane[g, a, t],
                 rhs=doc_codes[h, a].bitcast(FP8X4),
                 rhs_scale=doc_scales[h, a],
                 start=(a == 0),
-                stop=(a == 1),
+                stop=False,
             )
 
         def difference(h, g):
@@ -219,6 +223,7 @@ def tile_list_duplicate_match_features_kernel(
             for t in range(PACK):
                 bank = psum.tile([P, HALF], F32, name="diff%d%d%d" % (h, g, t), tag="bank")
                 doc_pass(bank, h, g, t, 0)
+                doc_pass(bank, h, g, t, 1)
                 cols = slice(P * t, P * (t + 1))
                 nc.tensor.matmul_mx(
                     out=bank[:],
@@ -227,19 +232,24 @@ def tile_list_duplicate_match_features_kernel(
                     rhs=query_codes[h].bitcast(FP8X4),
                     rhs_scale=query_scales[h],
                     start=False,
-                    stop=False,
+                    stop=True,
                 )
-                doc_pass(bank, h, g, t, 1)
                 banks.append(bank)
             return banks
 
+        PIECE = 256
         h_planar, h_grouped = {}, {}
+        first_grouped = tile("h_bf_first", [P, PACK * PIECE], BF16, tag="wq_raw1")
+        later_grouped = tile("h_bf_later", [P, 7 * PACK * PIECE], BF16, tag="wf_raw1")
         for h in range(2):
             for g in range(GROUPS):
                 h_planar[h, g] = tile("h_planar%d%d" % (h, g), [P, PACK, HALF], BF16)
-                h_grouped[h, g] = tile("h_bf%d%d" % (h, g), [P, PACK * HALF], BF16, tag="wf_raw1" if (h, g) == (1, 0) else None)
                 h_codes[h, g] = tile("h_codes%d%d" % (h, g), [P, HALF], U32)
                 h_plane[h, g] = tile("h_plane%d%d" % (h, g), [P, HALF], U8)
+        for k in range(4):
+            for g in range(GROUPS):
+                n = GROUPS * k + g - 1
+                h_grouped[k, g] = first_grouped[:] if n < 0 else later_grouped[:, PACK * PIECE * n : PACK * PIECE * (n + 1)]
 
         def square(h, g, banks, first, width):
             for t in range(PACK):
@@ -250,46 +260,53 @@ def tile_list_duplicate_match_features_kernel(
                     scale=root_gain[:, PACK * g + t : PACK * g + t + 1],
                 )
 
-        def quantize_h(h, g):
-            interleave_and_quantize(h_codes[h, g], h_plane[h, g], h_grouped[h, g], h_planar[h, g])
+        def piece_cols(k):
+            return slice(PIECE * (k % 2), PIECE * (k % 2 + 1))
 
-        def features(h, first, width):
-            cols = slice(first, first + width)
-            tokens = slice(HALF * h + first, HALF * h + first + width)
-            per_bank = HALF // width
-            for c0 in range(0, 4, per_bank):
-                bank = psum.tile([P, per_bank, width], F32, name="y%d%d%d" % (h, first, c0), tag="bank")
-                for e in range(per_bank):
-                    rows = slice(P * (c0 + e), P * (c0 + e + 1))
-                    for g in range(GROUPS):
-                        nc.tensor.matmul_mx(
-                            out=bank[:, e, :],
-                            lhsT=wf_codes[g][:, rows].bitcast(FP8X4),
-                            lhsT_scale=wf_plane[g][:, rows],
-                            rhs=h_codes[h, g][:, cols].bitcast(FP8X4),
-                            rhs_scale=h_plane[h, g][:, cols],
-                            start=(g == 0),
-                            stop=(g == GROUPS - 1),
-                        )
-                result = tile("result%d%d%d" % (h, first, c0), [P, per_bank, width], F32)
-                for e in range(per_bank):
-                    c = c0 + e
-                    nc.scalar.activation(out=result[:, e, :], in_=bank[:, e, :], func=ACT.Tanh, bias=bias[:, c : c + 1])
-                nc.sync.dma_start(
-                    out=out[P * c0 : P * (c0 + per_bank), tokens].rearrange("(e p) j -> p e j", p=P), in_=result[:]
-                )
+        def weave(k, g, copy=nc.vector.tensor_copy):
+            interleave(h_grouped[k, g], h_planar[k // 2, g][:, :, piece_cols(k)], copy)
 
-        permute_wd(0)
-        first_wq = prepare_wq(0, (0, 1, 2, 3))
-        warm = tile("warm", [P, 1], F32)
-        nc.scalar.activation(out=warm[:], in_=first_wq[:, 3, 0:1], func=ACT.Tanh, scale=root_gain[:, 0:1])
+        def quantize_h(k, g):
+            nc.vector.quantize_mx(
+                out=h_codes[k // 2, g][:, piece_cols(k)].bitcast(FP8X4),
+                scales=h_plane[k // 2, g][:, piece_cols(k)],
+                in_=h_grouped[k, g],
+            )
+
+        def features(k):
+            tokens = slice(PIECE * k, PIECE * (k + 1))
+            banks = [psum.tile([P, PIECE], F32, name="y%d%d" % (k, c), tag="bank") for c in range(4)]
+            for g in range(GROUPS):
+                for c in range(4):
+                    rows = slice(P * c, P * (c + 1))
+                    nc.tensor.matmul_mx(
+                        out=banks[c][:],
+                        lhsT=wf_codes[g][:, rows].bitcast(FP8X4),
+                        lhsT_scale=wf_plane[g][:, rows],
+                        rhs=h_codes[k // 2, g][:, piece_cols(k)].bitcast(FP8X4),
+                        rhs_scale=h_plane[k // 2, g][:, piece_cols(k)],
+                        start=(g == 0),
+                        stop=(g == GROUPS - 1),
+                    )
+            for c in range(4):
+                result = tile("result%d%d" % (k, c), [P, PIECE], F32)
+                nc.scalar.activation(out=result[:], in_=banks[c][:], func=ACT.Tanh, bias=bias[:, c : c + 1])
+                nc.sync.dma_start(out=out[P * c : P * (c + 1), tokens], in_=result[:])
+
+        permute_wd_codes(0)
+        permute_wd_scales(0, 0, PACK, tile("wd_plane_first", [P, 1024], U8)[:])
         gather_half(0)
-        banks00 = difference(0, 0)
         gather_half(1)
+        prepare_wq(0, tile("wq_plane_first", [P, 512], U8, tag="doc_win1")[:])
+        gather_query(0)
+        banks00 = difference(0, 0)
+        gather_query(1)
         banks10 = difference(1, 0)
-        permute_wd(1)
-        prepare_wq(1, (0, 1))
+        permute_wd_codes(1)
+        permute_wd_scales(1, 0, PACK, tile("wd_plane_second", [P, 1024], U8)[:])
+        prepare_wq(1, tile("wq_plane_second", [P, 512], U8)[:])
         square(0, 0, banks00, 0, HALF)
+        weave(0, 0)
         quantize_h(0, 0)
         banks01 = difference(0, 1)
         square(0, 1, banks01, 0, HALF)
@@ -297,13 +314,18 @@ def tile_list_duplicate_match_features_kernel(
         banks11 = difference(1, 1)
         prepare_wf(0)
         prepare_wf(1)
+        square(1, 1, banks11, 0, HALF)
+        weave(0, 1)
+        weave(1, 0)
         quantize_h(0, 1)
-        for first in (0, 256):
-            square(1, 1, banks11, first, 256)
-        features(0, 0, HALF)
-        for first in (0, 256):
+        features(0)
+        weave(1, 1)
+        quantize_h(1, 0)
+        quantize_h(1, 1)
+        features(1)
+        for k in (2, 3):
             for g in range(GROUPS):
-                interleave_cols(h_grouped[1, g], h_planar[1, g], first, 256)
+                weave(k, g)
             for g in range(GROUPS):
-                quantize_cols(h_codes[1, g], h_plane[1, g], h_grouped[1, g], first, 256)
-            features(1, first, 256)
+                quantize_h(k, g)
+            features(k)

@@ -75,12 +75,12 @@ def tile_list_duplicate_match_features_kernel(
             )
 
         nc.sync.dma_start(doc_list[:], offs2)
-        load_gain(0)
         for r in range(4):
             nc.sync.dma_start(
                 out=doc_scale_win[r:P:16, :],
                 in_=tab2_scales[:, r:16:4, :].rearrange("a q c -> q a c").bitcast(I32),
             )
+        load_gain(0)
         nc.sync.dma_start(out=doc_win[0][:], in_=table_words(tab2_words, 0))
         load_wd(0)
         load_gain(1)
@@ -89,6 +89,9 @@ def tile_list_duplicate_match_features_kernel(
                 out=wd_scale_raw[r:P:32, :, :],
                 in_=wd_scales[:, r:16:4, :].rearrange("a q c -> q a c").bitcast(I32),
             )
+        nc.sync.dma_start(out=doc_win[1][:], in_=table_words(tab2_words, 1))
+        doc_scales_picked = tile("doc_scales_picked", [P, S], U8)
+        nc.vector.tensor_copy(doc_scales_picked[:], doc_scale_win[:].bitcast(U8).indirect(doc_list[:]))
         load_wq(0)
         nc.sync.dma_start(query_list[:], offs)
         for r in range(4):
@@ -96,9 +99,6 @@ def tile_list_duplicate_match_features_kernel(
                 out=query_scale_win[QUERY_PLANE + r : P : 32, :],
                 in_=tab_scales[0, r:16:4, :].bitcast(I32),
             )
-        nc.sync.dma_start(out=doc_win[1][:], in_=table_words(tab2_words, 1))
-        doc_scales_picked = tile("doc_scales_picked", [P, S], U8)
-        nc.vector.tensor_copy(doc_scales_picked[:], doc_scale_win[:].bitcast(U8).indirect(doc_list[:]))
         nc.sync.dma_start(out=doc_scales_moved[0:112, :], in_=doc_scales_picked[16:128, :].bitcast(I32))
         nc.sync.dma_start(out=query_win[:], in_=table_words(tab_words, 0))
 
@@ -125,7 +125,6 @@ def tile_list_duplicate_match_features_kernel(
         doc_codes_first = tile("doc_codes_first", [P, S], U32)
         query_scales_all = tile("query_scales_all", [P, S], U8)
         gather(doc_codes_first[:], doc_win[0][:], doc_list[:])
-        gather(query_scales_all[:], query_scale_win[:], query_list[:])
         doc_scales, doc_codes, query_scales, query_codes = {}, {}, {}, {}
         for h in range(2):
             cols = slice(HALF * h, HALF * (h + 1))
@@ -168,13 +167,16 @@ def tile_list_duplicate_match_features_kernel(
             grouped = tile("wq_bf%d" % g, [P, PACK * 512], BF16)
             dst = grouped[:].rearrange("p (t b i j) -> p b t i j", t=PACK, i=8, j=PACK)
             src = wq_raw[g][:].rearrange("p j (b t i) -> p b t i j", t=PACK, i=8)
-            if g == 0:
-                nc.scalar.activation(out=dst, in_=src, func=ACT.Copy, scale=-1.0)
-            else:
-                nc.vector.tensor_scalar(dst, src, -1.0, None, ALU.mult)
             wq_codes[g] = tile("wq_codes%d" % g, [P, 512], U32)
             wq_plane[g] = plane
-            nc.vector.quantize_mx(out=wq_codes[g][:].bitcast(FP8X4), scales=plane, in_=grouped[:])
+            if g == 0:
+                nc.scalar.activation(out=dst, in_=src, func=ACT.Copy, scale=-1.0)
+                nc.vector.quantize_mx(out=wq_codes[g][:].bitcast(FP8X4), scales=plane, in_=grouped[:])
+            else:
+                for t in (0, 2):
+                    nc.vector.tensor_scalar(dst[:, :, t : t + 2], src[:, :, t : t + 2], -1.0, None, ALU.mult)
+                for first in (0, 256):
+                    quantize_cols(wq_codes[g], plane, grouped, first, 256)
 
         def interleave(dst, src, copy=nc.vector.tensor_copy):
             copy(
@@ -204,8 +206,6 @@ def tile_list_duplicate_match_features_kernel(
             wf_codes[g] = tile("wf_codes%d" % g, [P, N], U32)
             wf_plane[g] = tile("wf_plane%d" % g, [P, N], U8)
             interleave_and_quantize(wf_codes[g], wf_plane[g], grouped, wf_raw[g])
-
-        h_codes, h_plane = {}, {}
 
         def doc_pass(bank, h, g, t, a):
             nc.tensor.matmul_mx(
@@ -237,45 +237,42 @@ def tile_list_duplicate_match_features_kernel(
                 banks.append(bank)
             return banks
 
-        PIECE = 256
-        h_planar, h_grouped = {}, {}
-        first_grouped = tile("h_bf_first", [P, PACK * PIECE], BF16, tag="wq_raw1")
-        later_grouped = tile("h_bf_later", [P, 7 * PACK * PIECE], BF16, tag="wf_raw1")
+        h_planar = {}
+        first_grouped = tile("h_bf_first", [P, PACK * 256], BF16, tag="wq_raw1")
+        later_grouped = tile("h_bf_later", [P, GROUPS * PACK * S], BF16, tag="wf_raw1")
+        h_codes = [tile("h_codes%d" % g, [P, S], U32) for g in range(GROUPS)]
+        h_plane = [tile("h_plane%d" % g, [P, S], U8) for g in range(GROUPS)]
         for h in range(2):
             for g in range(GROUPS):
                 h_planar[h, g] = tile("h_planar%d%d" % (h, g), [P, PACK, HALF], BF16)
-                h_codes[h, g] = tile("h_codes%d%d" % (h, g), [P, HALF], U32)
-                h_plane[h, g] = tile("h_plane%d%d" % (h, g), [P, HALF], U8)
-        for k in range(4):
-            for g in range(GROUPS):
-                n = GROUPS * k + g - 1
-                h_grouped[k, g] = first_grouped[:] if n < 0 else later_grouped[:, PACK * PIECE * n : PACK * PIECE * (n + 1)]
 
-        def square(h, g, banks, first, width):
+        def h_grouped(g, first, width):
+            if g == 0 and first < 256:
+                return first_grouped[:, PACK * first : PACK * (first + width)]
+            return later_grouped[:, PACK * (S * g + first) : PACK * (S * g + first + width)]
+
+        def square(h, g, banks):
             for t in range(PACK):
                 nc.scalar.activation(
-                    out=h_planar[h, g][:, t, first : first + width],
-                    in_=banks[t][:, first : first + width],
+                    out=h_planar[h, g][:, t, :],
+                    in_=banks[t][:],
                     func=ACT.Square,
                     scale=root_gain[:, PACK * g + t : PACK * g + t + 1],
                 )
 
-        def piece_cols(k):
-            return slice(PIECE * (k % 2), PIECE * (k % 2 + 1))
+        def weave(g, first, width, copy=nc.vector.tensor_copy):
+            start = first % HALF
+            interleave(h_grouped(g, first, width), h_planar[first // HALF, g][:, :, start : start + width], copy)
 
-        def weave(k, g, copy=nc.vector.tensor_copy):
-            interleave(h_grouped[k, g], h_planar[k // 2, g][:, :, piece_cols(k)], copy)
-
-        def quantize_h(k, g):
+        def quantize_h(g, first, width):
+            cols = slice(first, first + width)
             nc.vector.quantize_mx(
-                out=h_codes[k // 2, g][:, piece_cols(k)].bitcast(FP8X4),
-                scales=h_plane[k // 2, g][:, piece_cols(k)],
-                in_=h_grouped[k, g],
+                out=h_codes[g][:, cols].bitcast(FP8X4), scales=h_plane[g][:, cols], in_=h_grouped(g, first, width)
             )
 
-        def features(k):
-            tokens = slice(PIECE * k, PIECE * (k + 1))
-            banks = [psum.tile([P, PIECE], F32, name="y%d%d" % (k, c), tag="bank") for c in range(4)]
+        def features(first, width):
+            tokens = slice(first, first + width)
+            banks = [psum.tile([P, width], F32, name="y%d_%d" % (first, c), tag="bank") for c in range(4)]
             for g in range(GROUPS):
                 for c in range(4):
                     rows = slice(P * c, P * (c + 1))
@@ -283,21 +280,26 @@ def tile_list_duplicate_match_features_kernel(
                         out=banks[c][:],
                         lhsT=wf_codes[g][:, rows].bitcast(FP8X4),
                         lhsT_scale=wf_plane[g][:, rows],
-                        rhs=h_codes[k // 2, g][:, piece_cols(k)].bitcast(FP8X4),
-                        rhs_scale=h_plane[k // 2, g][:, piece_cols(k)],
+                        rhs=h_codes[g][:, tokens].bitcast(FP8X4),
+                        rhs_scale=h_plane[g][:, tokens],
                         start=(g == 0),
                         stop=(g == GROUPS - 1),
                     )
-            for c in range(4):
-                result = tile("result%d%d" % (k, c), [P, PIECE], F32)
-                nc.scalar.activation(out=result[:], in_=banks[c][:], func=ACT.Tanh, bias=bias[:, c : c + 1])
-                nc.sync.dma_start(out=out[P * c : P * (c + 1), tokens], in_=result[:])
+            for c0 in (0, 2):
+                result = tile("result%d_%d" % (first, c0), [P, 2, width], F32)
+                for e in range(2):
+                    c = c0 + e
+                    nc.scalar.activation(out=result[:, e, :], in_=banks[c][:], func=ACT.Tanh, bias=bias[:, c : c + 1])
+                nc.sync.dma_start(
+                    out=out[P * c0 : P * (c0 + 2), tokens].rearrange("(e p) j -> p e j", p=P), in_=result[:]
+                )
 
         permute_wd_codes(0)
         permute_wd_scales(0, 0, PACK, tile("wd_plane_first", [P, 1024], U8)[:])
         gather_half(0)
         gather_half(1)
-        prepare_wq(0, tile("wq_plane_first", [P, 512], U8, tag="doc_win1")[:])
+        gather(query_scales_all[:], query_scale_win[:], query_list[:])
+        prepare_wq(0, tile("wq_plane_first", [P, 512], U8, tag="query_scale_win")[:])
         gather_query(0)
         banks00 = difference(0, 0)
         gather_query(1)
@@ -305,27 +307,36 @@ def tile_list_duplicate_match_features_kernel(
         permute_wd_codes(1)
         permute_wd_scales(1, 0, PACK, tile("wd_plane_second", [P, 1024], U8)[:])
         prepare_wq(1, tile("wq_plane_second", [P, 512], U8)[:])
-        square(0, 0, banks00, 0, HALF)
-        weave(0, 0)
-        quantize_h(0, 0)
+        square(0, 0, banks00)
+        for first in (0, 128):
+            weave(0, first, 128)
+        for first in (0, 128):
+            quantize_h(0, first, 128)
         banks01 = difference(0, 1)
-        square(0, 1, banks01, 0, HALF)
-        square(1, 0, banks10, 0, HALF)
+        square(0, 1, banks01)
+        square(1, 0, banks10)
         banks11 = difference(1, 1)
         prepare_wf(0)
         prepare_wf(1)
-        square(1, 1, banks11, 0, HALF)
-        weave(0, 1)
-        weave(1, 0)
-        quantize_h(0, 1)
-        features(0)
-        weave(1, 1)
-        quantize_h(1, 0)
-        quantize_h(1, 1)
-        features(1)
-        for k in (2, 3):
-            for g in range(GROUPS):
-                weave(k, g)
-            for g in range(GROUPS):
-                quantize_h(k, g)
-            features(k)
+        square(1, 1, banks11)
+        weave(0, 512, 256, nc.scalar.copy)
+        weave(1, 0, 256)
+        weave(0, 256, 256)
+        quantize_h(1, 0, 256)
+        features(0, 256)
+        weave(1, 256, 256)
+        quantize_h(0, 256, 256)
+        weave(1, 512, 256)
+        quantize_h(1, 256, 256)
+        features(256, 256)
+        quantize_h(0, 512, 256)
+        weave(0, 768, 256)
+        quantize_h(1, 512, 256)
+        features(512, 256)
+        weave(1, 768, 128)
+        quantize_h(0, 768, 256)
+        quantize_h(1, 768, 128)
+        features(768, 128)
+        weave(1, 896, 128)
+        quantize_h(1, 896, 128)
+        features(896, 128)

@@ -1,7 +1,6 @@
 from contextlib import ExitStack
 
 import concourse.mybir as mybir
-from concourse.masks import make_identity
 
 K, K2, H, N, T, S = 512, 1024, 1024, 512, 2048, 1024
 FLOPS = 2 * S * (K * H + K2 * H + H * N)
@@ -41,7 +40,7 @@ def tile_list_duplicate_match_features_kernel(
         doc_scales_moved = tile("doc_scales_moved", [P, S // 4], I32)
         query_scale_win = tile("query_scale_win", [P, T // 4], I32)
         wd_scale_raw = tile("wd_scale_raw", [P, 2, H // 4], I32)
-        vec_rows = tile("vec_rows", [P, P], F32)
+        gain_cols = tile("gain_cols", [P, GROUPS, PACK], F32)
         doc_win = [tile("doc_win%d" % a, [P, T], I32) for a in range(2)]
         query_win = tile("query_win", [P, T], I32)
         wd_raw = [tile("wd_raw%d" % g, [P, 2, 256], I32) for g in range(GROUPS)]
@@ -49,7 +48,6 @@ def tile_list_duplicate_match_features_kernel(
         wf_raw = [tile("wf_raw%d" % g, [P, PACK, N], F32) for g in range(GROUPS)]
 
         nc.gpsimd.memset(doc_scale_win[:], 0)
-        nc.vector.memset(vec_rows[:], 0.0)
         nc.vector.memset(wd_scale_raw[:], 0)
         nc.vector.memset(query_scale_win[:], 0)
         nc.vector.memset(doc_scales_moved[:], 0)
@@ -64,15 +62,7 @@ def tile_list_duplicate_match_features_kernel(
             nc.sync.dma_start(out=wq_raw[g][:], in_=wq[:, 512 * g : 512 * (g + 1)].rearrange("(p j) c -> p j c", j=PACK))
 
         def load_wf(g):
-            rows = wf[512 * g : 512 * (g + 1), :].rearrange("(b t i) n -> t b i n", t=PACK, i=8)
-            for t in range(PACK):
-                nc.sync.dma_start(out=wf_raw[g][:, t, :], in_=rows[t])
-
-        def load_gain(g):
-            nc.sync.dma_start(
-                out=vec_rows[4 * g : 4 * g + 4, :].rearrange("t (b i) -> t b i", i=8),
-                in_=gain[512 * g : 512 * (g + 1)].rearrange("(b t i) -> t b i", t=PACK, i=8),
-            )
+            nc.sync.dma_start(out=wf_raw[g][:], in_=wf[512 * g : 512 * (g + 1), :].rearrange("(p t) n -> p t n", t=PACK))
 
         nc.sync.dma_start(doc_list[:], offs2)
         for r in range(4):
@@ -80,10 +70,9 @@ def tile_list_duplicate_match_features_kernel(
                 out=doc_scale_win[r:P:16, :],
                 in_=tab2_scales[:, r:16:4, :].rearrange("a q c -> q a c").bitcast(I32),
             )
-        load_gain(0)
+        nc.sync.dma_start(out=gain_cols[:], in_=gain.rearrange("(g p t) -> p g t", g=GROUPS, t=PACK))
         nc.sync.dma_start(out=doc_win[0][:], in_=table_words(tab2_words, 0))
         load_wd(0)
-        load_gain(1)
         for r in range(4):
             nc.sync.dma_start(
                 out=wd_scale_raw[r:P:32, :, :],
@@ -102,12 +91,8 @@ def tile_list_duplicate_match_features_kernel(
         nc.sync.dma_start(out=doc_scales_moved[0:112, :], in_=doc_scales_picked[16:128, :].bitcast(I32))
         nc.sync.dma_start(out=query_win[:], in_=table_words(tab_words, 0))
 
-        ident = tile("ident", [P, P], F32)
-        make_identity(nc, ident[:])
-        vec_bank = psum.tile([P, HALF], F32, name="vec_bank", tag="bank")
-        nc.tensor.transpose(vec_bank[:, 0:P], vec_rows[:], ident[:])
-        root_gain = tile("root_gain", [P, 8], F32)
-        nc.scalar.activation(out=root_gain[:], in_=vec_bank[:, 0:8], func=ACT.Sqrt)
+        root_gain = tile("root_gain", [P, GROUPS * PACK], F32)
+        nc.scalar.activation(out=root_gain[:], in_=gain_cols[:].rearrange("p g t -> p (g t)"), func=ACT.Sqrt)
         warm = tile("warm", [P, 1], F32)
         nc.scalar.activation(out=warm[:], in_=root_gain[:, 0:1], func=ACT.Tanh)
 
@@ -148,35 +133,37 @@ def tile_list_duplicate_match_features_kernel(
         def permute_wd_codes(g):
             wd_codes[g] = tile("wd_codes%d" % g, [P, 2, PACK, 256], U8)
             nc.vector.tensor_copy(
-                out=wd_codes[g][:].bitcast(I32).rearrange("p a t (b w) -> p a t b w", w=4),
-                in_=wd_raw[g][:].rearrange("p a (b t w) -> p a t b w", t=PACK, w=4),
+                out=wd_codes[g][:].bitcast(U16),
+                in_=wd_raw[g][:].bitcast(U16).rearrange("p a (m t) -> p a t m", t=PACK),
             )
 
-        def permute_wd_scales(g, first, count, plane):
+        def permute_wd_scales(g, plane_tag):
+            plane = tile("wd_plane%d" % g, [P, 2, PACK, P], U8, tag=plane_tag)
             nc.vector.tensor_copy(
-                out=plane.bitcast(I32).rearrange("p (a t b w) -> p a t b w", a=2, t=count, w=2),
-                in_=wd_scale_raw[:, :, 128 * g : 128 * (g + 1)].rearrange("p a (b t w) -> p a t b w", t=PACK, w=2)[
-                    :, :, first : first + count
-                ],
+                out=plane[:],
+                in_=wd_scale_raw[:, :, 128 * g : 128 * (g + 1)].bitcast(U8).rearrange("p a (m t) -> p a t m", t=PACK),
             )
             for a in range(2):
-                for e in range(count):
-                    wd_plane[g, a, first + e] = plane[:, P * (count * a + e) : P * (count * a + e + 1)]
+                for t in range(PACK):
+                    wd_plane[g, a, t] = plane[:, a, t, :]
 
-        def prepare_wq(g, plane):
-            grouped = tile("wq_bf%d" % g, [P, PACK * 512], BF16)
-            dst = grouped[:].rearrange("p (t b i j) -> p b t i j", t=PACK, i=8, j=PACK)
-            src = wq_raw[g][:].rearrange("p j (b t i) -> p b t i j", t=PACK, i=8)
-            wq_codes[g] = tile("wq_codes%d" % g, [P, 512], U32)
-            wq_plane[g] = plane
+        wq_grouped = {}
+
+        def cast_wq(g):
+            wq_grouped[g] = tile("wq_bf%d" % g, [P, PACK * 512], BF16)
+            dst = wq_grouped[g][:].rearrange("p (t m j) -> p m t j", t=PACK, j=PACK)
+            src = wq_raw[g][:].rearrange("p j (m t) -> p m t j", t=PACK)
             if g == 0:
                 nc.scalar.activation(out=dst, in_=src, func=ACT.Copy, scale=-1.0)
-                nc.vector.quantize_mx(out=wq_codes[g][:].bitcast(FP8X4), scales=plane, in_=grouped[:])
             else:
                 for t in (0, 2):
                     nc.vector.tensor_scalar(dst[:, :, t : t + 2], src[:, :, t : t + 2], -1.0, None, ALU.mult)
-                for first in (0, 256):
-                    quantize_cols(wq_codes[g], plane, grouped, first, 256)
+
+        def quantize_wq(g, width, plane_tag):
+            wq_codes[g] = tile("wq_codes%d" % g, [P, 512], U32)
+            wq_plane[g] = tile("wq_plane%d" % g, [P, 512], U8, tag=plane_tag)
+            for first in range(0, 512, width):
+                quantize_cols(wq_codes[g], wq_plane[g], wq_grouped[g], first, width)
 
         def interleave(dst, src, copy=nc.vector.tensor_copy):
             copy(
@@ -295,18 +282,20 @@ def tile_list_duplicate_match_features_kernel(
                 )
 
         permute_wd_codes(0)
-        permute_wd_scales(0, 0, PACK, tile("wd_plane_first", [P, 1024], U8)[:])
+        permute_wd_scales(0, None)
         gather_half(0)
         gather_half(1)
+        permute_wd_scales(1, "doc_win1")
         gather(query_scales_all[:], query_scale_win[:], query_list[:])
-        prepare_wq(0, tile("wq_plane_first", [P, 512], U8, tag="query_scale_win")[:])
+        cast_wq(0)
+        quantize_wq(0, 512, "query_scale_win")
         gather_query(0)
         banks00 = difference(0, 0)
         gather_query(1)
         banks10 = difference(1, 0)
         permute_wd_codes(1)
-        permute_wd_scales(1, 0, PACK, tile("wd_plane_second", [P, 1024], U8)[:])
-        prepare_wq(1, tile("wq_plane_second", [P, 512], U8)[:])
+        cast_wq(1)
+        quantize_wq(1, 256, None)
         square(0, 0, banks00)
         for first in (0, 128):
             weave(0, first, 128)

@@ -18,8 +18,16 @@ ALU = mybir.AluOpType
 
 P = 128
 PACK = 4
-HALF = 512
-GROUPS = 2
+PASS = P * PACK
+GROUPS = H // PASS
+DOC_PASSES = K2 // PASS
+HALF = S // 2
+LIST_HALF = HALF // 16
+OUT_TILES = N // P
+PIECE = 256
+SMALL = PIECE // 2
+ROWS = 4
+SECOND = 16
 QUERY_PLANE = 8
 
 
@@ -37,59 +45,71 @@ def tile_list_duplicate_match_features_kernel(
         doc_list = tile("doc_list", [P, S // 16], U16)
         query_list = tile("query_list", [P, S // 16], U16)
         doc_scale_win = tile("doc_scale_win", [P, T // 4], I32)
-        doc_scales_moved = tile("doc_scales_moved", [P, S // 4], I32)
+        doc_plane_second = tile("doc_plane_second", [P, S // 4], I32)
         query_scale_win = tile("query_scale_win", [P, T // 4], I32)
-        wd_scale_raw = tile("wd_scale_raw", [P, 2, H // 4], I32)
+        wd_scale_raw = tile("wd_scale_raw", [P, H // 4], I32)
+        wd_plane_second = tile("wd_plane_second", [P, H // 4], I32)
         gain_cols = tile("gain_cols", [P, GROUPS, PACK], F32)
-        doc_win = [tile("doc_win%d" % a, [P, T], I32) for a in range(2)]
+        doc_win = [tile("doc_win%d" % a, [P, T], I32) for a in range(DOC_PASSES)]
         query_win = tile("query_win", [P, T], I32)
-        wd_raw = [tile("wd_raw%d" % g, [P, 2, 256], I32) for g in range(GROUPS)]
-        wq_raw = [tile("wq_raw%d" % g, [P, PACK, 512], F32) for g in range(GROUPS)]
+        wd_raw = [tile("wd_raw%d" % g, [P, DOC_PASSES, PASS // 2], I32) for g in range(GROUPS)]
+        wq_raw = [tile("wq_raw%d" % g, [P, PACK, PASS], F32) for g in range(GROUPS)]
         wf_raw = [tile("wf_raw%d" % g, [P, PACK, N], F32) for g in range(GROUPS)]
 
         nc.gpsimd.memset(doc_scale_win[:], 0)
-        nc.vector.memset(wd_scale_raw[:], 0)
-        nc.vector.memset(query_scale_win[:], 0)
-        nc.vector.memset(doc_scales_moved[:], 0)
+        for scale_tile in (wd_scale_raw, query_scale_win, doc_plane_second, wd_plane_second):
+            nc.vector.memset(scale_tile[:], 0)
 
-        def table_words(words, a):
-            return words[a].rearrange("p t i -> p (t i)").bitcast(I32)
+        def gather(picked, window, offsets):
+            nc.vector.tensor_copy(picked, window.bitcast(picked.dtype).indirect(offsets))
+
+        def load_table(window, words, a):
+            nc.sync.dma_start(out=window[:], in_=words[a].rearrange("p t i -> p (t i)").bitcast(I32))
+
+        def load_two_planes(dst, scales):
+            for r in range(ROWS):
+                nc.sync.dma_start(
+                    out=dst[r:P:SECOND, :], in_=scales[:, r:16:ROWS, :].rearrange("a q c -> q a c").bitcast(I32)
+                )
+
+        def move_second_plane(dst, both):
+            nc.sync.dma_start(out=dst[0 : P - SECOND, :], in_=both[SECOND:P, :].bitcast(I32))
 
         def load_wd(g):
-            nc.sync.dma_start(out=wd_raw[g][:], in_=wd_words[:, :, 1024 * g : 1024 * (g + 1)].rearrange("a p c -> p a c").bitcast(I32))
+            words = wd_words[:, :, 2 * PASS * g : 2 * PASS * (g + 1)]
+            nc.sync.dma_start(out=wd_raw[g][:], in_=words.rearrange("a p c -> p a c").bitcast(I32))
 
         def load_wq(g):
-            nc.sync.dma_start(out=wq_raw[g][:], in_=wq[:, 512 * g : 512 * (g + 1)].rearrange("(p j) c -> p j c", j=PACK))
+            cols = wq[:, PASS * g : PASS * (g + 1)]
+            nc.sync.dma_start(out=wq_raw[g][:], in_=cols.rearrange("(p i) c -> p i c", i=PACK))
 
         def load_wf(g):
-            nc.sync.dma_start(out=wf_raw[g][:], in_=wf[512 * g : 512 * (g + 1), :].rearrange("(p t) n -> p t n", t=PACK))
+            rows = wf[PASS * g : PASS * (g + 1), :]
+            nc.sync.dma_start(out=wf_raw[g][:], in_=rows.rearrange("(p t) n -> p t n", t=PACK))
 
         nc.sync.dma_start(doc_list[:], offs2)
-        for r in range(4):
-            nc.sync.dma_start(
-                out=doc_scale_win[r:P:16, :],
-                in_=tab2_scales[:, r:16:4, :].rearrange("a q c -> q a c").bitcast(I32),
-            )
+        load_two_planes(doc_scale_win, tab2_scales)
         nc.sync.dma_start(out=gain_cols[:], in_=gain.rearrange("(g p t) -> p g t", g=GROUPS, t=PACK))
-        nc.sync.dma_start(out=doc_win[0][:], in_=table_words(tab2_words, 0))
+        load_table(doc_win[0], tab2_words, 0)
         load_wd(0)
-        for r in range(4):
-            nc.sync.dma_start(
-                out=wd_scale_raw[r:P:32, :, :],
-                in_=wd_scales[:, r:16:4, :].rearrange("a q c -> q a c").bitcast(I32),
-            )
-        nc.sync.dma_start(out=doc_win[1][:], in_=table_words(tab2_words, 1))
-        doc_scales_picked = tile("doc_scales_picked", [P, S], U8)
-        nc.vector.tensor_copy(doc_scales_picked[:], doc_scale_win[:].bitcast(U8).indirect(doc_list[:]))
-        load_wq(0)
+        load_two_planes(wd_scale_raw, wd_scales)
         nc.sync.dma_start(query_list[:], offs)
-        for r in range(4):
+        load_table(doc_win[1], tab2_words, 1)
+        doc_plane_both = tile("doc_plane_both", [P, S], U8)
+        gather(doc_plane_both[:], doc_scale_win[:], doc_list[:])
+        load_wq(0)
+        for r in range(ROWS):
             nc.sync.dma_start(
-                out=query_scale_win[QUERY_PLANE + r : P : 32, :],
-                in_=tab_scales[0, r:16:4, :].bitcast(I32),
+                out=query_scale_win[QUERY_PLANE + r : P : 32, :], in_=tab_scales[0, r:16:ROWS, :].bitcast(I32)
             )
-        nc.sync.dma_start(out=doc_scales_moved[0:112, :], in_=doc_scales_picked[16:128, :].bitcast(I32))
-        nc.sync.dma_start(out=query_win[:], in_=table_words(tab_words, 0))
+        move_second_plane(doc_plane_second, doc_plane_both)
+        wd_plane_both = tile("wd_plane_both", [P, H], U8)
+        nc.vector.tensor_copy(
+            out=wd_plane_both[:].rearrange("p (g t m) -> p g t m", g=GROUPS, t=PACK),
+            in_=wd_scale_raw[:].bitcast(U8).rearrange("p (g m t) -> p g t m", g=GROUPS, t=PACK),
+        )
+        move_second_plane(wd_plane_second, wd_plane_both)
+        load_table(query_win, tab_words, 0)
 
         root_gain = tile("root_gain", [P, GROUPS * PACK], F32)
         nc.scalar.activation(out=root_gain[:], in_=gain_cols[:].rearrange("p g t -> p (g t)"), func=ACT.Sqrt)
@@ -100,232 +120,192 @@ def tile_list_duplicate_match_features_kernel(
         load_wq(1)
         load_wf(0)
         load_wf(1)
-        bias = tile("bias", [P, 4], F32)
+        bias = tile("bias", [P, OUT_TILES], F32)
         with nc.allow_non_contiguous_dma(reason="one bias value for each partition and output tile"):
             nc.sync.dma_start(out=bias[:], in_=bf.rearrange("(c p) -> p c", p=P))
 
-        def gather(picked, window, offsets):
-            nc.vector.tensor_copy(picked, window.bitcast(picked.dtype).indirect(offsets))
-
         doc_codes_first = tile("doc_codes_first", [P, S], U32)
-        query_scales_all = tile("query_scales_all", [P, S], U8)
+        query_plane_all = tile("query_plane_all", [P, S], U8)
         gather(doc_codes_first[:], doc_win[0][:], doc_list[:])
-        doc_scales, doc_codes, query_scales, query_codes = {}, {}, {}, {}
-        for h in range(2):
-            cols = slice(HALF * h, HALF * (h + 1))
-            doc_scales[h, 0] = doc_scales_picked[:, cols]
-            doc_scales[h, 1] = doc_scales_moved[:].bitcast(U8)[:, cols]
-            doc_codes[h, 0] = doc_codes_first[:, cols]
-            query_scales[h] = query_scales_all[QUERY_PLANE:P, cols]
+        doc_planes = (doc_plane_both[:], doc_plane_second[:].bitcast(U8))
+        wd_planes = (wd_plane_both[:], wd_plane_second[:].bitcast(U8))
+        doc_codes = {(half, 0): doc_codes_first[:, HALF * half : HALF * (half + 1)] for half in range(2)}
+        query_codes, wd_codes, wq_woven, wq_codes, wq_plane, wf_codes, wf_plane = {}, {}, {}, {}, {}, {}, {}
 
-        def gather_half(h):
-            picked = tile("doc_codes_second%d" % h, [P, HALF], U32)
-            gather(picked[:], doc_win[1][:], doc_list[:, 32 * h : 32 * (h + 1)])
-            doc_codes[h, 1] = picked[:]
+        def gather_half(name, window, offsets, half):
+            picked = tile("%s%d" % (name, half), [P, HALF], U32)
+            gather(picked[:], window[:], offsets[:, LIST_HALF * half : LIST_HALF * (half + 1)])
+            return picked[:]
 
-        def gather_query(h):
-            picked = tile("query_codes%d" % h, [P, HALF], U32)
-            gather(picked[:], query_win[:], query_list[:, 32 * h : 32 * (h + 1)])
-            query_codes[h] = picked[:]
-
-        wd_codes, wd_plane, wq_codes, wq_plane, wf_codes, wf_plane = {}, {}, {}, {}, {}, {}
-
-        def permute_wd_codes(g):
-            wd_codes[g] = tile("wd_codes%d" % g, [P, 2, PACK, 256], U8)
+        def permute_wd(g):
+            wd_codes[g] = tile("wd_codes%d" % g, [P, DOC_PASSES, PACK, 2 * P], U8)
             nc.vector.tensor_copy(
                 out=wd_codes[g][:].bitcast(U16),
                 in_=wd_raw[g][:].bitcast(U16).rearrange("p a (m t) -> p a t m", t=PACK),
             )
 
-        def permute_wd_scales(g, plane_tag):
-            plane = tile("wd_plane%d" % g, [P, 2, PACK, P], U8, tag=plane_tag)
-            nc.vector.tensor_copy(
-                out=plane[:],
-                in_=wd_scale_raw[:, :, 128 * g : 128 * (g + 1)].bitcast(U8).rearrange("p a (m t) -> p a t m", t=PACK),
-            )
-            for a in range(2):
-                for t in range(PACK):
-                    wd_plane[g, a, t] = plane[:, a, t, :]
+        def wq_views(g):
+            wq_woven[g] = tile("wq_woven%d" % g, [P, PACK * PASS], BF16)
+            dst = wq_woven[g][:].rearrange("p (t m i) -> p m t i", t=PACK, i=PACK)
+            src = wq_raw[g][:].rearrange("p i (m t) -> p m t i", t=PACK)
+            return dst, src
 
-        wq_grouped = {}
-
-        def cast_wq(g):
-            wq_grouped[g] = tile("wq_bf%d" % g, [P, PACK * 512], BF16)
-            dst = wq_grouped[g][:].rearrange("p (t m j) -> p m t j", t=PACK, j=PACK)
-            src = wq_raw[g][:].rearrange("p j (m t) -> p m t j", t=PACK)
-            if g == 0:
-                nc.scalar.activation(out=dst, in_=src, func=ACT.Copy, scale=-1.0)
-            else:
-                for t in (0, 2):
-                    nc.vector.tensor_scalar(dst[:, :, t : t + 2], src[:, :, t : t + 2], -1.0, None, ALU.mult)
+        def quantize(codes, plane, first, width, woven):
+            cols = slice(first, first + width)
+            nc.vector.quantize_mx(out=codes[:, cols].bitcast(FP8X4), scales=plane[:, cols], in_=woven)
 
         def quantize_wq(g, width, plane_tag):
-            wq_codes[g] = tile("wq_codes%d" % g, [P, 512], U32)
-            wq_plane[g] = tile("wq_plane%d" % g, [P, 512], U8, tag=plane_tag)
-            for first in range(0, 512, width):
-                quantize_cols(wq_codes[g], wq_plane[g], wq_grouped[g], first, width)
+            wq_codes[g] = tile("wq_codes%d" % g, [P, PASS], U32)
+            wq_plane[g] = tile("wq_plane%d" % g, [P, PASS], U8, tag=plane_tag)
+            for first in range(0, PASS, width):
+                woven = wq_woven[g][:, PACK * first : PACK * (first + width)]
+                quantize(wq_codes[g], wq_plane[g], first, width, woven)
 
-        def interleave(dst, src, copy=nc.vector.tensor_copy):
+        def weave(dst, src, copy):
             copy(
-                out=dst.rearrange("p (c i t) -> p c t i", i=4, t=PACK),
-                in_=src.rearrange("p t (c i) -> p c t i", i=4),
+                out=dst.rearrange("p (c e t) -> p c t e", e=4, t=PACK),
+                in_=src.rearrange("p t (c e) -> p c t e", e=4),
             )
-
-        def quantize_cols(codes, plane, grouped, first, width):
-            cols = slice(first, first + width)
-            nc.vector.quantize_mx(
-                out=codes[:, cols].bitcast(FP8X4),
-                scales=plane[:, cols],
-                in_=grouped[:, PACK * first : PACK * (first + width)],
-            )
-
-        def interleave_cols(grouped, planar, first, width, copy=nc.vector.tensor_copy):
-            interleave(grouped[:, PACK * first : PACK * (first + width)], planar[:, :, first : first + width], copy)
-
-        def interleave_and_quantize(codes, plane, grouped, planar):
-            for first in (0, 256):
-                interleave_cols(grouped, planar, first, 256)
-            for first in (0, 256):
-                quantize_cols(codes, plane, grouped, first, 256)
 
         def prepare_wf(g):
-            grouped = tile("wf_bf%d" % g, [P, PACK * N], BF16)
+            woven = tile("wf_woven%d" % g, [P, PACK * N], BF16)
             wf_codes[g] = tile("wf_codes%d" % g, [P, N], U32)
             wf_plane[g] = tile("wf_plane%d" % g, [P, N], U8)
-            interleave_and_quantize(wf_codes[g], wf_plane[g], grouped, wf_raw[g])
+            width = N // 2
+            for first in (0, width):
+                dst = woven[:, PACK * first : PACK * (first + width)]
+                weave(dst, wf_raw[g][:, :, first : first + width], nc.vector.tensor_copy)
+            for first in (0, width):
+                quantize(wf_codes[g], wf_plane[g], first, width, woven[:, PACK * first : PACK * (first + width)])
 
-        def doc_pass(bank, h, g, t, a):
-            nc.tensor.matmul_mx(
-                out=bank[:],
-                lhsT=wd_codes[g][:, a, t, :].bitcast(FP4X4),
-                lhsT_scale=wd_plane[g, a, t],
-                rhs=doc_codes[h, a].bitcast(FP8X4),
-                rhs_scale=doc_scales[h, a],
-                start=(a == 0),
-                stop=False,
-            )
-
-        def difference(h, g):
+        def difference(half, g):
+            pairs = slice(HALF * half, HALF * (half + 1))
             banks = []
             for t in range(PACK):
-                bank = psum.tile([P, HALF], F32, name="diff%d%d%d" % (h, g, t), tag="bank")
-                doc_pass(bank, h, g, t, 0)
-                doc_pass(bank, h, g, t, 1)
+                bank = psum.tile([P, HALF], F32, name="diff%d%d%d" % (half, g, t), tag="bank")
+                for a in range(DOC_PASSES):
+                    nc.tensor.matmul_mx(
+                        out=bank[:],
+                        lhsT=wd_codes[g][:, a, t, :].bitcast(FP4X4),
+                        lhsT_scale=wd_planes[a][:, PASS * g + P * t : PASS * g + P * (t + 1)],
+                        rhs=doc_codes[half, a].bitcast(FP8X4),
+                        rhs_scale=doc_planes[a][:, pairs],
+                        start=(a == 0),
+                        stop=False,
+                    )
                 cols = slice(P * t, P * (t + 1))
                 nc.tensor.matmul_mx(
                     out=bank[:],
                     lhsT=wq_codes[g][:, cols].bitcast(FP8X4),
                     lhsT_scale=wq_plane[g][:, cols],
-                    rhs=query_codes[h].bitcast(FP8X4),
-                    rhs_scale=query_scales[h],
+                    rhs=query_codes[half].bitcast(FP8X4),
+                    rhs_scale=query_plane_all[QUERY_PLANE:P, pairs],
                     start=False,
                     stop=True,
                 )
                 banks.append(bank)
             return banks
 
-        h_planar = {}
-        first_grouped = tile("h_bf_first", [P, PACK * 256], BF16, tag="wq_raw1")
-        later_grouped = tile("h_bf_later", [P, GROUPS * PACK * S], BF16, tag="wf_raw1")
+        h_woven_first = tile("h_woven_first", [P, PACK * PIECE], BF16, tag="wq_raw1")
+        h_woven_rest = tile("h_woven_rest", [P, GROUPS * PACK * S], BF16, tag="wf_raw1")
         h_codes = [tile("h_codes%d" % g, [P, S], U32) for g in range(GROUPS)]
         h_plane = [tile("h_plane%d" % g, [P, S], U8) for g in range(GROUPS)]
-        for h in range(2):
-            for g in range(GROUPS):
-                h_planar[h, g] = tile("h_planar%d%d" % (h, g), [P, PACK, HALF], BF16)
+        h_rows = {
+            (half, g): tile("h_rows%d%d" % (half, g), [P, PACK, HALF], BF16) for half in range(2) for g in range(GROUPS)
+        }
 
-        def h_grouped(g, first, width):
-            if g == 0 and first < 256:
-                return first_grouped[:, PACK * first : PACK * (first + width)]
-            return later_grouped[:, PACK * (S * g + first) : PACK * (S * g + first + width)]
+        def h_woven(g, first, width):
+            if g == 0 and first < PIECE:
+                return h_woven_first[:, PACK * first : PACK * (first + width)]
+            return h_woven_rest[:, PACK * (S * g + first) : PACK * (S * g + first + width)]
 
-        def square(h, g, banks):
+        def square(half, g, banks):
             for t in range(PACK):
                 nc.scalar.activation(
-                    out=h_planar[h, g][:, t, :],
+                    out=h_rows[half, g][:, t, :],
                     in_=banks[t][:],
                     func=ACT.Square,
                     scale=root_gain[:, PACK * g + t : PACK * g + t + 1],
                 )
 
-        def weave(g, first, width, copy=nc.vector.tensor_copy):
+        def weave_h(g, first, width, copy=nc.vector.tensor_copy):
             start = first % HALF
-            interleave(h_grouped(g, first, width), h_planar[first // HALF, g][:, :, start : start + width], copy)
+            weave(h_woven(g, first, width), h_rows[first // HALF, g][:, :, start : start + width], copy)
 
         def quantize_h(g, first, width):
-            cols = slice(first, first + width)
-            nc.vector.quantize_mx(
-                out=h_codes[g][:, cols].bitcast(FP8X4), scales=h_plane[g][:, cols], in_=h_grouped(g, first, width)
-            )
+            quantize(h_codes[g], h_plane[g], first, width, h_woven(g, first, width))
 
         def features(first, width):
-            tokens = slice(first, first + width)
-            banks = [psum.tile([P, width], F32, name="y%d_%d" % (first, c), tag="bank") for c in range(4)]
+            pairs = slice(first, first + width)
+            banks = [psum.tile([P, width], F32, name="y%d_%d" % (first, c), tag="bank") for c in range(OUT_TILES)]
             for g in range(GROUPS):
-                for c in range(4):
+                for c in range(OUT_TILES):
                     rows = slice(P * c, P * (c + 1))
                     nc.tensor.matmul_mx(
                         out=banks[c][:],
                         lhsT=wf_codes[g][:, rows].bitcast(FP8X4),
                         lhsT_scale=wf_plane[g][:, rows],
-                        rhs=h_codes[g][:, tokens].bitcast(FP8X4),
-                        rhs_scale=h_plane[g][:, tokens],
+                        rhs=h_codes[g][:, pairs].bitcast(FP8X4),
+                        rhs_scale=h_plane[g][:, pairs],
                         start=(g == 0),
                         stop=(g == GROUPS - 1),
                     )
-            for c0 in (0, 2):
+            for c0 in range(0, OUT_TILES, 2):
                 result = tile("result%d_%d" % (first, c0), [P, 2, width], F32)
                 for e in range(2):
                     c = c0 + e
                     nc.scalar.activation(out=result[:, e, :], in_=banks[c][:], func=ACT.Tanh, bias=bias[:, c : c + 1])
                 nc.sync.dma_start(
-                    out=out[P * c0 : P * (c0 + 2), tokens].rearrange("(e p) j -> p e j", p=P), in_=result[:]
+                    out=out[P * c0 : P * (c0 + 2), pairs].rearrange("(e p) j -> p e j", p=P), in_=result[:]
                 )
 
-        permute_wd_codes(0)
-        permute_wd_scales(0, None)
-        gather_half(0)
-        gather_half(1)
-        permute_wd_scales(1, "doc_win1")
-        gather(query_scales_all[:], query_scale_win[:], query_list[:])
-        cast_wq(0)
-        quantize_wq(0, 512, "query_scale_win")
-        gather_query(0)
-        banks00 = difference(0, 0)
-        gather_query(1)
-        banks10 = difference(1, 0)
-        permute_wd_codes(1)
-        cast_wq(1)
-        quantize_wq(1, 256, None)
-        square(0, 0, banks00)
-        for first in (0, 128):
-            weave(0, first, 128)
-        for first in (0, 128):
-            quantize_h(0, first, 128)
-        banks01 = difference(0, 1)
-        square(0, 1, banks01)
-        square(1, 0, banks10)
-        banks11 = difference(1, 1)
-        prepare_wf(0)
-        prepare_wf(1)
-        square(1, 1, banks11)
-        weave(0, 512, 256, nc.scalar.copy)
-        weave(1, 0, 256)
-        weave(0, 256, 256)
-        quantize_h(1, 0, 256)
-        features(0, 256)
-        weave(1, 256, 256)
-        quantize_h(0, 256, 256)
-        weave(1, 512, 256)
-        quantize_h(1, 256, 256)
-        features(256, 256)
-        quantize_h(0, 512, 256)
-        weave(0, 768, 256)
-        quantize_h(1, 512, 256)
-        features(512, 256)
-        weave(1, 768, 128)
-        quantize_h(0, 768, 256)
-        quantize_h(1, 768, 128)
-        features(768, 128)
-        weave(1, 896, 128)
-        quantize_h(1, 896, 128)
-        features(896, 128)
+        permute_wd(0)
+        for half in range(2):
+            doc_codes[half, 1] = gather_half("doc_codes_second", doc_win[1], doc_list, half)
+        gather(query_plane_all[:], query_scale_win[:], query_list[:])
+        dst, src = wq_views(0)
+        nc.scalar.activation(out=dst, in_=src, func=ACT.Copy, scale=-1.0)
+        quantize_wq(0, PASS, "query_scale_win")
+        banks = {}
+        for half in range(2):
+            query_codes[half] = gather_half("query_codes", query_win, query_list, half)
+            banks[half, 0] = difference(half, 0)
+
+        permute_wd(1)
+        dst, src = wq_views(1)
+        for t in (0, 2):
+            nc.vector.tensor_scalar(dst[:, :, t : t + 2], src[:, :, t : t + 2], -1.0, None, ALU.mult)
+        quantize_wq(1, PASS // 2, None)
+        square(0, 0, banks[0, 0])
+        for first in (0, SMALL):
+            weave_h(0, first, SMALL)
+        for first in (0, SMALL):
+            quantize_h(0, first, SMALL)
+        banks[0, 1] = difference(0, 1)
+        square(0, 1, banks[0, 1])
+        square(1, 0, banks[1, 0])
+        banks[1, 1] = difference(1, 1)
+        for g in range(GROUPS):
+            prepare_wf(g)
+        square(1, 1, banks[1, 1])
+
+        weave_h(0, 2 * PIECE, PIECE, nc.scalar.copy)
+        weave_h(1, 0, PIECE)
+        weave_h(0, PIECE, PIECE)
+        quantize_h(1, 0, PIECE)
+        features(0, PIECE)
+        weave_h(1, PIECE, PIECE)
+        quantize_h(0, PIECE, PIECE)
+        weave_h(1, 2 * PIECE, PIECE)
+        quantize_h(1, PIECE, PIECE)
+        features(PIECE, PIECE)
+        quantize_h(0, 2 * PIECE, PIECE)
+        weave_h(0, 3 * PIECE, PIECE)
+        quantize_h(1, 2 * PIECE, PIECE)
+        features(2 * PIECE, PIECE)
+        weave_h(1, 3 * PIECE, SMALL)
+        quantize_h(0, 3 * PIECE, PIECE)
+        weave_h(1, 3 * PIECE + SMALL, SMALL)
+        for first in (3 * PIECE, 3 * PIECE + SMALL):
+            quantize_h(1, first, SMALL)
+            features(first, SMALL)

@@ -56,8 +56,7 @@ def tile_list_duplicate_match_features_kernel(
         wq_raw = [tile("wq_raw%d" % g, [P, PACK, PASS], F32) for g in range(GROUPS)]
         wf_raw = [tile("wf_raw%d" % g, [P, PACK, N], F32) for g in range(GROUPS)]
 
-        nc.gpsimd.memset(doc_scale_win[:], 0)
-        for scale_tile in (wd_scale_raw, query_scale_win, doc_plane_second, wd_plane_second):
+        for scale_tile in (doc_scale_win, wd_scale_raw, query_scale_win, doc_plane_second, wd_plane_second):
             nc.vector.memset(scale_tile[:], 0)
 
         def gather(picked, window, offsets):
@@ -88,12 +87,12 @@ def tile_list_duplicate_match_features_kernel(
             nc.sync.dma_start(out=wf_raw[g][:], in_=rows.rearrange("(p t) n -> p t n", t=PACK))
 
         nc.sync.dma_start(doc_list[:], offs2)
-        load_two_planes(doc_scale_win, tab2_scales)
-        nc.sync.dma_start(out=gain_cols[:], in_=gain.rearrange("(g p t) -> p g t", g=GROUPS, t=PACK))
-        load_table(doc_win[0], tab2_words, 0)
         load_wd(0)
+        load_two_planes(doc_scale_win, tab2_scales)
+        load_table(doc_win[0], tab2_words, 0)
         load_two_planes(wd_scale_raw, wd_scales)
         nc.sync.dma_start(query_list[:], offs)
+        nc.sync.dma_start(out=gain_cols[:], in_=gain.rearrange("(g p t) -> p g t", g=GROUPS, t=PACK))
         load_table(doc_win[1], tab2_words, 1)
         doc_plane_both = tile("doc_plane_both", [P, S], U8)
         gather(doc_plane_both[:], doc_scale_win[:], doc_list[:])

@@ -86,8 +86,8 @@ def tile_list_duplicate_match_features_kernel(
             rows = wf[PASS * g : PASS * (g + 1), :]
             nc.sync.dma_start(out=wf_raw[g][:], in_=rows.rearrange("(p t) n -> p t n", t=PACK))
 
-        nc.sync.dma_start(doc_list[:], offs2)
         load_wd(0)
+        nc.sync.dma_start(doc_list[:], offs2)
         load_two_planes(doc_scale_win, tab2_scales)
         load_table(doc_win[0], tab2_words, 0)
         load_two_planes(wd_scale_raw, wd_scales)
@@ -96,11 +96,11 @@ def tile_list_duplicate_match_features_kernel(
         load_table(doc_win[1], tab2_words, 1)
         doc_plane_both = tile("doc_plane_both", [P, S], U8)
         gather(doc_plane_both[:], doc_scale_win[:], doc_list[:])
-        load_wq(0)
         for r in range(ROWS):
             nc.sync.dma_start(
                 out=query_scale_win[QUERY_PLANE + r : P : 32, :], in_=tab_scales[0, r:16:ROWS, :].bitcast(I32)
             )
+        load_wq(0)
         move_second_plane(doc_plane_second, doc_plane_both)
         wd_plane_both = tile("wd_plane_both", [P, H], U8)
         nc.vector.tensor_copy(
@@ -153,9 +153,9 @@ def tile_list_duplicate_match_features_kernel(
             cols = slice(first, first + width)
             nc.vector.quantize_mx(out=codes[:, cols].bitcast(FP8X4), scales=plane[:, cols], in_=woven)
 
-        def quantize_wq(g, width, plane_tag):
+        def quantize_wq(g, width):
             wq_codes[g] = tile("wq_codes%d" % g, [P, PASS], U32)
-            wq_plane[g] = tile("wq_plane%d" % g, [P, PASS], U8, tag=plane_tag)
+            wq_plane[g] = tile("wq_plane%d" % g, [P, PASS], U8)
             for first in range(0, PASS, width):
                 woven = wq_woven[g][:, PACK * first : PACK * (first + width)]
                 quantize(wq_codes[g], wq_plane[g], first, width, woven)
@@ -264,7 +264,7 @@ def tile_list_duplicate_match_features_kernel(
         gather(query_plane_all[:], query_scale_win[:], query_list[:])
         dst, src = wq_views(0)
         nc.scalar.activation(out=dst, in_=src, func=ACT.Copy, scale=-1.0)
-        quantize_wq(0, PASS, "query_scale_win")
+        quantize_wq(0, PASS)
         banks = {}
         for half in range(2):
             query_codes[half] = gather_half("query_codes", query_win, query_list, half)
@@ -274,7 +274,7 @@ def tile_list_duplicate_match_features_kernel(
         dst, src = wq_views(1)
         for t in (0, 2):
             nc.vector.tensor_scalar(dst[:, :, t : t + 2], src[:, :, t : t + 2], -1.0, None, ALU.mult)
-        quantize_wq(1, PASS // 2, None)
+        quantize_wq(1, PASS // 2)
         square(0, 0, banks[0, 0])
         for first in (0, SMALL):
             weave_h(0, first, SMALL)

@@ -53,7 +53,8 @@ def tile_list_duplicate_match_features_kernel(
         doc_win = [tile("doc_win%d" % a, [P, T], I32) for a in range(DOC_PASSES)]
         query_win = tile("query_win", [P, T], I32)
         wd_raw = [tile("wd_raw%d" % g, [P, DOC_PASSES, PASS // 2], I32) for g in range(GROUPS)]
-        wq_raw = [tile("wq_raw%d" % g, [P, PACK, PASS], F32) for g in range(GROUPS)]
+        wq_raw_first = [tile("wq_raw0%d" % u, [P, PACK, PASS // 2], F32) for u in range(2)]
+        wq_raw_second = tile("wq_raw1", [P, PACK, PASS], F32)
         wf_raw = [tile("wf_raw%d" % g, [P, PACK, N], F32) for g in range(GROUPS)]
 
         for scale_tile in (doc_scale_win, wd_scale_raw, query_scale_win, doc_plane_second, wd_plane_second):
@@ -78,9 +79,9 @@ def tile_list_duplicate_match_features_kernel(
             words = wd_words[:, :, 2 * PASS * g : 2 * PASS * (g + 1)]
             nc.sync.dma_start(out=wd_raw[g][:], in_=words.rearrange("a p c -> p a c").bitcast(I32))
 
-        def load_wq(g):
-            cols = wq[:, PASS * g : PASS * (g + 1)]
-            nc.sync.dma_start(out=wq_raw[g][:], in_=cols.rearrange("(p i) c -> p i c", i=PACK))
+        def load_wq(raw, first, width):
+            cols = wq[:, first : first + width]
+            nc.sync.dma_start(out=raw[:], in_=cols.rearrange("(p i) c -> p i c", i=PACK))
 
         def load_wf(g):
             rows = wf[PASS * g : PASS * (g + 1), :]
@@ -96,11 +97,12 @@ def tile_list_duplicate_match_features_kernel(
         load_table(doc_win[1], tab2_words, 1)
         doc_plane_both = tile("doc_plane_both", [P, S], U8)
         gather(doc_plane_both[:], doc_scale_win[:], doc_list[:])
+        load_wq(wq_raw_first[0], 0, PASS // 2)
         for r in range(ROWS):
             nc.sync.dma_start(
                 out=query_scale_win[QUERY_PLANE + r : P : 32, :], in_=tab_scales[0, r:16:ROWS, :].bitcast(I32)
             )
-        load_wq(0)
+        load_wq(wq_raw_first[1], PASS // 2, PASS // 2)
         move_second_plane(doc_plane_second, doc_plane_both)
         wd_plane_both = tile("wd_plane_both", [P, H], U8)
         nc.vector.tensor_copy(
@@ -116,7 +118,7 @@ def tile_list_duplicate_match_features_kernel(
         nc.scalar.activation(out=warm[:], in_=root_gain[:, 0:1], func=ACT.Tanh)
 
         load_wd(1)
-        load_wq(1)
+        load_wq(wq_raw_second, PASS, PASS)
         load_wf(0)
         load_wf(1)
         bias = tile("bias", [P, OUT_TILES], F32)
@@ -143,11 +145,12 @@ def tile_list_duplicate_match_features_kernel(
                 in_=wd_raw[g][:].bitcast(U16).rearrange("p a (m t) -> p a t m", t=PACK),
             )
 
-        def wq_views(g):
+        def wq_target(g):
             wq_woven[g] = tile("wq_woven%d" % g, [P, PACK * PASS], BF16)
-            dst = wq_woven[g][:].rearrange("p (t m i) -> p m t i", t=PACK, i=PACK)
-            src = wq_raw[g][:].rearrange("p i (m t) -> p m t i", t=PACK)
-            return dst, src
+            return wq_woven[g][:].rearrange("p (t m i) -> p m t i", t=PACK, i=PACK)
+
+        def wq_source(raw):
+            return raw[:].rearrange("p i (m t) -> p m t i", t=PACK)
 
         def quantize(codes, plane, first, width, woven):
             cols = slice(first, first + width)
@@ -160,8 +163,8 @@ def tile_list_duplicate_match_features_kernel(
                 woven = wq_woven[g][:, PACK * first : PACK * (first + width)]
                 quantize(wq_codes[g], wq_plane[g], first, width, woven)
 
-        def weave(dst, src, copy):
-            copy(
+        def weave(dst, src):
+            nc.vector.tensor_copy(
                 out=dst.rearrange("p (c e t) -> p c t e", e=4, t=PACK),
                 in_=src.rearrange("p t (c e) -> p c t e", e=4),
             )
@@ -173,7 +176,7 @@ def tile_list_duplicate_match_features_kernel(
             width = N // 2
             for first in (0, width):
                 dst = woven[:, PACK * first : PACK * (first + width)]
-                weave(dst, wf_raw[g][:, :, first : first + width], nc.vector.tensor_copy)
+                weave(dst, wf_raw[g][:, :, first : first + width])
             for first in (0, width):
                 quantize(wf_codes[g], wf_plane[g], first, width, woven[:, PACK * first : PACK * (first + width)])
 
@@ -205,7 +208,7 @@ def tile_list_duplicate_match_features_kernel(
                 banks.append(bank)
             return banks
 
-        h_woven_first = tile("h_woven_first", [P, PACK * PIECE], BF16, tag="wq_raw1")
+        h_woven_first = tile("h_woven_first", [P, PACK * HALF], BF16, tag="wq_raw1")
         h_woven_rest = tile("h_woven_rest", [P, GROUPS * PACK * S], BF16, tag="wf_raw1")
         h_codes = [tile("h_codes%d" % g, [P, S], U32) for g in range(GROUPS)]
         h_plane = [tile("h_plane%d" % g, [P, S], U8) for g in range(GROUPS)]
@@ -214,7 +217,7 @@ def tile_list_duplicate_match_features_kernel(
         }
 
         def h_woven(g, first, width):
-            if g == 0 and first < PIECE:
+            if g == 0 and first < HALF:
                 return h_woven_first[:, PACK * first : PACK * (first + width)]
             return h_woven_rest[:, PACK * (S * g + first) : PACK * (S * g + first + width)]
 
@@ -227,9 +230,9 @@ def tile_list_duplicate_match_features_kernel(
                     scale=root_gain[:, PACK * g + t : PACK * g + t + 1],
                 )
 
-        def weave_h(g, first, width, copy=nc.vector.tensor_copy):
+        def weave_h(g, first, width):
             start = first % HALF
-            weave(h_woven(g, first, width), h_rows[first // HALF, g][:, :, start : start + width], copy)
+            weave(h_woven(g, first, width), h_rows[first // HALF, g][:, :, start : start + width])
 
         def quantize_h(g, first, width):
             quantize(h_codes[g], h_plane[g], first, width, h_woven(g, first, width))
@@ -262,8 +265,10 @@ def tile_list_duplicate_match_features_kernel(
         for half in range(2):
             doc_codes[half, 1] = gather_half("doc_codes_second", doc_win[1], doc_list, half)
         gather(query_plane_all[:], query_scale_win[:], query_list[:])
-        dst, src = wq_views(0)
-        nc.scalar.activation(out=dst, in_=src, func=ACT.Copy, scale=-1.0)
+        dst = wq_target(0)
+        for u in range(2):
+            places = slice(P // 2 * u, P // 2 * (u + 1))
+            nc.scalar.activation(out=dst[:, places], in_=wq_source(wq_raw_first[u]), func=ACT.Copy, scale=-1.0)
         quantize_wq(0, PASS)
         banks = {}
         for half in range(2):
@@ -271,15 +276,15 @@ def tile_list_duplicate_match_features_kernel(
             banks[half, 0] = difference(half, 0)
 
         permute_wd(1)
-        dst, src = wq_views(1)
+        dst, src = wq_target(1), wq_source(wq_raw_second)
         for t in (0, 2):
             nc.vector.tensor_scalar(dst[:, :, t : t + 2], src[:, :, t : t + 2], -1.0, None, ALU.mult)
         quantize_wq(1, PASS // 2)
         square(0, 0, banks[0, 0])
-        for first in (0, SMALL):
-            weave_h(0, first, SMALL)
-        for first in (0, SMALL):
-            quantize_h(0, first, SMALL)
+        for first in (0, PIECE):
+            weave_h(0, first, PIECE)
+        for first in (0, PIECE):
+            quantize_h(0, first, PIECE)
         banks[0, 1] = difference(0, 1)
         square(0, 1, banks[0, 1])
         square(1, 0, banks[1, 0])
@@ -288,23 +293,14 @@ def tile_list_duplicate_match_features_kernel(
             prepare_wf(g)
         square(1, 1, banks[1, 1])
 
-        weave_h(0, 2 * PIECE, PIECE, nc.scalar.copy)
-        weave_h(1, 0, PIECE)
-        weave_h(0, PIECE, PIECE)
-        quantize_h(1, 0, PIECE)
-        features(0, PIECE)
-        weave_h(1, PIECE, PIECE)
-        quantize_h(0, PIECE, PIECE)
-        weave_h(1, 2 * PIECE, PIECE)
-        quantize_h(1, PIECE, PIECE)
-        features(PIECE, PIECE)
-        quantize_h(0, 2 * PIECE, PIECE)
-        weave_h(0, 3 * PIECE, PIECE)
-        quantize_h(1, 2 * PIECE, PIECE)
-        features(2 * PIECE, PIECE)
-        weave_h(1, 3 * PIECE, SMALL)
-        quantize_h(0, 3 * PIECE, PIECE)
-        weave_h(1, 3 * PIECE + SMALL, SMALL)
-        for first in (3 * PIECE, 3 * PIECE + SMALL):
-            quantize_h(1, first, SMALL)
-            features(first, SMALL)
+        for first in (0, PIECE):
+            weave_h(1, first, PIECE)
+        for first in (0, PIECE):
+            quantize_h(1, first, PIECE)
+            features(first, PIECE)
+        for first, width in ((2 * PIECE, PIECE), (3 * PIECE, SMALL), (3 * PIECE + SMALL, SMALL)):
+            for g in range(GROUPS):
+                weave_h(g, first, width)
+            for g in range(GROUPS):
+                quantize_h(g, first, width)
+            features(first, width)

@@ -49,7 +49,7 @@ def tile_list_duplicate_match_features_kernel(
         query_scale_win = tile("query_scale_win", [P, T // 4], I32)
         wd_scale_raw = tile("wd_scale_raw", [P, H // 4], I32)
         wd_plane_second = tile("wd_plane_second", [P, H // 4], I32)
-        gain_cols = tile("gain_cols", [P, GROUPS, PACK], F32)
+        gain_cols = tile("gain_cols", [P, GROUPS, 2 * PACK], F32)
         doc_win = [tile("doc_win%d" % a, [P, T], I32) for a in range(DOC_PASSES)]
         query_win = tile("query_win", [P, T], I32)
         wd_raw = [tile("wd_raw%d" % g, [P, DOC_PASSES, PASS // 2], I32) for g in range(GROUPS)]
@@ -93,7 +93,7 @@ def tile_list_duplicate_match_features_kernel(
         load_table(doc_win[0], tab2_words, 0)
         load_two_planes(wd_scale_raw, wd_scales)
         nc.sync.dma_start(query_list[:], offs)
-        nc.sync.dma_start(out=gain_cols[:], in_=gain.rearrange("(g p t) -> p g t", g=GROUPS, t=PACK))
+        nc.sync.dma_start(out=gain_cols[:, :, 0:PACK], in_=gain.rearrange("(g p t) -> p g t", g=GROUPS, t=PACK))
         load_table(doc_win[1], tab2_words, 1)
         doc_plane_both = tile("doc_plane_both", [P, S], U8)
         gather(doc_plane_both[:], doc_scale_win[:], doc_list[:])
@@ -113,7 +113,9 @@ def tile_list_duplicate_match_features_kernel(
         load_table(query_win, tab_words, 0)
 
         root_gain = tile("root_gain", [P, GROUPS * PACK], F32)
-        nc.scalar.activation(out=root_gain[:], in_=gain_cols[:].rearrange("p g t -> p (g t)"), func=ACT.Sqrt)
+        nc.scalar.activation(
+            out=root_gain[:].rearrange("p (g t) -> p g t", g=GROUPS), in_=gain_cols[:, :, 0:PACK], func=ACT.Sqrt
+        )
         warm = tile("warm", [P, 1], F32)
         nc.scalar.activation(out=warm[:], in_=root_gain[:, 0:1], func=ACT.Tanh)
 
@@ -208,7 +210,7 @@ def tile_list_duplicate_match_features_kernel(
                 banks.append(bank)
             return banks
 
-        h_woven_first = tile("h_woven_first", [P, PACK * HALF], BF16, tag="wq_raw1")
+        h_woven_first = tile("h_woven_first", [P, PACK * PIECE], BF16, tag="wq_raw1")
         h_woven_rest = tile("h_woven_rest", [P, GROUPS * PACK * S], BF16, tag="wf_raw1")
         h_codes = [tile("h_codes%d" % g, [P, S], U32) for g in range(GROUPS)]
         h_plane = [tile("h_plane%d" % g, [P, S], U8) for g in range(GROUPS)]
@@ -217,7 +219,7 @@ def tile_list_duplicate_match_features_kernel(
         }
 
         def h_woven(g, first, width):
-            if g == 0 and first < HALF:
+            if g == 0 and first < PIECE:
                 return h_woven_first[:, PACK * first : PACK * (first + width)]
             return h_woven_rest[:, PACK * (S * g + first) : PACK * (S * g + first + width)]
 
@@ -237,28 +239,29 @@ def tile_list_duplicate_match_features_kernel(
         def quantize_h(g, first, width):
             quantize(h_codes[g], h_plane[g], first, width, h_woven(g, first, width))
 
-        def features(first, width):
+        def features(first, width, passes, per_store=2):
             pairs = slice(first, first + width)
             banks = [psum.tile([P, width], F32, name="y%d_%d" % (first, c), tag="bank") for c in range(OUT_TILES)]
-            for g in range(GROUPS):
-                for c in range(OUT_TILES):
-                    rows = slice(P * c, P * (c + 1))
-                    nc.tensor.matmul_mx(
-                        out=banks[c][:],
-                        lhsT=wf_codes[g][:, rows].bitcast(FP8X4),
-                        lhsT_scale=wf_plane[g][:, rows],
-                        rhs=h_codes[g][:, pairs].bitcast(FP8X4),
-                        rhs_scale=h_plane[g][:, pairs],
-                        start=(g == 0),
-                        stop=(g == GROUPS - 1),
-                    )
-            for c0 in range(0, OUT_TILES, 2):
-                result = tile("result%d_%d" % (first, c0), [P, 2, width], F32)
-                for e in range(2):
+            opened = set()
+            for g, c in passes:
+                rows = slice(P * c, P * (c + 1))
+                nc.tensor.matmul_mx(
+                    out=banks[c][:],
+                    lhsT=wf_codes[g][:, rows].bitcast(FP8X4),
+                    lhsT_scale=wf_plane[g][:, rows],
+                    rhs=h_codes[g][:, pairs].bitcast(FP8X4),
+                    rhs_scale=h_plane[g][:, pairs],
+                    start=(c not in opened),
+                    stop=(c in opened),
+                )
+                opened.add(c)
+            for c0 in range(0, OUT_TILES, per_store):
+                result = tile("result%d_%d" % (first, c0), [P, per_store, width], F32)
+                for e in range(per_store):
                     c = c0 + e
                     nc.scalar.activation(out=result[:, e, :], in_=banks[c][:], func=ACT.Tanh, bias=bias[:, c : c + 1])
                 nc.sync.dma_start(
-                    out=out[P * c0 : P * (c0 + 2), pairs].rearrange("(e p) j -> p e j", p=P), in_=result[:]
+                    out=out[P * c0 : P * (c0 + per_store), pairs].rearrange("(e p) j -> p e j", p=P), in_=result[:]
                 )
 
         permute_wd(0)
@@ -276,15 +279,15 @@ def tile_list_duplicate_match_features_kernel(
             banks[half, 0] = difference(half, 0)
 
         permute_wd(1)
-        dst, src = wq_target(1), wq_source(wq_raw_second)
+        dst, src = (view.rearrange("p m t i -> p m i t") for view in (wq_target(1), wq_source(wq_raw_second)))
         for t in (0, 2):
-            nc.vector.tensor_scalar(dst[:, :, t : t + 2], src[:, :, t : t + 2], -1.0, None, ALU.mult)
+            nc.vector.tensor_scalar(dst[:, :, :, t : t + 2], src[:, :, :, t : t + 2], -1.0, None, ALU.mult)
         quantize_wq(1, PASS // 2)
         square(0, 0, banks[0, 0])
-        for first in (0, PIECE):
-            weave_h(0, first, PIECE)
-        for first in (0, PIECE):
-            quantize_h(0, first, PIECE)
+        for first in (0, SMALL):
+            weave_h(0, first, SMALL)
+        for first in (0, SMALL):
+            quantize_h(0, first, SMALL)
         banks[0, 1] = difference(0, 1)
         square(0, 1, banks[0, 1])
         square(1, 0, banks[1, 0])
@@ -293,14 +296,16 @@ def tile_list_duplicate_match_features_kernel(
             prepare_wf(g)
         square(1, 1, banks[1, 1])
 
-        for first in (0, PIECE):
-            weave_h(1, first, PIECE)
-        for first in (0, PIECE):
-            quantize_h(1, first, PIECE)
-            features(first, PIECE)
-        for first, width in ((2 * PIECE, PIECE), (3 * PIECE, SMALL), (3 * PIECE + SMALL, SMALL)):
+        by_tile = [(g, c) for c in range(OUT_TILES) for g in (1, 0)]
+        by_group = [(g, c) for g in range(GROUPS) for c in range(OUT_TILES)]
+        weave_h(1, 0, PIECE)
+        weave_h(0, PIECE, PIECE)
+        quantize_h(1, 0, PIECE)
+        features(0, PIECE, by_tile)
+        for first, width in ((PIECE, PIECE), (2 * PIECE, PIECE), (3 * PIECE, SMALL), (3 * PIECE + SMALL, SMALL)):
             for g in range(GROUPS):
-                weave_h(g, first, width)
+                if (g, first) != (0, PIECE):
+                    weave_h(g, first, width)
             for g in range(GROUPS):
                 quantize_h(g, first, width)
-            features(first, width)
+            features(first, width, by_group, 1 if first + width == S else 2)

@@ -149,10 +149,10 @@ def tile_list_duplicate_match_features_kernel(
 
         def wq_target(g):
             wq_woven[g] = tile("wq_woven%d" % g, [P, PACK * PASS], BF16)
-            return wq_woven[g][:].rearrange("p (t m i) -> p m t i", t=PACK, i=PACK)
+            return wq_woven[g][:].rearrange("p (t m i) -> p m i t", t=PACK, i=PACK)
 
         def wq_source(raw):
-            return raw[:].rearrange("p i (m t) -> p m t i", t=PACK)
+            return raw[:].rearrange("p i (m t) -> p m i t", t=PACK)
 
         def quantize(codes, plane, first, width, woven):
             cols = slice(first, first + width)
@@ -167,8 +167,8 @@ def tile_list_duplicate_match_features_kernel(
 
         def weave(dst, src):
             nc.vector.tensor_copy(
-                out=dst.rearrange("p (c e t) -> p c t e", e=4, t=PACK),
-                in_=src.rearrange("p t (c e) -> p c t e", e=4),
+                out=dst.rearrange("p (c e t) -> p c t e", e=2, t=PACK),
+                in_=src.rearrange("p t (c e) -> p c t e", e=2),
             )
 
         def prepare_wf(g):
@@ -279,7 +279,7 @@ def tile_list_duplicate_match_features_kernel(
             banks[half, 0] = difference(half, 0)
 
         permute_wd(1)
-        dst, src = (view.rearrange("p m t i -> p m i t") for view in (wq_target(1), wq_source(wq_raw_second)))
+        dst, src = wq_target(1), wq_source(wq_raw_second)
         for t in (0, 2):
             nc.vector.tensor_scalar(dst[:, :, :, t : t + 2], src[:, :, :, t : t + 2], -1.0, None, ALU.mult)
         quantize_wq(1, PASS // 2)

@@ -40,7 +40,7 @@ def tile_list_duplicate_match_features_kernel(
         psum = ctx.enter_context(tc.psum_pool(name="psum", bufs=8))
 
         def tile(name, shape, dtype, tag=None):
-            return sb.tile(shape, dtype, name=name, tag=tag or name, align_bytes=64)
+            return sb.tile(shape, dtype, name=name, tag=tag or name, align_bytes=256)
 
         doc_list = tile("doc_list", [P, S // 16], U16)
         query_list = tile("query_list", [P, S // 16], U16)

@@ -47,17 +47,17 @@ def tile_list_duplicate_match_features_kernel(
         doc_scale_win = tile("doc_scale_win", [P, T // 4], I32)
         doc_plane_second = tile("doc_plane_second", [P, S // 4], I32)
         query_scale_win = tile("query_scale_win", [P, T // 4], I32)
-        wd_scale_raw = tile("wd_scale_raw", [P, H // 4], I32)
-        wd_plane_second = tile("wd_plane_second", [P, H // 4], I32)
+        wd_scale_raw = tile("wd_scale_raw", [P, DOC_PASSES, H // 4], I32)
         gain_cols = tile("gain_cols", [P, GROUPS, 2 * PACK], F32)
         doc_win = [tile("doc_win%d" % a, [P, T], I32) for a in range(DOC_PASSES)]
         query_win = tile("query_win", [P, T], I32)
         wd_raw = [tile("wd_raw%d" % g, [P, DOC_PASSES, PASS // 2], I32) for g in range(GROUPS)]
-        wq_raw_first = [tile("wq_raw0%d" % u, [P, PACK, PASS // 2], F32) for u in range(2)]
-        wq_raw_second = tile("wq_raw1", [P, PACK, PASS], F32)
+        wq_raw = {
+            (g, u): tile("wq_raw%d%d" % (g, u), [P, PACK, PASS // 2], F32) for g in range(GROUPS) for u in range(2)
+        }
         wf_raw = [tile("wf_raw%d" % g, [P, PACK, N], F32) for g in range(GROUPS)]
 
-        for scale_tile in (doc_scale_win, wd_scale_raw, query_scale_win, doc_plane_second, wd_plane_second):
+        for scale_tile in (doc_scale_win, wd_scale_raw, query_scale_win, doc_plane_second):
             nc.vector.memset(scale_tile[:], 0)
 
         def gather(picked, window, offsets):
@@ -91,26 +91,29 @@ def tile_list_duplicate_match_features_kernel(
         nc.sync.dma_start(doc_list[:], offs2)
         load_two_planes(doc_scale_win, tab2_scales)
         load_table(doc_win[0], tab2_words, 0)
-        load_two_planes(wd_scale_raw, wd_scales)
-        nc.sync.dma_start(query_list[:], offs)
+        for r in range(ROWS):
+            nc.sync.dma_start(
+                out=wd_scale_raw[r:P:32, :, :],
+                in_=wd_scales[:, r:16:ROWS, :].rearrange("a q c -> q a c").bitcast(I32),
+            )
         nc.sync.dma_start(out=gain_cols[:, :, 0:PACK], in_=gain.rearrange("(g p t) -> p g t", g=GROUPS, t=PACK))
         load_table(doc_win[1], tab2_words, 1)
+        load_wq(wq_raw[0, 0], 0, PASS // 2)
+        nc.sync.dma_start(query_list[:], offs)
         doc_plane_both = tile("doc_plane_both", [P, S], U8)
         gather(doc_plane_both[:], doc_scale_win[:], doc_list[:])
-        load_wq(wq_raw_first[0], 0, PASS // 2)
         for r in range(ROWS):
             nc.sync.dma_start(
                 out=query_scale_win[QUERY_PLANE + r : P : 32, :], in_=tab_scales[0, r:16:ROWS, :].bitcast(I32)
             )
-        load_wq(wq_raw_first[1], PASS // 2, PASS // 2)
+        load_wq(wq_raw[0, 1], PASS // 2, PASS // 2)
         move_second_plane(doc_plane_second, doc_plane_both)
-        wd_plane_both = tile("wd_plane_both", [P, H], U8)
-        nc.vector.tensor_copy(
-            out=wd_plane_both[:].rearrange("p (g t m) -> p g t m", g=GROUPS, t=PACK),
-            in_=wd_scale_raw[:].bitcast(U8).rearrange("p (g m t) -> p g t m", g=GROUPS, t=PACK),
-        )
-        move_second_plane(wd_plane_second, wd_plane_both)
         load_table(query_win, tab_words, 0)
+        wd_planes = [tile("wd_planes%d" % g, [P, DOC_PASSES, PACK, P], U8) for g in range(GROUPS)]
+        for g in range(GROUPS):
+            for a in range(DOC_PASSES):
+                cols = wd_scale_raw[:].bitcast(U8)[:, a, PASS * g : PASS * (g + 1)]
+                nc.gpsimd.tensor_copy(out=wd_planes[g][:, a], in_=cols.rearrange("p (m t) -> p t m", t=PACK))
 
         root_gain = tile("root_gain", [P, GROUPS * PACK], F32)
         nc.scalar.activation(
@@ -120,7 +123,8 @@ def tile_list_duplicate_match_features_kernel(
         nc.scalar.activation(out=warm[:], in_=root_gain[:, 0:1], func=ACT.Tanh)
 
         load_wd(1)
-        load_wq(wq_raw_second, PASS, PASS)
+        for u in range(2):
+            load_wq(wq_raw[1, u], PASS + PASS // 2 * u, PASS // 2)
         load_wf(0)
         load_wf(1)
         bias = tile("bias", [P, OUT_TILES], F32)
@@ -131,7 +135,6 @@ def tile_list_duplicate_match_features_kernel(
         query_plane_all = tile("query_plane_all", [P, S], U8)
         gather(doc_codes_first[:], doc_win[0][:], doc_list[:])
         doc_planes = (doc_plane_both[:], doc_plane_second[:].bitcast(U8))
-        wd_planes = (wd_plane_both[:], wd_plane_second[:].bitcast(U8))
         doc_codes = {(half, 0): doc_codes_first[:, HALF * half : HALF * (half + 1)] for half in range(2)}
         query_codes, wd_codes, wq_woven, wq_codes, wq_plane, wf_codes, wf_plane = {}, {}, {}, {}, {}, {}, {}
 
@@ -142,7 +145,7 @@ def tile_list_duplicate_match_features_kernel(
 
         def permute_wd(g):
             wd_codes[g] = tile("wd_codes%d" % g, [P, DOC_PASSES, PACK, 2 * P], U8)
-            nc.vector.tensor_copy(
+            nc.scalar.copy(
                 out=wd_codes[g][:].bitcast(U16),
                 in_=wd_raw[g][:].bitcast(U16).rearrange("p a (m t) -> p a t m", t=PACK),
             )
@@ -191,7 +194,7 @@ def tile_list_duplicate_match_features_kernel(
                     nc.tensor.matmul_mx(
                         out=bank[:],
                         lhsT=wd_codes[g][:, a, t, :].bitcast(FP4X4),
-                        lhsT_scale=wd_planes[a][:, PASS * g + P * t : PASS * g + P * (t + 1)],
+                        lhsT_scale=wd_planes[g][:, a, t, :],
                         rhs=doc_codes[half, a].bitcast(FP8X4),
                         rhs_scale=doc_planes[a][:, pairs],
                         start=(a == 0),
@@ -210,7 +213,7 @@ def tile_list_duplicate_match_features_kernel(
                 banks.append(bank)
             return banks
 
-        h_woven_first = tile("h_woven_first", [P, PACK * PIECE], BF16, tag="wq_raw1")
+        h_woven_first = tile("h_woven_first", [P, PACK * PIECE], BF16, tag="wq_raw11")
         h_woven_rest = tile("h_woven_rest", [P, GROUPS * PACK * S], BF16, tag="wf_raw1")
         h_codes = [tile("h_codes%d" % g, [P, S], U32) for g in range(GROUPS)]
         h_plane = [tile("h_plane%d" % g, [P, S], U8) for g in range(GROUPS)]
@@ -271,7 +274,7 @@ def tile_list_duplicate_match_features_kernel(
         dst = wq_target(0)
         for u in range(2):
             places = slice(P // 2 * u, P // 2 * (u + 1))
-            nc.scalar.activation(out=dst[:, places], in_=wq_source(wq_raw_first[u]), func=ACT.Copy, scale=-1.0)
+            nc.scalar.activation(out=dst[:, places], in_=wq_source(wq_raw[0, u]), func=ACT.Copy, scale=-1.0)
         quantize_wq(0, PASS)
         banks = {}
         for half in range(2):
@@ -279,9 +282,11 @@ def tile_list_duplicate_match_features_kernel(
             banks[half, 0] = difference(half, 0)
 
         permute_wd(1)
-        dst, src = wq_target(1), wq_source(wq_raw_second)
-        for t in (0, 2):
-            nc.vector.tensor_scalar(dst[:, :, :, t : t + 2], src[:, :, :, t : t + 2], -1.0, None, ALU.mult)
+        dst = wq_target(1)
+        for u in range(2):
+            places, src = slice(P // 2 * u, P // 2 * (u + 1)), wq_source(wq_raw[1, u])
+            for t in (0, 2):
+                nc.vector.tensor_scalar(dst[:, places, :, t : t + 2], src[:, :, :, t : t + 2], -1.0, None, ALU.mult)
         quantize_wq(1, PASS // 2)
         square(0, 0, banks[0, 0])
         for first in (0, SMALL):

@@ -23,6 +23,7 @@ GROUPS = H // PASS
 DOC_PASSES = K2 // PASS
 HALF = S // 2
 LIST_HALF = HALF // 16
+QUARTER = S // 4
 OUT_TILES = N // P
 PIECE = 256
 SMALL = PIECE // 2
@@ -55,7 +56,8 @@ def tile_list_duplicate_match_features_kernel(
         wq_raw = {
             (g, u): tile("wq_raw%d%d" % (g, u), [P, PACK, PASS // 2], F32) for g in range(GROUPS) for u in range(2)
         }
-        wf_raw = [tile("wf_raw%d" % g, [P, PACK, N], F32) for g in range(GROUPS)]
+        wf_raw_first = [tile("wf_raw0%d" % u, [P, PACK, N // 2], F32) for u in range(2)]
+        wf_raw_second = tile("wf_raw1", [P, PACK, N], F32)
 
         for scale_tile in (doc_scale_win, wd_scale_raw, query_scale_win, doc_plane_second):
             nc.vector.memset(scale_tile[:], 0)
@@ -83,12 +85,13 @@ def tile_list_duplicate_match_features_kernel(
             cols = wq[:, first : first + width]
             nc.sync.dma_start(out=raw[:], in_=cols.rearrange("(p i) c -> p i c", i=PACK))
 
-        def load_wf(g):
-            rows = wf[PASS * g : PASS * (g + 1), :]
-            nc.sync.dma_start(out=wf_raw[g][:], in_=rows.rearrange("(p t) n -> p t n", t=PACK))
+        def load_wf(raw, g, first, width):
+            rows = wf[PASS * g : PASS * (g + 1), first : first + width]
+            nc.sync.dma_start(out=raw[:], in_=rows.rearrange("(p t) n -> p t n", t=PACK))
 
         load_wd(0)
         nc.sync.dma_start(doc_list[:], offs2)
+        nc.sync.dma_start(out=gain_cols[:, :, 0:PACK], in_=gain.rearrange("(g p t) -> p g t", g=GROUPS, t=PACK))
         load_two_planes(doc_scale_win, tab2_scales)
         load_table(doc_win[0], tab2_words, 0)
         for r in range(ROWS):
@@ -96,7 +99,6 @@ def tile_list_duplicate_match_features_kernel(
                 out=wd_scale_raw[r:P:32, :, :],
                 in_=wd_scales[:, r:16:ROWS, :].rearrange("a q c -> q a c").bitcast(I32),
             )
-        nc.sync.dma_start(out=gain_cols[:, :, 0:PACK], in_=gain.rearrange("(g p t) -> p g t", g=GROUPS, t=PACK))
         load_table(doc_win[1], tab2_words, 1)
         load_wq(wq_raw[0, 0], 0, PASS // 2)
         nc.sync.dma_start(query_list[:], offs)
@@ -125,8 +127,9 @@ def tile_list_duplicate_match_features_kernel(
         load_wd(1)
         for u in range(2):
             load_wq(wq_raw[1, u], PASS + PASS // 2 * u, PASS // 2)
-        load_wf(0)
-        load_wf(1)
+        for u in range(2):
+            load_wf(wf_raw_first[u], 0, N // 2 * u, N // 2)
+        load_wf(wf_raw_second, 1, 0, N)
         bias = tile("bias", [P, OUT_TILES], F32)
         with nc.allow_non_contiguous_dma(reason="one bias value for each partition and output tile"):
             nc.sync.dma_start(out=bias[:], in_=bf.rearrange("(c p) -> p c", p=P))
@@ -174,14 +177,13 @@ def tile_list_duplicate_match_features_kernel(
                 in_=src.rearrange("p t (c e) -> p c t e", e=2),
             )
 
-        def prepare_wf(g):
+        def prepare_wf(g, halves):
             woven = tile("wf_woven%d" % g, [P, PACK * N], BF16)
             wf_codes[g] = tile("wf_codes%d" % g, [P, N], U32)
             wf_plane[g] = tile("wf_plane%d" % g, [P, N], U8)
             width = N // 2
-            for first in (0, width):
-                dst = woven[:, PACK * first : PACK * (first + width)]
-                weave(dst, wf_raw[g][:, :, first : first + width])
+            for first, raw in zip((0, width), halves):
+                weave(woven[:, PACK * first : PACK * (first + width)], raw)
             for first in (0, width):
                 quantize(wf_codes[g], wf_plane[g], first, width, woven[:, PACK * first : PACK * (first + width)])
 
@@ -190,16 +192,22 @@ def tile_list_duplicate_match_features_kernel(
             banks = []
             for t in range(PACK):
                 bank = psum.tile([P, HALF], F32, name="diff%d%d%d" % (half, g, t), tag="bank")
-                for a in range(DOC_PASSES):
+                def doc_pass(a, codes, first, width, start, stop):
                     nc.tensor.matmul_mx(
-                        out=bank[:],
+                        out=bank[:, first : first + width],
                         lhsT=wd_codes[g][:, a, t, :].bitcast(FP4X4),
                         lhsT_scale=wd_planes[g][:, a, t, :],
-                        rhs=doc_codes[half, a].bitcast(FP8X4),
-                        rhs_scale=doc_planes[a][:, pairs],
-                        start=(a == 0),
-                        stop=False,
+                        rhs=codes.bitcast(FP8X4),
+                        rhs_scale=doc_planes[a][:, HALF * half + first : HALF * half + first + width],
+                        start=start,
+                        stop=stop,
                     )
+
+                doc_pass(0, doc_codes[half, 0], 0, HALF, True, False)
+                if half == 0:
+                    doc_pass(1, doc_codes[0, 1], 0, HALF, False, False)
+                else:
+                    doc_pass(1, doc_third[:], 0, QUARTER, False, False)
                 cols = slice(P * t, P * (t + 1))
                 nc.tensor.matmul_mx(
                     out=bank[:],
@@ -208,8 +216,10 @@ def tile_list_duplicate_match_features_kernel(
                     rhs=query_codes[half].bitcast(FP8X4),
                     rhs_scale=query_plane_all[QUERY_PLANE:P, pairs],
                     start=False,
-                    stop=True,
+                    stop=(half == 0),
                 )
+                if half == 1:
+                    doc_pass(1, doc_fourth[:], QUARTER, QUARTER, False, True)
                 banks.append(bank)
             return banks
 
@@ -268,8 +278,9 @@ def tile_list_duplicate_match_features_kernel(
                 )
 
         permute_wd(0)
-        for half in range(2):
-            doc_codes[half, 1] = gather_half("doc_codes_second", doc_win[1], doc_list, half)
+        doc_codes[0, 1] = gather_half("doc_codes_second", doc_win[1], doc_list, 0)
+        doc_third = tile("doc_third", [P, QUARTER], U32)
+        gather(doc_third[:], doc_win[1][:], doc_list[:, LIST_HALF : LIST_HALF + LIST_HALF // 2])
         gather(query_plane_all[:], query_scale_win[:], query_list[:])
         dst = wq_target(0)
         for u in range(2):
@@ -277,11 +288,14 @@ def tile_list_duplicate_match_features_kernel(
             nc.scalar.activation(out=dst[:, places], in_=wq_source(wq_raw[0, u]), func=ACT.Copy, scale=-1.0)
         quantize_wq(0, PASS)
         banks = {}
-        for half in range(2):
-            query_codes[half] = gather_half("query_codes", query_win, query_list, half)
-            banks[half, 0] = difference(half, 0)
-
+        query_codes[0] = gather_half("query_codes", query_win, query_list, 0)
+        banks[0, 0] = difference(0, 0)
+        query_codes[1] = gather_half("query_codes", query_win, query_list, 1)
         permute_wd(1)
+        doc_fourth = tile("doc_fourth", [P, QUARTER], U32, tag="wd_raw1")
+        gather(doc_fourth[:], doc_win[1][:], doc_list[:, LIST_HALF + LIST_HALF // 2 : 2 * LIST_HALF])
+        banks[1, 0] = difference(1, 0)
+
         dst = wq_target(1)
         for u in range(2):
             places, src = slice(P // 2 * u, P // 2 * (u + 1)), wq_source(wq_raw[1, u])
@@ -297,8 +311,8 @@ def tile_list_duplicate_match_features_kernel(
         square(0, 1, banks[0, 1])
         square(1, 0, banks[1, 0])
         banks[1, 1] = difference(1, 1)
-        for g in range(GROUPS):
-            prepare_wf(g)
+        prepare_wf(0, [raw[:] for raw in wf_raw_first])
+        prepare_wf(1, [wf_raw_second[:, :, 0 : N // 2], wf_raw_second[:, :, N // 2 : N]])
         square(1, 1, banks[1, 1])
 
         by_tile = [(g, c) for c in range(OUT_TILES) for g in (1, 0)]

@@ -28,8 +28,6 @@ OUT_TILES = N // P
 PIECE = 256
 SMALL = PIECE // 2
 ROWS = 4
-SECOND = 16
-QUERY_PLANE = 8
 
 
 def tile_list_duplicate_match_features_kernel(
@@ -48,6 +46,7 @@ def tile_list_duplicate_match_features_kernel(
         doc_scale_win = tile("doc_scale_win", [P, T // 4], I32)
         doc_plane_second = tile("doc_plane_second", [P, S // 4], I32)
         query_scale_win = tile("query_scale_win", [P, T // 4], I32)
+        query_plane = tile("query_plane", [P, S // 4], I32)
         wd_scale_raw = tile("wd_scale_raw", [P, DOC_PASSES, H // 4], I32)
         gain_cols = tile("gain_cols", [P, GROUPS, 2 * PACK], F32)
         doc_win = [tile("doc_win%d" % a, [P, T], I32) for a in range(DOC_PASSES)]
@@ -59,7 +58,8 @@ def tile_list_duplicate_match_features_kernel(
         wf_raw_first = [tile("wf_raw0%d" % u, [P, PACK, N // 2], F32) for u in range(2)]
         wf_raw_second = tile("wf_raw1", [P, PACK, N], F32)
 
-        for scale_tile in (doc_scale_win, wd_scale_raw, query_scale_win, doc_plane_second):
+        nc.gpsimd.dma_start(out=gain_cols[:, :, 0:PACK], in_=gain.rearrange("(g p t) -> p g t", g=GROUPS, t=PACK))
+        for scale_tile in (doc_scale_win, wd_scale_raw, query_scale_win, doc_plane_second, query_plane):
             nc.vector.memset(scale_tile[:], 0)
 
         def gather(picked, window, offsets):
@@ -67,15 +67,6 @@ def tile_list_duplicate_match_features_kernel(
 
         def load_table(window, words, a):
             nc.sync.dma_start(out=window[:], in_=words[a].rearrange("p t i -> p (t i)").bitcast(I32))
-
-        def load_two_planes(dst, scales):
-            for r in range(ROWS):
-                nc.sync.dma_start(
-                    out=dst[r:P:SECOND, :], in_=scales[:, r:16:ROWS, :].rearrange("a q c -> q a c").bitcast(I32)
-                )
-
-        def move_second_plane(dst, both):
-            nc.sync.dma_start(out=dst[0 : P - SECOND, :], in_=both[SECOND:P, :].bitcast(I32))
 
         def load_wd(g):
             words = wd_words[:, :, 2 * PASS * g : 2 * PASS * (g + 1)]
@@ -91,26 +82,34 @@ def tile_list_duplicate_match_features_kernel(
 
         load_wd(0)
         nc.sync.dma_start(doc_list[:], offs2)
-        nc.sync.dma_start(out=gain_cols[:, :, 0:PACK], in_=gain.rearrange("(g p t) -> p g t", g=GROUPS, t=PACK))
-        load_two_planes(doc_scale_win, tab2_scales)
+        for r in range(ROWS):
+            nc.sync.dma_start(out=doc_scale_win[r:P:32, :], in_=tab2_scales[0, r:16:ROWS, :].bitcast(I32))
+        nc.sync.dma_start(out=doc_scale_win[ROWS : P : 2 * ROWS, :], in_=tab2_scales[1].bitcast(I32))
         load_table(doc_win[0], tab2_words, 0)
         for r in range(ROWS):
             nc.sync.dma_start(
                 out=wd_scale_raw[r:P:32, :, :],
                 in_=wd_scales[:, r:16:ROWS, :].rearrange("a q c -> q a c").bitcast(I32),
             )
-        load_table(doc_win[1], tab2_words, 1)
-        load_wq(wq_raw[0, 0], 0, PASS // 2)
         nc.sync.dma_start(query_list[:], offs)
+        nc.sync.dma_start(out=query_scale_win[0 : P : 2 * ROWS, :], in_=tab_scales[0].bitcast(I32))
+        load_table(doc_win[1], tab2_words, 1)
         doc_plane_both = tile("doc_plane_both", [P, S], U8)
         gather(doc_plane_both[:], doc_scale_win[:], doc_list[:])
+        load_wq(wq_raw[0, 0], 0, PASS // 2)
+        load_wq(wq_raw[0, 1], PASS // 2, PASS // 2)
         for r in range(ROWS):
             nc.sync.dma_start(
-                out=query_scale_win[QUERY_PLANE + r : P : 32, :], in_=tab_scales[0, r:16:ROWS, :].bitcast(I32)
+                out=doc_plane_second[r:P:32, :], in_=doc_plane_both[ROWS + 2 * ROWS * r : P : 32, :].bitcast(I32)
             )
-        load_wq(wq_raw[0, 1], PASS // 2, PASS // 2)
-        move_second_plane(doc_plane_second, doc_plane_both)
         load_table(query_win, tab_words, 0)
+        load_wd(1)
+        doc_codes_first = tile("doc_codes_first", [P, S], U32)
+        gather(doc_codes_first[:], doc_win[0][:], doc_list[:])
+        query_rows = tile("query_rows", [P, S], U8)
+        gather(query_rows[:], query_scale_win[:], query_list[:])
+        for r in range(ROWS):
+            nc.sync.dma_start(out=query_plane[r:P:32, :], in_=query_rows[2 * ROWS * r : P : 32, :].bitcast(I32))
         wd_planes = [tile("wd_planes%d" % g, [P, DOC_PASSES, PACK, P], U8) for g in range(GROUPS)]
         for g in range(GROUPS):
             for a in range(DOC_PASSES):
@@ -124,7 +123,6 @@ def tile_list_duplicate_match_features_kernel(
         warm = tile("warm", [P, 1], F32)
         nc.scalar.activation(out=warm[:], in_=root_gain[:, 0:1], func=ACT.Tanh)
 
-        load_wd(1)
         for u in range(2):
             load_wq(wq_raw[1, u], PASS + PASS // 2 * u, PASS // 2)
         for u in range(2):
@@ -134,9 +132,6 @@ def tile_list_duplicate_match_features_kernel(
         with nc.allow_non_contiguous_dma(reason="one bias value for each partition and output tile"):
             nc.sync.dma_start(out=bias[:], in_=bf.rearrange("(c p) -> p c", p=P))
 
-        doc_codes_first = tile("doc_codes_first", [P, S], U32)
-        query_plane_all = tile("query_plane_all", [P, S], U8)
-        gather(doc_codes_first[:], doc_win[0][:], doc_list[:])
         doc_planes = (doc_plane_both[:], doc_plane_second[:].bitcast(U8))
         doc_codes = {(half, 0): doc_codes_first[:, HALF * half : HALF * (half + 1)] for half in range(2)}
         query_codes, wd_codes, wq_woven, wq_codes, wq_plane, wf_codes, wf_plane = {}, {}, {}, {}, {}, {}, {}
@@ -214,7 +209,7 @@ def tile_list_duplicate_match_features_kernel(
                     lhsT=wq_codes[g][:, cols].bitcast(FP8X4),
                     lhsT_scale=wq_plane[g][:, cols],
                     rhs=query_codes[half].bitcast(FP8X4),
-                    rhs_scale=query_plane_all[QUERY_PLANE:P, pairs],
+                    rhs_scale=query_plane[:].bitcast(U8)[:, pairs],
                     start=False,
                     stop=(half == 0),
                 )
@@ -281,7 +276,6 @@ def tile_list_duplicate_match_features_kernel(
         doc_codes[0, 1] = gather_half("doc_codes_second", doc_win[1], doc_list, 0)
         doc_third = tile("doc_third", [P, QUARTER], U32)
         gather(doc_third[:], doc_win[1][:], doc_list[:, LIST_HALF : LIST_HALF + LIST_HALF // 2])
-        gather(query_plane_all[:], query_scale_win[:], query_list[:])
         dst = wq_target(0)
         for u in range(2):
             places = slice(P // 2 * u, P // 2 * (u + 1))

@@ -21,13 +21,14 @@ PACK = 4
 PASS = P * PACK
 GROUPS = H // PASS
 DOC_PASSES = K2 // PASS
+BLOCKS = PASS // 32
 HALF = S // 2
 LIST_HALF = HALF // 16
-QUARTER = S // 4
 OUT_TILES = N // P
 PIECE = 256
 SMALL = PIECE // 2
 ROWS = 4
+DOC_ROWS_AT = P - DOC_PASSES * BLOCKS
 
 
 def tile_list_duplicate_match_features_kernel(
@@ -44,10 +45,10 @@ def tile_list_duplicate_match_features_kernel(
         doc_list = tile("doc_list", [P, S // 16], U16)
         query_list = tile("query_list", [P, S // 16], U16)
         doc_scale_win = tile("doc_scale_win", [P, T // 4], I32)
-        doc_plane_second = tile("doc_plane_second", [P, S // 4], I32)
         query_scale_win = tile("query_scale_win", [P, T // 4], I32)
-        query_plane = tile("query_plane", [P, S // 4], I32)
         wd_scale_raw = tile("wd_scale_raw", [P, DOC_PASSES, H // 4], I32)
+        doc_plane = [tile("doc_plane%d" % a, [P, S // 4], I32) for a in range(DOC_PASSES)]
+        query_plane = tile("query_plane", [P, S // 4], I32)
         gain_cols = tile("gain_cols", [P, GROUPS, 2 * PACK], F32)
         doc_win = [tile("doc_win%d" % a, [P, T], I32) for a in range(DOC_PASSES)]
         query_win = tile("query_win", [P, T], I32)
@@ -55,12 +56,14 @@ def tile_list_duplicate_match_features_kernel(
         wq_raw = {
             (g, u): tile("wq_raw%d%d" % (g, u), [P, PACK, PASS // 2], F32) for g in range(GROUPS) for u in range(2)
         }
-        wf_raw_first = [tile("wf_raw0%d" % u, [P, PACK, N // 2], F32) for u in range(2)]
-        wf_raw_second = tile("wf_raw1", [P, PACK, N], F32)
+        wf_raw = [tile("wf_raw%d" % g, [P, PACK, N], F32) for g in range(GROUPS)]
 
         nc.gpsimd.dma_start(out=gain_cols[:, :, 0:PACK], in_=gain.rearrange("(g p t) -> p g t", g=GROUPS, t=PACK))
-        for scale_tile in (doc_scale_win, wd_scale_raw, query_scale_win, doc_plane_second, query_plane):
-            nc.vector.memset(scale_tile[:], 0)
+        nc.vector.memset(wd_scale_raw[:], 0)
+        nc.vector.memset(query_scale_win[:], 0)
+        nc.vector.memset(doc_scale_win[0:DOC_ROWS_AT, :], 0)
+        for plane in doc_plane + [query_plane]:
+            nc.vector.memset(plane[:], 0)
 
         def gather(picked, window, offsets):
             nc.vector.tensor_copy(picked, window.bitcast(picked.dtype).indirect(offsets))
@@ -72,44 +75,55 @@ def tile_list_duplicate_match_features_kernel(
             words = wd_words[:, :, 2 * PASS * g : 2 * PASS * (g + 1)]
             nc.sync.dma_start(out=wd_raw[g][:], in_=words.rearrange("a p c -> p a c").bitcast(I32))
 
-        def load_wq(raw, first, width):
-            cols = wq[:, first : first + width]
-            nc.sync.dma_start(out=raw[:], in_=cols.rearrange("(p i) c -> p i c", i=PACK))
+        def load_wq(g, u):
+            first = PASS * g + PASS // 2 * u
+            cols = wq[:, first : first + PASS // 2]
+            nc.sync.dma_start(out=wq_raw[g, u][:], in_=cols.rearrange("(p i) c -> p i c", i=PACK))
 
-        def load_wf(raw, g, first, width):
-            rows = wf[PASS * g : PASS * (g + 1), first : first + width]
-            nc.sync.dma_start(out=raw[:], in_=rows.rearrange("(p t) n -> p t n", t=PACK))
+        def load_wf(g):
+            rows = wf[PASS * g : PASS * (g + 1), :]
+            nc.sync.dma_start(out=wf_raw[g][:], in_=rows.rearrange("(p t) n -> p t n", t=PACK))
 
-        load_wd(0)
+        def move_rows(plane, rows, first, step):
+            for r in range(ROWS):
+                picked = rows[first + step * r : first + step * BLOCKS : step * ROWS, :]
+                nc.sync.dma_start(out=plane[r:P:32, :], in_=picked.bitcast(I32))
+
+        nc.sync.dma_start(
+            out=doc_scale_win[DOC_ROWS_AT:P, :], in_=tab2_scales.rearrange("a q t -> (a q) t").bitcast(I32)
+        )
         nc.sync.dma_start(doc_list[:], offs2)
-        for r in range(ROWS):
-            nc.sync.dma_start(out=doc_scale_win[r:P:32, :], in_=tab2_scales[0, r:16:ROWS, :].bitcast(I32))
-        nc.sync.dma_start(out=doc_scale_win[ROWS : P : 2 * ROWS, :], in_=tab2_scales[1].bitcast(I32))
         load_table(doc_win[0], tab2_words, 0)
+        load_wd(0)
         for r in range(ROWS):
             nc.sync.dma_start(
                 out=wd_scale_raw[r:P:32, :, :],
-                in_=wd_scales[:, r:16:ROWS, :].rearrange("a q c -> q a c").bitcast(I32),
+                in_=wd_scales[:, r:BLOCKS:ROWS, :].rearrange("a q c -> q a c").bitcast(I32),
             )
         nc.sync.dma_start(query_list[:], offs)
-        nc.sync.dma_start(out=query_scale_win[0 : P : 2 * ROWS, :], in_=tab_scales[0].bitcast(I32))
+        nc.sync.dma_start(out=query_scale_win[0 : P : P // BLOCKS, :], in_=tab_scales[0].bitcast(I32))
         load_table(doc_win[1], tab2_words, 1)
-        doc_plane_both = tile("doc_plane_both", [P, S], U8)
-        gather(doc_plane_both[:], doc_scale_win[:], doc_list[:])
-        load_wq(wq_raw[0, 0], 0, PASS // 2)
-        load_wq(wq_raw[0, 1], PASS // 2, PASS // 2)
-        for r in range(ROWS):
-            nc.sync.dma_start(
-                out=doc_plane_second[r:P:32, :], in_=doc_plane_both[ROWS + 2 * ROWS * r : P : 32, :].bitcast(I32)
-            )
+        doc_rows = tile("doc_rows", [P, S], U8)
+        gather(doc_rows[:], doc_scale_win[:], doc_list[:])
+        move_rows(doc_plane[0], doc_rows, DOC_ROWS_AT, 1)
         load_table(query_win, tab_words, 0)
-        load_wd(1)
+        move_rows(doc_plane[1], doc_rows, DOC_ROWS_AT + BLOCKS, 1)
+        load_wq(0, 0)
+        load_wq(0, 1)
         doc_codes_first = tile("doc_codes_first", [P, S], U32)
         gather(doc_codes_first[:], doc_win[0][:], doc_list[:])
         query_rows = tile("query_rows", [P, S], U8)
         gather(query_rows[:], query_scale_win[:], query_list[:])
-        for r in range(ROWS):
-            nc.sync.dma_start(out=query_plane[r:P:32, :], in_=query_rows[2 * ROWS * r : P : 32, :].bitcast(I32))
+        move_rows(query_plane, query_rows, 0, P // BLOCKS)
+        load_wd(1)
+        load_wq(1, 0)
+        load_wq(1, 1)
+        load_wf(0)
+        load_wf(1)
+        bias = tile("bias", [P, OUT_TILES], F32)
+        with nc.allow_non_contiguous_dma(reason="one bias value for each partition and output tile"):
+            nc.sync.dma_start(out=bias[:], in_=bf.rearrange("(c p) -> p c", p=P))
+
         wd_planes = [tile("wd_planes%d" % g, [P, DOC_PASSES, PACK, P], U8) for g in range(GROUPS)]
         for g in range(GROUPS):
             for a in range(DOC_PASSES):
@@ -123,48 +137,48 @@ def tile_list_duplicate_match_features_kernel(
         warm = tile("warm", [P, 1], F32)
         nc.scalar.activation(out=warm[:], in_=root_gain[:, 0:1], func=ACT.Tanh)
 
-        for u in range(2):
-            load_wq(wq_raw[1, u], PASS + PASS // 2 * u, PASS // 2)
-        for u in range(2):
-            load_wf(wf_raw_first[u], 0, N // 2 * u, N // 2)
-        load_wf(wf_raw_second, 1, 0, N)
-        bias = tile("bias", [P, OUT_TILES], F32)
-        with nc.allow_non_contiguous_dma(reason="one bias value for each partition and output tile"):
-            nc.sync.dma_start(out=bias[:], in_=bf.rearrange("(c p) -> p c", p=P))
-
-        doc_planes = (doc_plane_both[:], doc_plane_second[:].bitcast(U8))
         doc_codes = {(half, 0): doc_codes_first[:, HALF * half : HALF * (half + 1)] for half in range(2)}
-        query_codes, wd_codes, wq_woven, wq_codes, wq_plane, wf_codes, wf_plane = {}, {}, {}, {}, {}, {}, {}
+        query_codes, wd_codes, wq_codes, wq_plane, wf_codes, wf_plane = {}, {}, {}, {}, {}, {}
 
-        def gather_half(name, window, offsets, half):
-            picked = tile("%s%d" % (name, half), [P, HALF], U32)
+        def gather_half(name, window, offsets, half, tag=None):
+            picked = tile("%s%d" % (name, half), [P, HALF], U32, tag)
             gather(picked[:], window[:], offsets[:, LIST_HALF * half : LIST_HALF * (half + 1)])
             return picked[:]
 
-        def permute_wd(g):
-            wd_codes[g] = tile("wd_codes%d" % g, [P, DOC_PASSES, PACK, 2 * P], U8)
-            nc.scalar.copy(
-                out=wd_codes[g][:].bitcast(U16),
-                in_=wd_raw[g][:].bitcast(U16).rearrange("p a (m t) -> p a t m", t=PACK),
-            )
+        def permute_wd(g, a, copy):
+            wd_codes[g, a] = tile("wd_codes%d%d" % (g, a), [P, PACK, 2 * P], U8)
+            words = wd_raw[g][:, a, :].bitcast(U16)
+            copy(out=wd_codes[g, a][:].bitcast(U16), in_=words.rearrange("p (m t) -> p t m", t=PACK))
 
-        def wq_target(g):
-            wq_woven[g] = tile("wq_woven%d" % g, [P, PACK * PASS], BF16)
-            return wq_woven[g][:].rearrange("p (t m i) -> p m i t", t=PACK, i=PACK)
+        wq_woven = {
+            (g, e): tile("wq_woven%d%d" % (g, e), [P, 2 * PASS], BF16) for g in range(GROUPS) for e in range(2)
+        }
 
-        def wq_source(raw):
-            return raw[:].rearrange("p i (m t) -> p m i t", t=PACK)
+        def wq_views(g, u, e):
+            dst = wq_woven[g, e][:].rearrange("p (t m i) -> p m i t", t=2, i=PACK)[:, P // 2 * u : P // 2 * (u + 1)]
+            src = wq_raw[g, u][:].rearrange("p i (m t) -> p m i t", t=PACK)[:, :, :, 2 * e : 2 * e + 2]
+            return dst, src
+
+        def round_wq_scalar(g, u, e):
+            dst, src = wq_views(g, u, e)
+            nc.scalar.activation(out=dst, in_=src, func=ACT.Copy, scale=-1.0)
+
+        def round_wq_vector(g, u, e):
+            dst, src = wq_views(g, u, e)
+            nc.vector.tensor_scalar(dst, src, -1.0, None, ALU.mult)
 
         def quantize(codes, plane, first, width, woven):
             cols = slice(first, first + width)
             nc.vector.quantize_mx(out=codes[:, cols].bitcast(FP8X4), scales=plane[:, cols], in_=woven)
 
-        def quantize_wq(g, width):
+        def quantize_wq(g, first, width):
+            e, start = divmod(first, 2 * P)
+            woven = wq_woven[g, e][:, PACK * start : PACK * (start + width)]
+            quantize(wq_codes[g], wq_plane[g], first, width, woven)
+
+        for g in range(GROUPS):
             wq_codes[g] = tile("wq_codes%d" % g, [P, PASS], U32)
             wq_plane[g] = tile("wq_plane%d" % g, [P, PASS], U8)
-            for first in range(0, PASS, width):
-                woven = wq_woven[g][:, PACK * first : PACK * (first + width)]
-                quantize(wq_codes[g], wq_plane[g], first, width, woven)
 
         def weave(dst, src):
             nc.vector.tensor_copy(
@@ -172,54 +186,49 @@ def tile_list_duplicate_match_features_kernel(
                 in_=src.rearrange("p t (c e) -> p c t e", e=2),
             )
 
-        def prepare_wf(g, halves):
-            woven = tile("wf_woven%d" % g, [P, PACK * N], BF16)
+        wf_woven = [tile("wf_woven%d" % g, [P, PACK * N], BF16) for g in range(GROUPS)]
+        for g in range(GROUPS):
             wf_codes[g] = tile("wf_codes%d" % g, [P, N], U32)
             wf_plane[g] = tile("wf_plane%d" % g, [P, N], U8)
-            width = N // 2
-            for first, raw in zip((0, width), halves):
-                weave(woven[:, PACK * first : PACK * (first + width)], raw)
-            for first in (0, width):
-                quantize(wf_codes[g], wf_plane[g], first, width, woven[:, PACK * first : PACK * (first + width)])
 
-        def difference(half, g):
-            pairs = slice(HALF * half, HALF * (half + 1))
-            banks = []
-            for t in range(PACK):
-                bank = psum.tile([P, HALF], F32, name="diff%d%d%d" % (half, g, t), tag="bank")
-                def doc_pass(a, codes, first, width, start, stop):
-                    nc.tensor.matmul_mx(
-                        out=bank[:, first : first + width],
-                        lhsT=wd_codes[g][:, a, t, :].bitcast(FP4X4),
-                        lhsT_scale=wd_planes[g][:, a, t, :],
-                        rhs=codes.bitcast(FP8X4),
-                        rhs_scale=doc_planes[a][:, HALF * half + first : HALF * half + first + width],
-                        start=start,
-                        stop=stop,
-                    )
+        def weave_wf(g, u):
+            first = N // 2 * u
+            weave(wf_woven[g][:, PACK * first : PACK * (first + N // 2)], wf_raw[g][:, :, first : first + N // 2])
 
-                doc_pass(0, doc_codes[half, 0], 0, HALF, True, False)
-                if half == 0:
-                    doc_pass(1, doc_codes[0, 1], 0, HALF, False, False)
-                else:
-                    doc_pass(1, doc_third[:], 0, QUARTER, False, False)
-                cols = slice(P * t, P * (t + 1))
-                nc.tensor.matmul_mx(
-                    out=bank[:],
-                    lhsT=wq_codes[g][:, cols].bitcast(FP8X4),
-                    lhsT_scale=wq_plane[g][:, cols],
-                    rhs=query_codes[half].bitcast(FP8X4),
-                    rhs_scale=query_plane[:].bitcast(U8)[:, pairs],
-                    start=False,
-                    stop=(half == 0),
-                )
-                if half == 1:
-                    doc_pass(1, doc_fourth[:], QUARTER, QUARTER, False, True)
-                banks.append(bank)
-            return banks
+        def quantize_wf(g, u):
+            first = N // 2 * u
+            quantize(wf_codes[g], wf_plane[g], first, N // 2, wf_woven[g][:, PACK * first : PACK * (first + N // 2)])
 
-        h_woven_first = tile("h_woven_first", [P, PACK * PIECE], BF16, tag="wq_raw11")
-        h_woven_rest = tile("h_woven_rest", [P, GROUPS * PACK * S], BF16, tag="wf_raw1")
+        banks = {}
+
+        def doc_pass(half, g, t, a):
+            if a == 0:
+                banks[half, g, t] = psum.tile([P, HALF], F32, name="diff%d%d%d" % (half, g, t), tag="bank")
+            nc.tensor.matmul_mx(
+                out=banks[half, g, t][:],
+                lhsT=wd_codes[g, a][:, t, :].bitcast(FP4X4),
+                lhsT_scale=wd_planes[g][:, a, t, :],
+                rhs=doc_codes[half, a].bitcast(FP8X4),
+                rhs_scale=doc_plane[a][:].bitcast(U8)[:, HALF * half : HALF * (half + 1)],
+                start=(a == 0),
+                stop=False,
+            )
+
+        def query_pass(half, g, t):
+            cols = slice(P * t, P * (t + 1))
+            nc.tensor.matmul_mx(
+                out=banks[half, g, t][:],
+                lhsT=wq_codes[g][:, cols].bitcast(FP8X4),
+                lhsT_scale=wq_plane[g][:, cols],
+                rhs=query_codes[half].bitcast(FP8X4),
+                rhs_scale=query_plane[:].bitcast(U8)[:, HALF * half : HALF * (half + 1)],
+                start=False,
+                stop=True,
+            )
+
+        h_woven_first = tile("h_woven_first", [P, PACK * HALF], BF16)
+        h_woven_second = tile("h_woven_second", [P, PACK * PIECE], BF16, tag="wf_raw1")
+        h_woven_rest = tile("h_woven_rest", [P, GROUPS * PACK * S], BF16, tag="wf_woven1")
         h_codes = [tile("h_codes%d" % g, [P, S], U32) for g in range(GROUPS)]
         h_plane = [tile("h_plane%d" % g, [P, S], U8) for g in range(GROUPS)]
         h_rows = {
@@ -227,15 +236,17 @@ def tile_list_duplicate_match_features_kernel(
         }
 
         def h_woven(g, first, width):
-            if g == 0 and first < PIECE:
+            if g == 0 and first < HALF:
                 return h_woven_first[:, PACK * first : PACK * (first + width)]
+            if g == 1 and first < PIECE:
+                return h_woven_second[:, PACK * first : PACK * (first + width)]
             return h_woven_rest[:, PACK * (S * g + first) : PACK * (S * g + first + width)]
 
-        def square(half, g, banks):
+        def square(half, g):
             for t in range(PACK):
                 nc.scalar.activation(
                     out=h_rows[half, g][:, t, :],
-                    in_=banks[t][:],
+                    in_=banks[half, g, t][:],
                     func=ACT.Square,
                     scale=root_gain[:, PACK * g + t : PACK * g + t + 1],
                 )
@@ -249,12 +260,12 @@ def tile_list_duplicate_match_features_kernel(
 
         def features(first, width, passes, per_store=2):
             pairs = slice(first, first + width)
-            banks = [psum.tile([P, width], F32, name="y%d_%d" % (first, c), tag="bank") for c in range(OUT_TILES)]
+            sums = [psum.tile([P, width], F32, name="y%d_%d" % (first, c), tag="bank") for c in range(OUT_TILES)]
             opened = set()
             for g, c in passes:
                 rows = slice(P * c, P * (c + 1))
                 nc.tensor.matmul_mx(
-                    out=banks[c][:],
+                    out=sums[c][:],
                     lhsT=wf_codes[g][:, rows].bitcast(FP8X4),
                     lhsT_scale=wf_plane[g][:, rows],
                     rhs=h_codes[g][:, pairs].bitcast(FP8X4),
@@ -267,57 +278,73 @@ def tile_list_duplicate_match_features_kernel(
                 result = tile("result%d_%d" % (first, c0), [P, per_store, width], F32)
                 for e in range(per_store):
                     c = c0 + e
-                    nc.scalar.activation(out=result[:, e, :], in_=banks[c][:], func=ACT.Tanh, bias=bias[:, c : c + 1])
+                    nc.scalar.activation(out=result[:, e, :], in_=sums[c][:], func=ACT.Tanh, bias=bias[:, c : c + 1])
                 nc.sync.dma_start(
                     out=out[P * c0 : P * (c0 + per_store), pairs].rearrange("(e p) j -> p e j", p=P), in_=result[:]
                 )
 
-        permute_wd(0)
-        doc_codes[0, 1] = gather_half("doc_codes_second", doc_win[1], doc_list, 0)
-        doc_third = tile("doc_third", [P, QUARTER], U32)
-        gather(doc_third[:], doc_win[1][:], doc_list[:, LIST_HALF : LIST_HALF + LIST_HALF // 2])
-        dst = wq_target(0)
-        for u in range(2):
-            places = slice(P // 2 * u, P // 2 * (u + 1))
-            nc.scalar.activation(out=dst[:, places], in_=wq_source(wq_raw[0, u]), func=ACT.Copy, scale=-1.0)
-        quantize_wq(0, PASS)
-        banks = {}
+        for a in range(DOC_PASSES):
+            permute_wd(0, a, nc.scalar.copy)
+        for half in range(2):
+            doc_codes[half, 1] = gather_half("doc_codes_second", doc_win[1], doc_list, half)
+        for a in range(DOC_PASSES):
+            for half in range(2):
+                for t in range(PACK):
+                    doc_pass(half, 0, t, a)
         query_codes[0] = gather_half("query_codes", query_win, query_list, 0)
-        banks[0, 0] = difference(0, 0)
-        query_codes[1] = gather_half("query_codes", query_win, query_list, 1)
-        permute_wd(1)
-        doc_fourth = tile("doc_fourth", [P, QUARTER], U32, tag="wd_raw1")
-        gather(doc_fourth[:], doc_win[1][:], doc_list[:, LIST_HALF + LIST_HALF // 2 : 2 * LIST_HALF])
-        banks[1, 0] = difference(1, 0)
+        for e in range(2):
+            round_wq_scalar(0, 0, e)
+        round_wq_vector(0, 1, 0)
+        round_wq_scalar(0, 1, 1)
+        permute_wd(1, 0, nc.scalar.copy)
+        quantize_wq(0, 0, P)
+        quantize_wq(0, P, P)
+        quantize_wq(0, 2 * P, 2 * P)
+        query_codes[1] = gather_half("query_codes", query_win, query_list, 1, "wq_woven00")
+        for half in range(2):
+            for t in range(PACK):
+                query_pass(half, 0, t)
 
-        dst = wq_target(1)
+        for e in range(2):
+            round_wq_vector(1, 0, e)
+        permute_wd(1, 1, nc.vector.tensor_copy)
+        for e in range(2):
+            round_wq_vector(1, 1, e)
+        for e in range(2):
+            quantize_wq(1, 2 * P * e, 2 * P)
+        square(0, 0)
+        square(1, 0)
+        for half in range(2):
+            for t in range(PACK):
+                for a in range(DOC_PASSES):
+                    doc_pass(half, 1, t, a)
+                query_pass(half, 1, t)
+            square(half, 1)
+        for first in (0, PIECE):
+            weave_h(0, first, PIECE)
+        for first in (0, PIECE):
+            quantize_h(0, first, PIECE)
         for u in range(2):
-            places, src = slice(P // 2 * u, P // 2 * (u + 1)), wq_source(wq_raw[1, u])
-            for t in (0, 2):
-                nc.vector.tensor_scalar(dst[:, places, :, t : t + 2], src[:, :, :, t : t + 2], -1.0, None, ALU.mult)
-        quantize_wq(1, PASS // 2)
-        square(0, 0, banks[0, 0])
-        for first in (0, SMALL):
-            weave_h(0, first, SMALL)
-        for first in (0, SMALL):
-            quantize_h(0, first, SMALL)
-        banks[0, 1] = difference(0, 1)
-        square(0, 1, banks[0, 1])
-        square(1, 0, banks[1, 0])
-        banks[1, 1] = difference(1, 1)
-        prepare_wf(0, [raw[:] for raw in wf_raw_first])
-        prepare_wf(1, [wf_raw_second[:, :, 0 : N // 2], wf_raw_second[:, :, N // 2 : N]])
-        square(1, 1, banks[1, 1])
+            weave_wf(0, u)
+        for u in range(2):
+            quantize_wf(0, u)
+        for u in range(2):
+            weave_wf(1, u)
+        quantize_wf(1, 0)
+        weave_h(1, 0, PIECE)
+        quantize_wf(1, 1)
+        quantize_h(1, 0, PIECE)
 
         by_tile = [(g, c) for c in range(OUT_TILES) for g in (1, 0)]
         by_group = [(g, c) for g in range(GROUPS) for c in range(OUT_TILES)]
-        weave_h(1, 0, PIECE)
-        weave_h(0, PIECE, PIECE)
-        quantize_h(1, 0, PIECE)
         features(0, PIECE, by_tile)
-        for first, width in ((PIECE, PIECE), (2 * PIECE, PIECE), (3 * PIECE, SMALL), (3 * PIECE + SMALL, SMALL)):
+        weave_h(1, PIECE, PIECE)
+        weave_h(0, 2 * PIECE, PIECE)
+        quantize_h(1, PIECE, PIECE)
+        features(PIECE, PIECE, by_group)
+        for first, width in ((2 * PIECE, PIECE), (3 * PIECE, SMALL), (3 * PIECE + SMALL, SMALL)):
             for g in range(GROUPS):
-                if (g, first) != (0, PIECE):
+                if (g, first) != (0, 2 * PIECE):
                     weave_h(g, first, width)
             for g in range(GROUPS):
                 quantize_h(g, first, width)

@@ -52,12 +52,16 @@ def tile_list_duplicate_match_features_kernel(
         gain_cols = tile("gain_cols", [P, GROUPS, 2 * PACK], F32)
         doc_win = [tile("doc_win%d" % a, [P, T], I32) for a in range(DOC_PASSES)]
         query_win = tile("query_win", [P, T], I32)
-        wd_raw = [tile("wd_raw%d" % g, [P, DOC_PASSES, PASS // 2], I32) for g in range(GROUPS)]
+        wd_raw = tile("wd_raw", [P, DOC_PASSES, H // 2], I32)
         wq_raw = {
             (g, u): tile("wq_raw%d%d" % (g, u), [P, PACK, PASS // 2], F32) for g in range(GROUPS) for u in range(2)
         }
         wf_raw = [tile("wf_raw%d" % g, [P, PACK, N], F32) for g in range(GROUPS)]
 
+        halves = tile("halves", [P, GROUPS * PACK], F32)
+        nc.gpsimd.memset(halves[:], 0.5)
+        warm = tile("warm", [P, 1], F32)
+        nc.scalar.activation(out=warm[:], in_=halves[:, 0:1], func=ACT.Tanh)
         nc.gpsimd.dma_start(out=gain_cols[:, :, 0:PACK], in_=gain.rearrange("(g p t) -> p g t", g=GROUPS, t=PACK))
         nc.vector.memset(wd_scale_raw[:], 0)
         nc.vector.memset(query_scale_win[:], 0)
@@ -70,10 +74,6 @@ def tile_list_duplicate_match_features_kernel(
 
         def load_table(window, words, a):
             nc.sync.dma_start(out=window[:], in_=words[a].rearrange("p t i -> p (t i)").bitcast(I32))
-
-        def load_wd(g):
-            words = wd_words[:, :, 2 * PASS * g : 2 * PASS * (g + 1)]
-            nc.sync.dma_start(out=wd_raw[g][:], in_=words.rearrange("a p c -> p a c").bitcast(I32))
 
         def load_wq(g, u):
             first = PASS * g + PASS // 2 * u
@@ -94,14 +94,14 @@ def tile_list_duplicate_match_features_kernel(
         )
         nc.sync.dma_start(doc_list[:], offs2)
         load_table(doc_win[0], tab2_words, 0)
-        load_wd(0)
+        nc.sync.dma_start(query_list[:], offs)
+        nc.sync.dma_start(out=query_scale_win[0 : P : P // BLOCKS, :], in_=tab_scales[0].bitcast(I32))
         for r in range(ROWS):
             nc.sync.dma_start(
                 out=wd_scale_raw[r:P:32, :, :],
                 in_=wd_scales[:, r:BLOCKS:ROWS, :].rearrange("a q c -> q a c").bitcast(I32),
             )
-        nc.sync.dma_start(query_list[:], offs)
-        nc.sync.dma_start(out=query_scale_win[0 : P : P // BLOCKS, :], in_=tab_scales[0].bitcast(I32))
+        nc.sync.dma_start(out=wd_raw[:], in_=wd_words.rearrange("a p c -> p a c").bitcast(I32))
         load_table(doc_win[1], tab2_words, 1)
         doc_rows = tile("doc_rows", [P, S], U8)
         gather(doc_rows[:], doc_scale_win[:], doc_list[:])
@@ -115,7 +115,6 @@ def tile_list_duplicate_match_features_kernel(
         query_rows = tile("query_rows", [P, S], U8)
         gather(query_rows[:], query_scale_win[:], query_list[:])
         move_rows(query_plane, query_rows, 0, P // BLOCKS)
-        load_wd(1)
         load_wq(1, 0)
         load_wq(1, 1)
         load_wf(0)
@@ -131,11 +130,12 @@ def tile_list_duplicate_match_features_kernel(
                 nc.gpsimd.tensor_copy(out=wd_planes[g][:, a], in_=cols.rearrange("p (m t) -> p t m", t=PACK))
 
         root_gain = tile("root_gain", [P, GROUPS * PACK], F32)
-        nc.scalar.activation(
-            out=root_gain[:].rearrange("p (g t) -> p g t", g=GROUPS), in_=gain_cols[:, :, 0:PACK], func=ACT.Sqrt
+        nc.gpsimd.tensor_tensor(
+            out=root_gain[:].rearrange("p (g t) -> p g t", g=GROUPS),
+            in0=gain_cols[:, :, 0:PACK],
+            in1=halves[:].rearrange("p (g t) -> p g t", g=GROUPS),
+            op=ALU.pow,
         )
-        warm = tile("warm", [P, 1], F32)
-        nc.scalar.activation(out=warm[:], in_=root_gain[:, 0:1], func=ACT.Tanh)
 
         doc_codes = {(half, 0): doc_codes_first[:, HALF * half : HALF * (half + 1)] for half in range(2)}
         query_codes, wd_codes, wq_codes, wq_plane, wf_codes, wf_plane = {}, {}, {}, {}, {}, {}
@@ -145,10 +145,10 @@ def tile_list_duplicate_match_features_kernel(
             gather(picked[:], window[:], offsets[:, LIST_HALF * half : LIST_HALF * (half + 1)])
             return picked[:]
 
-        def permute_wd(g, a, copy):
+        def permute_wd(g, a):
             wd_codes[g, a] = tile("wd_codes%d%d" % (g, a), [P, PACK, 2 * P], U8)
-            words = wd_raw[g][:, a, :].bitcast(U16)
-            copy(out=wd_codes[g, a][:].bitcast(U16), in_=words.rearrange("p (m t) -> p t m", t=PACK))
+            words = wd_raw[:, a, PASS // 2 * g : PASS // 2 * (g + 1)].bitcast(U16)
+            nc.scalar.copy(out=wd_codes[g, a][:].bitcast(U16), in_=words.rearrange("p (m t) -> p t m", t=PACK))
 
         wq_woven = {
             (g, e): tile("wq_woven%d%d" % (g, e), [P, 2 * PASS], BF16) for g in range(GROUPS) for e in range(2)
@@ -283,8 +283,9 @@ def tile_list_duplicate_match_features_kernel(
                     out=out[P * c0 : P * (c0 + per_store), pairs].rearrange("(e p) j -> p e j", p=P), in_=result[:]
                 )
 
-        for a in range(DOC_PASSES):
-            permute_wd(0, a, nc.scalar.copy)
+        for g in range(GROUPS):
+            for a in range(DOC_PASSES):
+                permute_wd(g, a)
         for half in range(2):
             doc_codes[half, 1] = gather_half("doc_codes_second", doc_win[1], doc_list, half)
         for a in range(DOC_PASSES):
@@ -296,7 +297,6 @@ def tile_list_duplicate_match_features_kernel(
             round_wq_scalar(0, 0, e)
         round_wq_vector(0, 1, 0)
         round_wq_scalar(0, 1, 1)
-        permute_wd(1, 0, nc.scalar.copy)
         quantize_wq(0, 0, P)
         quantize_wq(0, P, P)
         quantize_wq(0, 2 * P, 2 * P)
@@ -307,7 +307,6 @@ def tile_list_duplicate_match_features_kernel(
 
         for e in range(2):
             round_wq_vector(1, 0, e)
-        permute_wd(1, 1, nc.vector.tensor_copy)
         for e in range(2):
             round_wq_vector(1, 1, e)
         for e in range(2):

@@ -295,11 +295,12 @@ def tile_list_duplicate_match_features_kernel(
         query_codes[0] = gather_half("query_codes", query_win, query_list, 0)
         for e in range(2):
             round_wq_scalar(0, 0, e)
+        for t in range(PACK):
+            quantize_wq(0, P * t, P // 2)
         round_wq_vector(0, 1, 0)
         round_wq_scalar(0, 1, 1)
-        quantize_wq(0, 0, P)
-        quantize_wq(0, P, P)
-        quantize_wq(0, 2 * P, 2 * P)
+        for t in range(PACK):
+            quantize_wq(0, P * t + P // 2, P // 2)
         query_codes[1] = gather_half("query_codes", query_win, query_list, 1, "wq_woven00")
         for half in range(2):
             for t in range(PACK):

@@ -72,8 +72,9 @@ def tile_list_duplicate_match_features_kernel(
         def gather(picked, window, offsets):
             nc.vector.tensor_copy(picked, window.bitcast(picked.dtype).indirect(offsets))
 
-        def load_table(window, words, a):
-            nc.sync.dma_start(out=window[:], in_=words[a].rearrange("p t i -> p (t i)").bitcast(I32))
+        def load_table(window, words, a, first=0, width=T):
+            cols = words[a].rearrange("p t i -> p (t i)").bitcast(I32)[:, first : first + width]
+            nc.sync.dma_start(out=window[:, first : first + width], in_=cols)
 
         def load_wq(g, u):
             first = PASS * g + PASS // 2 * u
@@ -102,12 +103,14 @@ def tile_list_duplicate_match_features_kernel(
                 in_=wd_scales[:, r:BLOCKS:ROWS, :].rearrange("a q c -> q a c").bitcast(I32),
             )
         nc.sync.dma_start(out=wd_raw[:], in_=wd_words.rearrange("a p c -> p a c").bitcast(I32))
-        load_table(doc_win[1], tab2_words, 1)
+        load_table(doc_win[1], tab2_words, 1, 0, T // 2)
         doc_rows = tile("doc_rows", [P, S], U8)
         gather(doc_rows[:], doc_scale_win[:], doc_list[:])
         move_rows(doc_plane[0], doc_rows, DOC_ROWS_AT, 1)
-        load_table(query_win, tab_words, 0)
+        load_table(doc_win[1], tab2_words, 1, T // 2, T // 2)
+        load_table(query_win, tab_words, 0, 0, T // 2)
         move_rows(doc_plane[1], doc_rows, DOC_ROWS_AT + BLOCKS, 1)
+        load_table(query_win, tab_words, 0, T // 2, T // 2)
         load_wq(0, 0)
         load_wq(0, 1)
         doc_codes_first = tile("doc_codes_first", [P, S], U32)

@@ -29,6 +29,8 @@ PIECE = 256
 SMALL = PIECE // 2
 ROWS = 4
 DOC_ROWS_AT = P - DOC_PASSES * BLOCKS
+QUERY_ROWS_AT = 4
+QUERY_PLANE_AT = 8
 
 
 def tile_list_duplicate_match_features_kernel(
@@ -85,10 +87,10 @@ def tile_list_duplicate_match_features_kernel(
             rows = wf[PASS * g : PASS * (g + 1), :]
             nc.sync.dma_start(out=wf_raw[g][:], in_=rows.rearrange("(p t) n -> p t n", t=PACK))
 
-        def move_rows(plane, rows, first, step):
+        def move_rows(plane, rows, first, step, up=0):
             for r in range(ROWS):
-                picked = rows[first + step * r : first + step * BLOCKS : step * ROWS, :]
-                nc.sync.dma_start(out=plane[r:P:32, :], in_=picked.bitcast(I32))
+                picked = rows[first + step * r : first + step * (BLOCKS - 1) + 1 : step * ROWS, :]
+                nc.sync.dma_start(out=plane[up + r : P : 32, :], in_=picked.bitcast(I32))
 
         nc.sync.dma_start(
             out=doc_scale_win[DOC_ROWS_AT:P, :], in_=tab2_scales.rearrange("a q t -> (a q) t").bitcast(I32)
@@ -96,7 +98,7 @@ def tile_list_duplicate_match_features_kernel(
         nc.sync.dma_start(doc_list[:], offs2)
         load_table(doc_win[0], tab2_words, 0)
         nc.sync.dma_start(query_list[:], offs)
-        nc.sync.dma_start(out=query_scale_win[0 : P : P // BLOCKS, :], in_=tab_scales[0].bitcast(I32))
+        nc.sync.dma_start(out=query_scale_win[QUERY_ROWS_AT : P : P // BLOCKS, :], in_=tab_scales[0].bitcast(I32))
         for r in range(ROWS):
             nc.sync.dma_start(
                 out=wd_scale_raw[r:P:32, :, :],
@@ -117,7 +119,7 @@ def tile_list_duplicate_match_features_kernel(
         gather(doc_codes_first[:], doc_win[0][:], doc_list[:])
         query_rows = tile("query_rows", [P, S], U8)
         gather(query_rows[:], query_scale_win[:], query_list[:])
-        move_rows(query_plane, query_rows, 0, P // BLOCKS)
+        move_rows(query_plane, query_rows, QUERY_ROWS_AT, P // BLOCKS, QUERY_PLANE_AT)
         load_wq(1, 0)
         load_wq(1, 1)
         load_wf(0)
@@ -224,7 +226,7 @@ def tile_list_duplicate_match_features_kernel(
                 lhsT=wq_codes[g][:, cols].bitcast(FP8X4),
                 lhsT_scale=wq_plane[g][:, cols],
                 rhs=query_codes[half].bitcast(FP8X4),
-                rhs_scale=query_plane[:].bitcast(U8)[:, HALF * half : HALF * (half + 1)],
+                rhs_scale=query_plane[:].bitcast(U8)[QUERY_PLANE_AT:P, HALF * half : HALF * (half + 1)],
                 start=False,
                 stop=True,
             )

@@ -27,6 +27,7 @@ LIST_HALF = HALF // 16
 OUT_TILES = N // P
 PIECE = 256
 SMALL = PIECE // 2
+PAD = 32
 ROWS = 4
 DOC_ROWS_AT = P - DOC_PASSES * BLOCKS
 QUERY_ROWS_AT = 4
@@ -64,7 +65,6 @@ def tile_list_duplicate_match_features_kernel(
         nc.gpsimd.memset(halves[:], 0.5)
         warm = tile("warm", [P, 1], F32)
         nc.scalar.activation(out=warm[:], in_=halves[:, 0:1], func=ACT.Tanh)
-        nc.gpsimd.dma_start(out=gain_cols[:, :, 0:PACK], in_=gain.rearrange("(g p t) -> p g t", g=GROUPS, t=PACK))
         nc.vector.memset(wd_scale_raw[:], 0)
         nc.vector.memset(query_scale_win[:], 0)
         nc.vector.memset(doc_scale_win[0:DOC_ROWS_AT, :], 0)
@@ -106,6 +106,7 @@ def tile_list_duplicate_match_features_kernel(
             )
         nc.sync.dma_start(out=wd_raw[:], in_=wd_words.rearrange("a p c -> p a c").bitcast(I32))
         load_table(doc_win[1], tab2_words, 1, 0, T // 2)
+        nc.sync.dma_start(out=gain_cols[:, :, 0:PACK], in_=gain.rearrange("(g p t) -> p g t", g=GROUPS, t=PACK))
         doc_rows = tile("doc_rows", [P, S], U8)
         gather(doc_rows[:], doc_scale_win[:], doc_list[:])
         move_rows(doc_plane[0], doc_rows, DOC_ROWS_AT, 1)
@@ -237,7 +238,7 @@ def tile_list_duplicate_match_features_kernel(
         h_codes = [tile("h_codes%d" % g, [P, S], U32) for g in range(GROUPS)]
         h_plane = [tile("h_plane%d" % g, [P, S], U8) for g in range(GROUPS)]
         h_rows = {
-            (half, g): tile("h_rows%d%d" % (half, g), [P, PACK, HALF], BF16) for half in range(2) for g in range(GROUPS)
+            (half, g): tile("h_rows%d%d" % (half, g), [P, PACK, HALF + PAD], BF16) for half in range(2) for g in range(GROUPS)
         }
 
         def h_woven(g, first, width):
@@ -250,7 +251,7 @@ def tile_list_duplicate_match_features_kernel(
         def square(half, g):
             for t in range(PACK):
                 nc.scalar.activation(
-                    out=h_rows[half, g][:, t, :],
+                    out=h_rows[half, g][:, t, 0:HALF],
                     in_=banks[half, g, t][:],
                     func=ACT.Square,
                     scale=root_gain[:, PACK * g + t : PACK * g + t + 1],

from contextlib import ExitStack

import concourse.mybir as mybir

K, K2, H, N, T, S = 512, 1024, 1024, 512, 2048, 1024
FLOPS = 2 * S * (K * H + K2 * H + H * N)

F32 = mybir.dt.float32
BF16 = mybir.dt.bfloat16
I32 = mybir.dt.int32
U32 = mybir.dt.uint32
U16 = mybir.dt.uint16
U8 = mybir.dt.uint8
FP8X4 = mybir.dt.float8_e4m3fn_x4
FP4X4 = mybir.dt.float4_e2m1fn_x4
ACT = mybir.ActivationFunctionType
ALU = mybir.AluOpType

P = 128
PACK = 4
PASS = P * PACK
GROUPS = H // PASS
DOC_PASSES = K2 // PASS
BLOCKS = PASS // 32
HALF = S // 2
LIST_HALF = HALF // 16
OUT_TILES = N // P
PIECE = 256
SMALL = PIECE // 2
PAD = 32
ROWS = 4
DOC_ROWS_AT = P - DOC_PASSES * BLOCKS
QUERY_ROWS_AT = 4
QUERY_PLANE_AT = 8


def tile_list_duplicate_match_features_kernel(
    tc, tab_words, tab_scales, tab2_words, tab2_scales, offs, offs2, wq, wd_words, wd_scales, gain, wf, bf, out
):
    nc = tc.nc
    with ExitStack() as ctx:
        sb = ctx.enter_context(tc.tile_pool(name="sb", bufs=1))
        psum = ctx.enter_context(tc.psum_pool(name="psum", bufs=8))

        def tile(name, shape, dtype, tag=None):
            return sb.tile(shape, dtype, name=name, tag=tag or name, align_bytes=256)

        doc_list = tile("doc_list", [P, S // 16], U16)
        query_list = tile("query_list", [P, S // 16], U16)
        doc_scale_win = tile("doc_scale_win", [P, T // 4], I32)
        query_scale_win = tile("query_scale_win", [P, T // 4], I32)
        wd_scale_raw = tile("wd_scale_raw", [P, DOC_PASSES, H // 4], I32)
        doc_plane = [tile("doc_plane%d" % a, [P, S // 4], I32) for a in range(DOC_PASSES)]
        query_plane = tile("query_plane", [P, S // 4], I32)
        gain_cols = tile("gain_cols", [P, GROUPS, 2 * PACK], F32)
        doc_win = [tile("doc_win%d" % a, [P, T], I32) for a in range(DOC_PASSES)]
        query_win = tile("query_win", [P, T], I32)
        wd_raw = tile("wd_raw", [P, DOC_PASSES, H // 2], I32)
        wq_raw = {
            (g, u): tile("wq_raw%d%d" % (g, u), [P, PACK, PASS // 2], F32) for g in range(GROUPS) for u in range(2)
        }
        wf_raw = [tile("wf_raw%d" % g, [P, PACK, N], F32) for g in range(GROUPS)]

        halves = tile("halves", [P, GROUPS * PACK], F32)
        nc.gpsimd.memset(halves[:], 0.5)
        warm = tile("warm", [P, 1], F32)
        nc.scalar.activation(out=warm[:], in_=halves[:, 0:1], func=ACT.Tanh)
        nc.vector.memset(wd_scale_raw[:], 0)
        nc.vector.memset(query_scale_win[:], 0)
        nc.vector.memset(doc_scale_win[0:DOC_ROWS_AT, :], 0)
        for plane in doc_plane + [query_plane]:
            nc.vector.memset(plane[:], 0)

        def gather(picked, window, offsets):
            nc.vector.tensor_copy(picked, window.bitcast(picked.dtype).indirect(offsets))

        def load_table(window, words, a, first=0, width=T):
            cols = words[a].rearrange("p t i -> p (t i)").bitcast(I32)[:, first : first + width]
            nc.sync.dma_start(out=window[:, first : first + width], in_=cols)

        def load_wq(g, u):
            first = PASS * g + PASS // 2 * u
            cols = wq[:, first : first + PASS // 2]
            nc.sync.dma_start(out=wq_raw[g, u][:], in_=cols.rearrange("(p i) c -> p i c", i=PACK))

        def load_wf(g):
            rows = wf[PASS * g : PASS * (g + 1), :]
            nc.sync.dma_start(out=wf_raw[g][:], in_=rows.rearrange("(p t) n -> p t n", t=PACK))

        def move_rows(plane, rows, first, step, up=0):
            for r in range(ROWS):
                picked = rows[first + step * r : first + step * (BLOCKS - 1) + 1 : step * ROWS, :]
                nc.sync.dma_start(out=plane[up + r : P : 32, :], in_=picked.bitcast(I32))

        nc.sync.dma_start(
            out=doc_scale_win[DOC_ROWS_AT:P, :], in_=tab2_scales.rearrange("a q t -> (a q) t").bitcast(I32)
        )
        nc.sync.dma_start(doc_list[:], offs2)
        load_table(doc_win[0], tab2_words, 0)
        nc.sync.dma_start(query_list[:], offs)
        nc.sync.dma_start(out=query_scale_win[QUERY_ROWS_AT : P : P // BLOCKS, :], in_=tab_scales[0].bitcast(I32))
        for r in range(ROWS):
            nc.sync.dma_start(
                out=wd_scale_raw[r:P:32, :, :],
                in_=wd_scales[:, r:BLOCKS:ROWS, :].rearrange("a q c -> q a c").bitcast(I32),
            )
        nc.sync.dma_start(out=wd_raw[:], in_=wd_words.rearrange("a p c -> p a c").bitcast(I32))
        load_table(doc_win[1], tab2_words, 1, 0, T // 2)
        nc.sync.dma_start(out=gain_cols[:, :, 0:PACK], in_=gain.rearrange("(g p t) -> p g t", g=GROUPS, t=PACK))
        doc_rows = tile("doc_rows", [P, S], U8)
        gather(doc_rows[:], doc_scale_win[:], doc_list[:])
        move_rows(doc_plane[0], doc_rows, DOC_ROWS_AT, 1)
        load_table(doc_win[1], tab2_words, 1, T // 2, T // 2)
        load_table(query_win, tab_words, 0, 0, T // 2)
        move_rows(doc_plane[1], doc_rows, DOC_ROWS_AT + BLOCKS, 1)
        load_table(query_win, tab_words, 0, T // 2, T // 2)
        load_wq(0, 0)
        load_wq(0, 1)
        doc_codes_first = tile("doc_codes_first", [P, S], U32)
        gather(doc_codes_first[:], doc_win[0][:], doc_list[:])
        query_rows = tile("query_rows", [P, S], U8)
        gather(query_rows[:], query_scale_win[:], query_list[:])
        move_rows(query_plane, query_rows, QUERY_ROWS_AT, P // BLOCKS, QUERY_PLANE_AT)
        load_wq(1, 0)
        load_wq(1, 1)
        load_wf(0)
        load_wf(1)
        bias = tile("bias", [P, OUT_TILES], F32)
        with nc.allow_non_contiguous_dma(reason="one bias value for each partition and output tile"):
            nc.sync.dma_start(out=bias[:], in_=bf.rearrange("(c p) -> p c", p=P))

        wd_planes = [tile("wd_planes%d" % g, [P, DOC_PASSES, PACK, P], U8) for g in range(GROUPS)]
        for g in range(GROUPS):
            for a in range(DOC_PASSES):
                cols = wd_scale_raw[:].bitcast(U8)[:, a, PASS * g : PASS * (g + 1)]
                nc.gpsimd.tensor_copy(out=wd_planes[g][:, a], in_=cols.rearrange("p (m t) -> p t m", t=PACK))

        root_gain = tile("root_gain", [P, GROUPS * PACK], F32)
        nc.gpsimd.tensor_tensor(
            out=root_gain[:].rearrange("p (g t) -> p g t", g=GROUPS),
            in0=gain_cols[:, :, 0:PACK],
            in1=halves[:].rearrange("p (g t) -> p g t", g=GROUPS),
            op=ALU.pow,
        )

        doc_codes = {(half, 0): doc_codes_first[:, HALF * half : HALF * (half + 1)] for half in range(2)}
        query_codes, wd_codes, wq_codes, wq_plane, wf_codes, wf_plane = {}, {}, {}, {}, {}, {}

        def gather_half(name, window, offsets, half, tag=None):
            picked = tile("%s%d" % (name, half), [P, HALF], U32, tag)
            gather(picked[:], window[:], offsets[:, LIST_HALF * half : LIST_HALF * (half + 1)])
            return picked[:]

        def permute_wd(g, a):
            wd_codes[g, a] = tile("wd_codes%d%d" % (g, a), [P, PACK, 2 * P], U8)
            words = wd_raw[:, a, PASS // 2 * g : PASS // 2 * (g + 1)].bitcast(U16)
            nc.scalar.copy(out=wd_codes[g, a][:].bitcast(U16), in_=words.rearrange("p (m t) -> p t m", t=PACK))

        wq_woven = {
            (g, e): tile("wq_woven%d%d" % (g, e), [P, 2 * PASS], BF16) for g in range(GROUPS) for e in range(2)
        }

        def wq_views(g, u, e):
            dst = wq_woven[g, e][:].rearrange("p (t m i) -> p m i t", t=2, i=PACK)[:, P // 2 * u : P // 2 * (u + 1)]
            src = wq_raw[g, u][:].rearrange("p i (m t) -> p m i t", t=PACK)[:, :, :, 2 * e : 2 * e + 2]
            return dst, src

        def round_wq_scalar(g, u, e):
            dst, src = wq_views(g, u, e)
            nc.scalar.activation(out=dst, in_=src, func=ACT.Copy, scale=-1.0)

        def round_wq_vector(g, u, e):
            dst, src = wq_views(g, u, e)
            nc.vector.tensor_scalar(dst, src, -1.0, None, ALU.mult)

        def quantize(codes, plane, first, width, woven):
            cols = slice(first, first + width)
            nc.vector.quantize_mx(out=codes[:, cols].bitcast(FP8X4), scales=plane[:, cols], in_=woven)

        def quantize_wq(g, first, width):
            e, start = divmod(first, 2 * P)
            woven = wq_woven[g, e][:, PACK * start : PACK * (start + width)]
            quantize(wq_codes[g], wq_plane[g], first, width, woven)

        for g in range(GROUPS):
            wq_codes[g] = tile("wq_codes%d" % g, [P, PASS], U32)
            wq_plane[g] = tile("wq_plane%d" % g, [P, PASS], U8)

        def weave(dst, src):
            nc.vector.tensor_copy(
                out=dst.rearrange("p (c e t) -> p c t e", e=2, t=PACK),
                in_=src.rearrange("p t (c e) -> p c t e", e=2),
            )

        wf_woven = [tile("wf_woven%d" % g, [P, PACK * N], BF16) for g in range(GROUPS)]
        for g in range(GROUPS):
            wf_codes[g] = tile("wf_codes%d" % g, [P, N], U32)
            wf_plane[g] = tile("wf_plane%d" % g, [P, N], U8)

        def weave_wf(g, u):
            first = N // 2 * u
            weave(wf_woven[g][:, PACK * first : PACK * (first + N // 2)], wf_raw[g][:, :, first : first + N // 2])

        def quantize_wf(g, u):
            first = N // 2 * u
            quantize(wf_codes[g], wf_plane[g], first, N // 2, wf_woven[g][:, PACK * first : PACK * (first + N // 2)])

        banks = {}

        def doc_pass(half, g, t, a):
            if a == 0:
                banks[half, g, t] = psum.tile([P, HALF], F32, name="diff%d%d%d" % (half, g, t), tag="bank")
            nc.tensor.matmul_mx(
                out=banks[half, g, t][:],
                lhsT=wd_codes[g, a][:, t, :].bitcast(FP4X4),
                lhsT_scale=wd_planes[g][:, a, t, :],
                rhs=doc_codes[half, a].bitcast(FP8X4),
                rhs_scale=doc_plane[a][:].bitcast(U8)[:, HALF * half : HALF * (half + 1)],
                start=(a == 0),
                stop=False,
            )

        def query_pass(half, g, t):
            cols = slice(P * t, P * (t + 1))
            nc.tensor.matmul_mx(
                out=banks[half, g, t][:],
                lhsT=wq_codes[g][:, cols].bitcast(FP8X4),
                lhsT_scale=wq_plane[g][:, cols],
                rhs=query_codes[half].bitcast(FP8X4),
                rhs_scale=query_plane[:].bitcast(U8)[QUERY_PLANE_AT:P, HALF * half : HALF * (half + 1)],
                start=False,
                stop=True,
            )

        h_woven_first = tile("h_woven_first", [P, PACK * HALF], BF16)
        h_woven_second = tile("h_woven_second", [P, PACK * PIECE], BF16, tag="wf_raw1")
        h_woven_rest = tile("h_woven_rest", [P, GROUPS * PACK * S], BF16, tag="wf_woven1")
        h_codes = [tile("h_codes%d" % g, [P, S], U32) for g in range(GROUPS)]
        h_plane = [tile("h_plane%d" % g, [P, S], U8) for g in range(GROUPS)]
        h_rows = {
            (half, g): tile("h_rows%d%d" % (half, g), [P, PACK, HALF + PAD], BF16) for half in range(2) for g in range(GROUPS)
        }

        def h_woven(g, first, width):
            if g == 0 and first < HALF:
                return h_woven_first[:, PACK * first : PACK * (first + width)]
            if g == 1 and first < PIECE:
                return h_woven_second[:, PACK * first : PACK * (first + width)]
            return h_woven_rest[:, PACK * (S * g + first) : PACK * (S * g + first + width)]

        def square(half, g):
            for t in range(PACK):
                nc.scalar.activation(
                    out=h_rows[half, g][:, t, 0:HALF],
                    in_=banks[half, g, t][:],
                    func=ACT.Square,
                    scale=root_gain[:, PACK * g + t : PACK * g + t + 1],
                )

        def weave_h(g, first, width):
            start = first % HALF
            weave(h_woven(g, first, width), h_rows[first // HALF, g][:, :, start : start + width])

        def quantize_h(g, first, width):
            quantize(h_codes[g], h_plane[g], first, width, h_woven(g, first, width))

        def features(first, width, passes, per_store=2):
            pairs = slice(first, first + width)
            sums = [psum.tile([P, width], F32, name="y%d_%d" % (first, c), tag="bank") for c in range(OUT_TILES)]
            opened = set()
            for g, c in passes:
                rows = slice(P * c, P * (c + 1))
                nc.tensor.matmul_mx(
                    out=sums[c][:],
                    lhsT=wf_codes[g][:, rows].bitcast(FP8X4),
                    lhsT_scale=wf_plane[g][:, rows],
                    rhs=h_codes[g][:, pairs].bitcast(FP8X4),
                    rhs_scale=h_plane[g][:, pairs],
                    start=(c not in opened),
                    stop=(c in opened),
                )
                opened.add(c)
            for c0 in range(0, OUT_TILES, per_store):
                result = tile("result%d_%d" % (first, c0), [P, per_store, width], F32)
                for e in range(per_store):
                    c = c0 + e
                    nc.scalar.activation(out=result[:, e, :], in_=sums[c][:], func=ACT.Tanh, bias=bias[:, c : c + 1])
                nc.sync.dma_start(
                    out=out[P * c0 : P * (c0 + per_store), pairs].rearrange("(e p) j -> p e j", p=P), in_=result[:]
                )

        for g in range(GROUPS):
            for a in range(DOC_PASSES):
                permute_wd(g, a)
        for half in range(2):
            doc_codes[half, 1] = gather_half("doc_codes_second", doc_win[1], doc_list, half)
        for a in range(DOC_PASSES):
            for half in range(2):
                for t in range(PACK):
                    doc_pass(half, 0, t, a)
        query_codes[0] = gather_half("query_codes", query_win, query_list, 0)
        for e in range(2):
            round_wq_scalar(0, 0, e)
        for t in range(PACK):
            quantize_wq(0, P * t, P // 2)
        round_wq_vector(0, 1, 0)
        round_wq_scalar(0, 1, 1)
        for t in range(PACK):
            quantize_wq(0, P * t + P // 2, P // 2)
        query_codes[1] = gather_half("query_codes", query_win, query_list, 1, "wq_woven00")
        for half in range(2):
            for t in range(PACK):
                query_pass(half, 0, t)

        for e in range(2):
            round_wq_vector(1, 0, e)
        for e in range(2):
            round_wq_vector(1, 1, e)
        for e in range(2):
            quantize_wq(1, 2 * P * e, 2 * P)
        square(0, 0)
        square(1, 0)
        for half in range(2):
            for t in range(PACK):
                for a in range(DOC_PASSES):
                    doc_pass(half, 1, t, a)
                query_pass(half, 1, t)
            square(half, 1)
        for first in (0, PIECE):
            weave_h(0, first, PIECE)
        for first in (0, PIECE):
            quantize_h(0, first, PIECE)
        for u in range(2):
            weave_wf(0, u)
        for u in range(2):
            quantize_wf(0, u)
        for u in range(2):
            weave_wf(1, u)
        quantize_wf(1, 0)
        weave_h(1, 0, PIECE)
        quantize_wf(1, 1)
        quantize_h(1, 0, PIECE)

        by_tile = [(g, c) for c in range(OUT_TILES) for g in (1, 0)]
        by_group = [(g, c) for g in range(GROUPS) for c in range(OUT_TILES)]
        features(0, PIECE, by_tile)
        weave_h(1, PIECE, PIECE)
        weave_h(0, 2 * PIECE, PIECE)
        quantize_h(1, PIECE, PIECE)
        features(PIECE, PIECE, by_group)
        for first, width in ((2 * PIECE, PIECE), (3 * PIECE, SMALL), (3 * PIECE + SMALL, SMALL)):
            for g in range(GROUPS):
                if (g, first) != (0, 2 * PIECE):
                    weave_h(g, first, width)
            for g in range(GROUPS):
                quantize_h(g, first, width)
            features(first, width, by_group, 1 if first + width == S else 2)
